import numpy as np, ml_dtypes
CORES = [3,7,11,15,131,135,139,143]
N = 8
import mx_ref
BF = ml_dtypes.bfloat16
def gcols(t, e):
    v = np.concatenate([t.reshape(8, 16, -1, 4), np.zeros((8, 16, 1, 4), BF)], axis=2)
    return np.ascontiguousarray(np.stack([v[g][:, e[g]] for g in range(8)])).reshape(128, -1)
def tile(rs):
    return np.stack(rs, axis=2).reshape(128, -1).astype(BF)
def cut(t, i, w=512):
    return t[:, w * i:w * i + w]
def pick(q, e):
    c = np.concatenate([q[0].reshape(128, -1, 4), np.zeros((128, 1, 4), np.uint8)], axis=1); s = np.concatenate([q[1], np.ones((16, 1), np.uint8)], axis=1)
    return (np.ascontiguousarray(c[:, e].reshape(128, -1)), np.ascontiguousarray(s[:, e]))
def join(*qs):
    return (np.concatenate([q[0] for q in qs], axis=1), np.concatenate([q[1] for q in qs], axis=1))
def put(q, e, v):
    c, s = q[0].reshape(128, -1, 4).copy(), q[1].copy(); c[:, e] = v[0].reshape(128, -1, 4); s[:, e] = v[1]
    return (c.reshape(128, -1), s)
def pk(c, s):
    return (np.ascontiguousarray(c), mx_ref.live(s))
def emit(q):
    return q[0], q[1]
def packed(v, rng):
    q = [mx_ref.quantize(np.ascontiguousarray(v[r])) for r in range(N)]
    return np.stack([a for a, b in q]), np.stack([mx_ref.plane(b, rng) for a, b in q])
def values_of_codes():
    e, c = np.zeros((128, 128, 4), np.float32), np.zeros((128, 2, 4), np.uint8)
    e[np.arange(128), np.arange(128), 0] = 1
    c[:127, :, 0] = np.arange(256).reshape(2, 128).T[:127]
    return mx_ref.matmul(mx_ref.quantize(e.reshape(128, 512).astype(BF)), (c.reshape(128, 8), np.full((16, 2), 127, np.uint8))).T.reshape(-1).astype(np.float64)
CODE_VALUE, SCALE_VALUE = values_of_codes(), 2.0 ** (np.arange(256) - 127.0)
def decode(q):
    return (CODE_VALUE[q[0]].reshape(16, 8, -1, 4) * SCALE_VALUE[q[1]][:, None, :, None] + 0.0).reshape(128, -1).astype(np.float32)
def f(rng, *shape):
    return mx_ref.flush((rng.standard_normal(shape, dtype=np.float32) * np.exp2(rng.integers(-2, 3, shape[:-1] + (1,)))).astype(BF))
def wide(rng, *shape, cols=0):
    v = rng.standard_normal(shape, dtype=np.float32) * np.exp2(rng.integers(-12, 13, shape)).astype(np.float32)
    if cols: v *= np.repeat(np.exp2(rng.integers(-cols, cols + 1, shape[:-2] + (1, shape[-1] // 4))) * (rng.random(shape[:-2] + (1, shape[-1] // 4)) > 0.0625), 4, axis=-1).astype(np.float32)
    return mx_ref.flush(v.astype(BF))
C, K, M, S, H, R = 352, 160, 44, 8, 9, 3
STEP = [3, 1, 5]
def gap(p, q):
    return np.abs(p.reshape(8, M, 1, S) - q.reshape(8, 1, M, S))
def match(p, q, lag):
    back = (np.arange(C) - lag[:, None]) % C
    d = np.maximum(gap(p, q), gap(np.take_along_axis(p, back, 1), np.take_along_axis(q, back, 1)))
    m = (S * np.argmin(d, axis=2) + np.arange(S)).reshape(8, C)
    e = np.sort(np.argsort(np.min(d, axis=2).reshape(8, C), axis=1, kind="stable")[:, :K], axis=1)
    return e, np.take_along_axis(m, e, 1)
def gput(t, e, h):
    a, b = t.reshape(8, 16, -1, 4).copy(), h.reshape(8, 16, -1, 4)
    for g in range(8): a[g][:, e[g]] = b[g]
    return a.reshape(128, -1)
def big(v):
    v = v.astype(np.float32)
    v[np.abs(v) < np.float32(2.0 ** -16)] = 0
    return v.astype(BF)
def numbers_of(rng):
    return {"x": big(f(rng, N, 128, 4 * C)), "u": np.array(f(rng, N, 128, 512)), "v": np.array(f(rng, N, 128, 512))}
def weights(rng, still=[]):
    w = big(f(rng, N, 128, 2048)).reshape(N, 8, 16, 4, 8, 16, 4)
    for i in still:
        w[:, :, i] = 0
        w[:, :, :, :, :, i] = 0
    c, p = packed(w.reshape(N, 128, 2048), rng)
    return {"wc": c, "ws": p}
def setup_inputs(rng):
    return {**numbers_of(rng), **weights(rng)}
def setup_inputs_ties(rng):
    d = numbers_of(rng)
    e = rng.permutation(N)
    x = d["x"].reshape(N, 8, 16, C, 4)
    a = x[0][:, :8, :3].copy()
    a[:, :, 2] = 0
    for r in range(N):
        k = np.zeros(C, int) if r == e[0] else rng.permutation(C) % 3
        x[r][:, :8] = a[:, :, k]
    x[e[1]] = 0
    u = d["u"].reshape(N, 8, 16, 128, 4)
    u[1:, :, :, ::32] = u[:1, :, :, ::32].copy()
    u[:, :, 8:, ::16] = 0
    return {"x": x.reshape(N, 128, 4 * C), "u": u.reshape(N, 128, 512), "v": d["v"], **weights(rng, range(8))}
def setup_inputs_near(rng):
    d = numbers_of(rng)
    x = d["x"].astype(np.float32).reshape(N, 8, 16, C, 4)
    u = d["u"].reshape(N, 128, 128, 4)
    u[:, :, ::16] = 0
    x[:, :, 0] = 0
    o = rng.permutation(8) % 4
    for r in range(N):
        for g in range(8):
            size = 2.0 ** -7 if o[g] == 3 else 1.0
            sign = -1.0 if r % 2 == 1 and o[g] < 3 else 1.0
            s = rng.integers(0, 256, C)
            b = ((s[:, None] >> np.arange(8)) & 1) * np.exp2(np.arange(8) - 23.0) * size * sign
            x[r, g, 8] = b[:, :4]
            x[r, g, 9] = b[:, 4:]
            x[r, g, 10:] = rng.integers(4, 8, (6, C, 4)) * 2.0 ** -20 * size
            if sign < 0: x[r, g, 0, :, 0] = -1
            if o[g] % 2 == 0 or o[g] == 3 and r % 2 == 0: x[r, g, 0, int(rng.integers(C)), 0] = sign * 2.0 ** 30
            k = 2.0 ** -30 if o[g] >= 2 else 1.0
            u[r, 16 * g, 16 * g, 0] = 1.0 if o[g] == 3 else k
            u[r, 16 * g + 8:16 * g + 10, 16 * g] = k
            if sign < 0 and r % 4 == 1:
                x[r, g, 0, :, 1] = -2.0 ** -9
                u[r, 16 * g, 16 * g, 1] = k
            if o[g] == 3:
                h = rng.integers(0, 6, C)
                x[r, g, 10, :, 0] = (8 + h) * 2.0 ** -33
                x[r, g, 11, :, 0] = (9 + h) * 2.0 ** -33
                u[r, 16 * g + 10, 16 * g, 0] = 9 * 2.0 ** -33
                u[r, 16 * g + 11, 16 * g, 0] = -8 * 2.0 ** -33
    return {"x": x.reshape(N, 128, 4 * C).astype(BF), "u": u.reshape(N, 128, 512), "v": d["v"], **weights(rng, [0, 8, 9, 10, 11, 12, 13, 14, 15])}
def setup_inputs_lags(rng):
    d = numbers_of(rng)
    x = d["x"].astype(np.float32).reshape(N, 8, 16, C, 4)
    u = d["u"].reshape(N, 128, 128, 4)
    size = np.where(rng.permutation(N) < N // 2, 2.0 ** -30, 1.0).astype(np.float32)
    x[:, :, :11] = 0
    ring = np.argsort(rng.random((8, C)), axis=1)
    key = np.zeros((N, 8, C), int)
    full, first = rng.permutation(8) < 4, rng.integers(0, S, 8)
    kept = [0, 1, 3, 4] if S == 8 else [0, 1, 3]
    for r in range(N):
        n = rng.permutation([0, 1, 2, 3, C // 2 + 2, 257, C - 1, C])
        for g in range(8):
            a = np.where(rng.permutation(C) < n[g], 1, -rng.integers(0, 2, C)) * size[r]
            x[r, g, 0, :, 0] = a * 1.125
            x[r, g, 1, :, 0] = a * 1.25
            gone, new = rng.permutation(C) < C // 4, rng.permutation(C)
            if full[g]: gone, new = ~np.isin((np.arange(C) - first[g]) % S, kept), new + 512 * (r % 2)
            key[r, g] = np.where(gone, new, np.roll(ring[g], S * int(rng.integers(M))))
    z = ((key[:, :, :, None] >> np.arange(12)) & 1) * np.exp2(np.arange(12.0))
    for i in range(3): x[:, :, 8 + i] = z[:, :, :, 4 * i:4 * i + 4]
    u[:, :, ::16] = 0
    u[:, :, 1::16] = 0
    for h in range(0, 128, 16):
        u[:, h + 8:h + 11, h] = 1
        u[:, h, h + 1, 0] = (size * np.float32(1.125)).astype(BF)
        u[:, h + 1, h + 1, 0] = (-size).astype(BF)
    return {"x": x.reshape(N, 128, 4 * C).astype(BF), "u": u.reshape(N, 128, 512), "v": d["v"], **weights(rng, range(11))}
def setup_inputs_huge(rng):
    d = numbers_of(rng)
    x = 2.0 ** 30 * (0.9 + 0.1 * rng.random((N, 128, C, 4)))
    x[:, ::8] = 2.0 ** 30
    far, c = rng.permutation(8) % 2, rng.permutation(8) % 2 * 2.0 - 1.0
    u = d["u"].reshape(N, 128, 8, 16, 4)
    for r in range(N):
        k = np.where((far == 1) & (r % 2 == 1), -c, c)
        a = 2.0 ** 30 * (1 - 0.05 * rng.random((128, 8, 4)))
        a[::8] = 2.0 ** 30
        u[r, :, :, 0] = (a * k[:, None]).astype(np.float32).astype(BF)
    w = np.zeros((N, 128, 4, 128, 4), np.float32)
    i = np.flatnonzero(np.arange(128) % 8)
    for b in range(4): w[:, i, b, i, b] = -1
    wc, ws = packed(w.reshape(N, 128, 2048).astype(BF), rng)
    return {"x": x.astype(np.float32).reshape(N, 128, 4 * C).astype(BF), "u": u.reshape(N, 128, 512), "v": d["v"], "wc": wc, "ws": ws}
def setup_inputs_spread(rng):
    d = setup_inputs(rng)
    d["x"] = big(wide(rng, N, 128, 4 * C, cols=6))
    return d
def check_inputs(d):
    b = []
    for k in ("x", "u", "v"):
        a = np.abs(d[k].astype(np.float32))
        if not (np.isfinite(a).all() and ((a == 0) | (a >= 2.0 ** -30) & (a <= 2.0 ** 30)).all()): b.append("a value of " + k)
    none, least, most = [emit(mx_ref.quantize(np.full((128, 16), k, np.float32).astype(BF)))[1][0, 0] for k in (0.0, 2.0 ** -30, 2.0 ** 30)]
    for r in range(N):
        if ((d["wc"][r] == 0x7F) | (d["wc"][r] == 0xFF)).any(): b.append("wc: a code that is no number")
        s = mx_ref.live(d["ws"][r])
        if ((s != none) & ((s < least) | (s > most))).any(): b.append("ws: a scale out of range")
        if ((s == none) & ((d["wc"][r].reshape(16, 8, -1, 4) & 0x7F) != 0).any(axis=(1, 3))).any(): b.append("wc: a code that isn't zero under the scale of zeros")
    return b
def reference(x, u, v, wc, ws):
    qu = [mx_ref.quantize(u[r]) for r in range(N)]
    lay = [pk(wc[r], ws[r]) for r in range(N)]
    now = [x[r] for r in range(N)]
    for t in range(R):
        sent = [mx_ref.quantize(now[r]) for r in range(N)]
        p = [mx_ref.matmul(qu[r], sent[r]) for r in range(N)]
        came = decode(join(*sent)).astype(BF)
        made, places = [], []
        for r in range(N):
            s = (r + STEP[t]) % N
            lag = 1 + np.sum(p[r][1::16] > 0, axis=1) % 4
            e, m = match(p[r][::16], p[s][::16], lag)
            q = mx_ref.quantize(gcols(cut(came, s, 4 * C), (m + H) % C))
            own = gcols(now[r], e)
            h = tile([mx_ref.matmul(pick(lay[r], np.arange(128 * b, 128 * b + 128)), q) * np.float32(0.015625) + own[:, b::4].astype(np.float32) for b in range(4)])
            made.append(gput(now[r], e, h))
            places.append(e)
        now = made
    y, oe = np.zeros((N, 128, C), np.float32), np.zeros((N, 8, K), np.float32)
    oc, osc = np.zeros((N, 128, 4 * C), np.uint8), np.zeros((N, 16, C), np.uint8)
    for r in range(N):
        q = mx_ref.quantize(now[r])
        y[r] = mx_ref.matmul(mx_ref.quantize(v[r]), q)
        oe[r] = places[r]
        oc[r], osc[r] = emit(q)
    return {"y": y, "oe": oe, "oc": oc, "osc": osc}

@@ -1,0 +1,506 @@
+from concourse.bass import DstId, RemoteDMATransfer
+from concourse.mybir import dt, AluOpType, AxisListType, ActivationFunctionType
+
+C, K, M, R = 352, 160, 44, 3
+STEP = [3, 1, 5]
+NC = 384
+BIG = float(2 ** 80)
+Q4, U8, F32, BF, I32, U16 = "float8_e4m3fn_x4", "uint8", "float32", "bfloat16", "int32", "uint16"
+
+SCRATCH = {}
+
+
+def _sb(name, n, dtype):
+    SCRATCH[name] = ("sbuf", [128, n], dtype)
+
+
+def _mx(name, n):
+    _sb(name, n, Q4)
+    _sb(name + "s", n, U8)
+
+
+for _n, _w in (("qu", 128), ("uc", 16), ("su0", 128), ("su1", 128), ("qv", 128), ("qw", 512), ("qe", 512),
+               ("q0n", 368), ("q3", NC), ("q3n", C), ("qz", K)):
+    _mx(_n, _w)
+for _t in range(R):
+    _mx("q%d" % _t, NC)
+    _mx("land%d" % _t, NC)
+    _mx("lu%d" % _t, 16)
+    _mx("sl%d" % _t, 128)
+for _n, _s, _d in (
+        ("xt", 4 * 368, BF), ("ut", 512, BF), ("vt", 512, BF), ("et", 2048, BF), ("xs", 4 * NC, BF),
+        ("wd", 4 * 544, BF), ("dsb", 4 * NC, BF), ("zall", 4 * NC, BF), ("zt", 4 * K, BF), ("f64", 4 * K, F32),
+        ("pi", 8, I32), ("kc", 16, F32), ("io5", 512, F32), ("m16", NC, F32), ("sm", 64, F32),
+        ("bt", NC, F32), ("jt", C, F32), ("c1", C, F32), ("plc", NC, F32), ("diag", NC, F32),
+        ("mab", 128, F32), ("keep16", 512, BF), ("reset", C, BF), ("keepc", 3 * C, BF),
+        ("keep24", 48, F32), ("mk", 160, F32), ("kt", 22 * 12, F32), ("ki", 22 * 3, I32),
+        ("kw", 24 * 3, F32), ("lc", 284, U16),
+        ("mm", 512, F32), ("ms", 512, F32), ("aa", 32, F32), ("arep", 4 * NC, F32), ("pos1", NC, BF),
+        ("tc", 8, F32), ("ti", 8, I32), ("bl", 66, F32), ("lb", 22, U16),
+        ("dd", 4 * NC, F32), ("ab", 3 * C, F32), ("aw", 4 * NC, F32), ("dm", 1056, F32), ("rr", 1064, F32),
+        ("nf", 1056, F32), ("st", 1056, F32), ("zi", 48, I32), ("lz", 24, U16), ("wb", 32, F32), ("t1", 32, F32),
+        ("xg", 480, F32), ("rw", 480, F32), ("row", C, F32), ("srt", 40, F32), ("cand", 16, F32), ("cnt", 16, F32),
+        ("junk", 13 * C, BF), ("cmp", 3 * C, BF), ("cms", 3 * C, BF), ("pen", 24, F32), ("lh", 40, F32),
+        ("r3", 16, F32), ("xe", 96, F32), ("xf", 96, F32), ("le", 48, F32), ("cs", 48, F32),
+        ("pw", 24 * 10, F32), ("lo", 24, U16), ("win", 544, F32), ("em", K, F32), ("es", K, F32),
+        ("lk", 10, U16), ("oeb", K, F32), ("yb", C, F32)):
+    _sb(_n, _s, _d)
+for _n in ("pa", "pb", "pc", "pd0", "pd1", "pd2", "pd3"):
+    SCRATCH[_n] = ("psum", [128, 512], F32)
+
+SEMAPHORES = ["v", "s", "t", "g", "lx", "lu", "lv", "lw", "out", "u0", "u1", "a0", "a1", "a2", "loc"]
+
+A = AluOpType
+AF = ActivationFunctionType
+X = AxisListType.X
+
+
+def rank_program(g, core, T, topo):
+    rank = T.rank_of(core)
+    if rank is None:
+        return
+    N = len(T.cores)
+    eng = {"v": g.vector, "s": g.scalar, "t": g.tensor, "g": g, "y": g.sync}
+    known = {q: {} for q in eng}
+    total = {}
+    clock = {}
+    wrote, read = {}, {}
+
+    def wait(q, ev):
+        s, n = ev
+        if known[q].get(s, 0) >= n:
+            return
+        eng[q].wait_ge(T.sem[s], n)
+        for a, b in list(clock.get(ev, {}).items()) + [ev]:
+            if known[q].get(a, 0) < b:
+                known[q][a] = b
+
+    def op(q, fn, r, w, sem=None, inc=1):
+        need = {}
+        evs = [wrote[k] for k in list(r) + list(w) if k in wrote]
+        for k in w:
+            evs += read.get(k, [])
+        for s, n in evs:
+            need[s] = max(need.get(s, 0), n)
+        for s, n in need.items():
+            wait(q, (s, n))
+        ins = fn()
+        if inc == 0:
+            return
+        s = sem or q
+        ins.then_inc(T.sem[s], inc)
+        total[s] = total.get(s, 0) + inc
+        ev = (s, total[s])
+        clock[ev] = dict(known[q])
+        for k in r:
+            read.setdefault(k, []).append(ev)
+        for k in w:
+            wrote[k] = ev
+            read[k] = []
+
+    V, S, PE = g.vector, g.scalar, g.tensor
+
+    def ts(o, i, s1, s2, o0, o1, r, w):
+        if o1 is None:
+            op("v", lambda: V.tensor_scalar(o, i, s1, None, o0), r, w)
+        else:
+            op("v", lambda: V.tensor_scalar(o, i, s1, s2, o0, o1), r, w)
+
+    def tt(o, a, b, f, r, w):
+        op("v", lambda: V.tensor_tensor(o, a, b, f), r, w)
+
+    def cp(o, i, r, w):
+        op("v", lambda: V.tensor_copy(o, i), r, w)
+
+    def ms(o, c, w):
+        op("v", lambda: V.memset(o, c), [], w)
+
+    def scan(o, a, b, o0, o1, r, w):
+        op("v", lambda: V.tensor_tensor_scan(o, a, b, 0.0, o0, o1), r, w)
+
+    def red(o, i, f, r, w):
+        op("v", lambda: V.tensor_reduce(o, i, X, f), r, w)
+
+    def tr(o, i, r, w):
+        op("v", lambda: V.transpose(o, i), r, w)
+
+    def act(o, i, f, r, w, **kw):
+        op("s", lambda: S.activation(o, i, f, **kw), r, w)
+
+    def quant(name, n, tile, r):
+        op("v", lambda: V.quantize_mx(T[name][:, 0:n], T[name + "s"][:, 0:n], tile), r, [name, name + "s"])
+
+    def mm(ps, lhs, l0, rhs, n, r):
+        op("t", lambda: PE.matmul_mx(T[ps][:, 0:n], T[lhs][:, l0:l0 + 128], T[lhs + "s"][:, l0:l0 + 128],
+                                     T[rhs][:, 0:n], T[rhs + "s"][:, 0:n], True, True),
+           r + [rhs, rhs + "s"], [ps])
+
+    def pick(dst, n, src, w, off, okey, on_s=True):
+        op("v", lambda: V.tensor_copy(T[dst][:, 0:n].bitcast(dt.uint32), T[src][:, 0:w].bitcast(dt.uint32).indirect(off)),
+           [src, okey], [dst])
+        if on_s:
+            act(T[dst + "s"][:, 0:n], T[src + "s"][:, 0:w].indirect(off), AF.Copy, [src + "s", okey], [dst + "s"])
+        else:
+            cp(T[dst + "s"][:, 0:n], T[src + "s"][:, 0:w].indirect(off), [src + "s", okey], [dst + "s"])
+
+    def iota(o, pat, base, cm, w, f=True):
+        if f:
+            op("g", lambda: g.iota(o, pat, base, cm, allow_small_or_imprecise_dtypes=True), [], w)
+        else:
+            op("g", lambda: g.iota(o, pat, base, cm), [], w)
+
+    def dma(q, o, i, sem, r, w):
+        op(q, lambda: eng[q].dma_start(o, i), r, w, sem=sem, inc=16)
+
+    def bits(es):
+        return sum(1 << e for e in es)
+
+    askers = [T.cores[(rank - STEP[t]) % N] for t in range(R)]
+    ne = min(len(topo.engines(core, d)) for d in askers)
+
+    def send_state(t):
+        d = askers[t]
+        rid, pid = topo.addr(d, core)
+        mask = bits(topo.engines(core, d)[:ne])
+        q, l = "q%d" % t, "land%d" % t
+        op("g", lambda: g.remote_dma(T[l][:].bitcast(dt.uint8), T[q][:].bitcast(dt.uint8), T.sem["a%d" % t], T.sem.loc,
+                                     pid, rid, mask), [q], [], inc=0)
+        op("g", lambda: g.remote_dma(T[l + "s"][:], T[q + "s"][:], T.sem["a%d" % t], T.sem.loc, pid, rid, mask),
+           [q + "s"], [], inc=0)
+        total["loc"] = total.get("loc", 0) + 2 * ne
+        total["a%d" % t] = 2 * ne
+        wrote[l] = wrote[l + "s"] = ("a%d" % t, 2 * ne)
+
+    def send_u(rounds, sem):
+        per = ne // len(rounds)
+        for sfx in ("", "s"):
+            trs = []
+            for i, t in enumerate(rounds):
+                rid, pid = topo.addr(askers[t], core)
+                es = topo.engines(core, askers[t])[per * i:per * (i + 1)]
+                src, dst = T["uc" + sfx][:], T["lu%d%s" % (t, sfx)][:]
+                if not sfx:
+                    src, dst = src.bitcast(dt.uint8), dst.bitcast(dt.uint8)
+                trs.append(RemoteDMATransfer(dst_ids=[DstId(rid=rid, pnc=pid)], dma_engine_mask=bits(es),
+                                             remote_sem=T.sem[sem], src=src, dst=dst))
+            op("g", lambda: g.remote_dma_fused(trs, local_sem=T.sem.loc), ["uc" + sfx], [], inc=0)
+        total["loc"] = total.get("loc", 0) + 2 * ne
+        total[sem] = 2 * ne
+        for t in rounds:
+            wrote["lu%d" % t] = wrote["lu%ds" % t] = (sem, 2 * ne)
+
+    io, kc, lc, kt, kw, mk = T.io5, T.kc, T.lc, T.kt, T.kw, T.mk
+    col = lambda b, i: b[:, i:i + 1]
+    L_U, L_16, L_S, L_ROW, L_0, L_X, L_ABS, L_SUC, L_NAT, L_CMP = 0, 2, 18, 42, 72, 96, 192, 214, 236, 258
+    lst = lambda a, n: lc[:, a:a + n]
+    k22 = lambda i: kt[:, 22 * i:22 * i + 22]
+
+    def tables():
+        k = k22
+        ki = lambda i: T.ki[:, 22 * i:22 * i + 22]
+        ts(k(0), io[:, 0:22], 16.0, col(kc, 0), A.mult, A.add, ["io", "q"], ["e"])
+        ts(k(1), k(0), -21.5, 1.0 / M, A.add, A.mult, ["e"], ["k1"])
+        ts(k(9), k(0), -11.5, 1.0 / 24, A.add, A.mult, ["e"], ["k9"])
+        cp(ki(0), k(1), ["k1"], ["si"])
+        cp(ki(2), k(9), ["k9"], ["ni"])
+        cp(k(1), ki(0), ["si"], ["sf"])
+        ts(k(2), ki(0), -float(M), None, A.mult, None, ["si"], ["k2t"])
+        ts(k(9), ki(2), -383.0, None, A.mult, None, ["ni"], ["k9"])
+        ts(k(10), k(0), 16.0, None, A.mult, None, ["e"], ["k10"])
+        tt(k(2), k(2), k(0), A.add, ["k2t", "e"], ["j"])
+        tt(k(9), k(9), k(10), A.add, ["k9", "k10"], ["k9"])
+        ts(k(8), ki(2), 8.0, None, A.mult, None, ["ni"], ["k8"])
+        ts(k(3), k(2), -1.0, 1.0 / 3, A.add, A.mult, ["j"], ["k3"])
+        ts(k(4), k(2), 128.0, None, A.mult, None, ["j"], ["k4"])
+        ts(k(5), k(1), 16.0, None, A.mult, None, ["sf"], ["k5"])
+        cp(lst(L_NAT, 22), k(9), ["k9"], ["L_NAT"])
+        tt(k(8), k(8), k(0), A.add, ["k8", "e"], ["k8"])
+        cp(ki(1), k(3), ["k3"], ["ai"])
+        tt(k(4), k(4), k(5), A.add, ["k4", "k5"], ["k4"])
+        ts(k(6), k(2), 0.0, -113.0, A.is_equal, A.mult, ["j"], ["k6"])
+        ts(k(11), ki(1), 3.0, None, A.mult, None, ["ai"], ["k11"])
+        ts(k(3), ki(1), -383.0, None, A.mult, None, ["ai"], ["k3"])
+        tt(k(11), k(11), k(2), A.is_equal, ["k11", "j"], ["k11"])
+        tt(k(4), k(4), k(3), A.add, ["k4", "k3"], ["k4"])
+        ts(k(11), k(11), 383.0, -384.0, A.mult, A.add, ["k11"], ["k11"])
+        cp(lst(L_CMP, 12), kt[:, 176:188], ["k8"], ["L_CA"])
+        ts(lst(L_CMP + 12, 10), kt[:, 188:198], -256.0, None, A.add, None, ["k8"], ["L_CB"])
+        tt(k(6), k(6), k(11), A.add, ["k6", "k11"], ["adj"])
+        ts(k(7), k(4), NC - 16.0, None, A.add, None, ["k4"], ["base"])
+        cp(lst(L_ABS, 22), k(4), ["k4"], ["L_ABS"])
+
+    def masks():
+        ts(T.pi[:, 2:3], T.pi[:, 0:1], 16, None, A.bitwise_and, None, ["pi0"], ["pi2"])
+        ts(kw[:, 24:48], kw[:, 0:24], float(C), BIG, A.is_ge, A.mult, ["n0"], ["pad"])
+        cp(col(kc, 9), T.pi[:, 2:3], ["pi2"], ["h"])
+        ts(kw[:, 48:72], io[:, 0:24], 16.0, col(kc, 0), A.mult, A.add, ["io", "q"], ["J"])
+        ts(col(kc, 10), col(kc, 9), 16.0, None, A.add, None, ["h"], ["h16"])
+        tt(col(kc, 11), col(kc, 9), col(kc, 0), A.add, ["h", "q"], ["r32"])
+        ts(mk[:, 0:32], io[:, 0:32], col(kc, 9), None, A.is_ge, None, ["io", "h"], ["mk0"])
+        ts(mk[:, 64:96], io[:, 0:32], col(kc, 10), None, A.is_lt, None, ["io", "h16"], ["mk2"])
+        ts(mk[:, 32:64], io[:, 0:32], col(kc, 11), None, A.is_gt, None, ["io", "r32"], ["mk1"])
+        ts(kw[:, 48:72], kw[:, 48:72], float(K), None, A.add, None, ["J"], ["J"])
+        tt(mk[:, 0:32], mk[:, 0:32], mk[:, 64:96], A.mult, ["mk0", "mk2"], ["same"])
+        tt(mk[:, 32:64], mk[:, 32:64], mk[:, 64:96], A.mult, ["mk1", "mk2"], ["tri"])
+        ms(T.keep24[:], 1.0, ["keep24"])
+        ts(mk[:, 96:128], mk[:, 0:32], -BIG, BIG, A.mult, A.add, ["same"], ["other"])
+        ts(mk[:, 128:160], mk[:, 0:32], -1.0, None, A.mult, None, ["same"], ["nsame"])
+        ms(T.keep24[:, 0::24], 0.0, ["keep24"])
+        ms(T.keepc[:, 0::C], 0.0, ["keepc0", "keepc1", "keepc2"])
+
+    def successors():
+        k = k22
+        ts(k(5), k(1), 7.0, None, A.is_equal, None, ["sf"], ["k5"])
+        ts(k(8), k(1), 1.0, 48.0, A.add, A.mult, ["sf"], ["k8"])
+        tt(k(10), k(5), k(2), A.add, ["k5", "j"], ["k10"])
+        ts(k(5), k(5), -384.0, 1.0, A.mult, A.add, ["k5"], ["k5"])
+        ts(k(11), k(10), M - 1.0, -float(M), A.is_ge, A.mult, ["k10"], ["k11"])
+        tt(k(8), k(8), k(5), A.add, ["k8", "k5"], ["k8"])
+        tt(k(10), k(10), k(11), A.add, ["k10", "k11"], ["k10"])
+        tt(k(8), k(8), k(10), A.add, ["k8", "k10"], ["k8"])
+        cp(lst(L_SUC, 22), k(8), ["k8"], ["L_SUC"])
+        tt(T.c1[:], T.bt[:].indirect(lst(L_SUC, 22)), T.jt[:], A.add, ["bt", "jt", "L_SUC"], ["c1"])
+
+    dma("y", T.ut[:], T.u[:], "lu", [], ["ut"])
+    dma("s", T.xt[:, 0:4 * C], T.x[:], "lx", [], ["xt"])
+    iota(T.pi[:, 0:1], [[0, 1]], 0, 1, ["pi0"], f=False)
+    iota(io[:], [[1, 512]], 0, 0, ["io"])
+    iota(T.sm[:, 0:24], [[0, 3], [1, 8]], 0, 0, ["sm0"])
+    iota(T.sm[:, 24:54], [[1, 15], [16, 2]], 0, 0, ["sm1"])
+    iota(T.m16[:], [[0, 24], [1, 16]], 0, 0, ["m16"])
+    ms(T.xt[:, 4 * C:], 0.0, ["xz"])
+    for b in range(4):
+        act(T.et[:, 512 * b:512 * b + 512], io[:], AF.Identity, ["io"], ["et%d" % b], bias=1.0, scale=0.0)
+    ms(T.keep16[:], 1.0, ["keep16"])
+    ms(T.reset[:], 0.0, ["reset"])
+    ms(T.aa[:, 0:4], 0.0, ["aaz"])
+    ms(T.aw[:, 0:64], 0.0, ["awz"])
+    ms(T.wb[:, 24:32], BIG, ["wbz"])
+    ms(T.rr[:, 0:8], 0.0, ["rrz"])
+    ms(T.keep16[:, 0::16], 0.0, ["keep16"])
+    ms(T.reset[:, 0::M], BIG, ["reset"])
+    ts(T.pi[:, 1:2], T.pi[:, 0:1], 15, None, A.bitwise_and, None, ["pi0"], ["pi1"])
+    cp(col(kc, 0), T.pi[:, 1:2], ["pi1"], ["q"])
+    ts(col(kc, 1), col(kc, 0), 24.0, None, A.mult, None, ["q"], ["q24"])
+    ts(col(kc, 2), col(kc, 0), 8.0, -127.0, A.is_ge, A.mult, ["q"], ["k2"])
+    ts(col(kc, 3), col(kc, 0), 0.0, None, A.is_equal, None, ["q"], ["qz0"])
+    ts(col(kc, 4), col(kc, 0), -1.0, None, A.add, None, ["q"], ["qm1"])
+    ts(lst(L_U, 1), col(kc, 0), 16.0, col(kc, 2), A.mult, A.add, ["q", "k2"], ["L_U"])
+    ts(kw[:, 0:24], io[:, 0:24], col(kc, 1), float(C), A.add, A.min, ["io", "q24"], ["n0"])
+    cp(lst(L_16, 16), io[:, 0:16], ["io"], ["L_16"])
+    cp(lst(L_0, 24), kw[:, 0:24], ["n0"], ["L_0"])
+    quant("qu", 128, T.ut[:], ["ut"])
+    pick("uc", 16, "qu", 128, lst(L_U, 1), "L_U", on_s=False)
+    send_u([0], "u0")
+    tables()
+    quant("q0n", 368, T.xt[:], ["xt", "xz"])
+    pick("q0", NC, "q0n", 368, lst(L_0, 24), "L_0")
+    send_state(0)
+    iota(T.bt[:], [[16, 8], [1, 16], [128, 3]], 0, 0, ["bt"])
+    iota(T.jt[:], [[0, 8], [-512, M]], 64 * 512, 0, ["jt"])
+    ek = ["et%d" % b for b in range(4)]
+    op("g", lambda: g.affine_select(T.et[:], T.et[:], [[-1, 4], [1, 512]], A.is_equal, 0.0, 0, -4), ek, ek)
+    send_u([1, 2], "u1")
+    iota(T.plc[:], [[1, 24], [24, 16]], 0, 0, ["plc"])
+    pick("su0", 128, "uc", 16, lst(L_16, 8), "L_16")
+    pick("su1", 128, "uc", 16, lst(L_16 + 8, 8), "L_16")
+    for b in range(3):
+        act(T.keepc[:, C * b:C * b + C], io[:, 0:C], AF.Identity, ["io"], ["keepc%d" % b], bias=1.0, scale=0.0)
+    ts(T.diag[:], T.m16[:], col(kc, 0), None, A.is_equal, None, ["m16", "q"], ["diag"])
+    ts(T.mab[:, 0:64], T.m16[:, 0:64], 14.0, col(kc, 3), A.is_equal, A.mult, ["m16", "qz0"], ["ma"])
+    ts(T.mab[:, 64:128], T.m16[:, 0:64], col(kc, 4), None, A.is_equal, None, ["m16", "qm1"], ["mb"])
+    cp(lst(L_S, 54), T.sm[:, 0:54], ["sm0", "sm1"], ["L_S"])
+    for b in range(4):
+        ts(lst(L_X + 24 * b, 24), kw[:, 0:24], 4.0, float(b), A.mult, A.add, ["n0"], ["L_X%d" % b])
+
+    wd = T.wd
+    xpl = lambda b: wd[:, 544 * b + K:544 * b + 544]
+    for t in range(R):
+        q, land, sl = "q%d" % t, "land%d" % t, "sl%d" % t
+        mm("pa", "su0", 0, q, NC, ["su0", "su0s"])
+        mm("pb", "su1", 0, q, NC, ["su1", "su1s"])
+        tt(T.mm[:, 0:NC], T.pa[:, 0:NC], T.diag[:], A.mult, ["pa", "diag"], ["mm0"])
+        tt(T.mm[:, 384:448], T.pa[:, 192:256], T.mab[:, 0:64], A.mult, ["pa", "ma"], ["mm1"])
+        tt(T.mm[:, 448:512], T.pa[:, 320:384], T.mab[:, 64:128], A.mult, ["pa", "mb"], ["mm2"])
+        scan(T.ms[:], T.keep16[:], T.mm[:], A.mult, A.add, ["keep16", "mm0", "mm1", "mm2"], ["ms"])
+        cp(T.aa[:, 8:32], T.ms[:, 15:384:16], ["ms"], ["aa1"])
+        tt(T.aa[:, 4:8], T.ms[:, 399:448:16], T.ms[:, 463:512:16], A.add, ["ms"], ["aa0"])
+        for kb in (1, 2, 3):
+            act(T.arep[:, NC * kb:NC * kb + NC], T.aa[:, 8 * kb:8 * kb + 8].indirect(lst(L_S, 24)), AF.Copy,
+                ["aa1", "L_S"], ["arep%d" % kb])
+        if t == 0:
+            pick(sl, 128, "lu0", 16, lst(L_16, 8), "L_16")
+        for b in range(4):
+            if t == 0:
+                act(xpl(b), T.xt[:].indirect(lst(L_X + 24 * b, 24)), AF.Copy, ["xt", "xz", "L_X%d" % b], ["xp%d" % b], scale=64.0)
+            else:
+                act(xpl(b), T.xs[:, b::4], AF.Copy, ["xs%d" % b, "xs4"], ["xp%d" % b], scale=64.0)
+        cp(T.arep[:, 64:NC], T.aa[:, 0:8].indirect(lst(L_S + 4, 20)), ["aa0", "aaz", "L_S"], ["arep0"])
+        ts(T.pos1[:], T.pb[:, 0:NC], 0.0, None, A.is_gt, None, ["pb"], ["pos1"])
+        red(col(T.tc, 0), T.pos1[:], A.add, ["pos1"], ["tc0"])
+        cp(col(T.ti, 0), col(T.tc, 0), ["tc0"], ["ti0"])
+        ts(col(T.ti, 1), col(T.ti, 0), 3, None, A.bitwise_and, None, ["ti0"], ["ti1"])
+        cp(col(T.tc, 1), col(T.ti, 1), ["ti1"], ["tc1"])
+        ts(col(T.tc, 2), col(T.ti, 1), -16.0, None, A.mult, None, ["ti1"], ["tc2"])
+        ts(T.bl[:, 0:22], k22(1), col(T.tc, 1), None, A.is_le, None, ["sf", "tc1"], ["bl0"])
+        tt(T.bl[:, 22:44], T.bl[:, 0:22], k22(6), A.mult, ["bl0", "adj"], ["bl1"])
+        tt(T.bl[:, 44:66], T.bl[:, 22:44], k22(7), A.add, ["bl1", "base"], ["bl2"])
+        ts(T.lb[:], T.bl[:, 44:66], col(T.tc, 2), None, A.add, None, ["bl2", "tc2"], ["lb"])
+        if t == 0:
+            masks()
+            successors()
+        mm("pc", sl, 0, land, NC, [sl, sl + "s"])
+        if t == 0:
+            wait("y", wrote[land])
+            dma("y", T.qw[:].bitcast(dt.uint8), T.wc[:], "lw", [], ["qw"])
+            dma("y", T.qws[:], T.ws[:], "lw", [], ["qw"])
+            dma("y", T.vt[:], T.v[:], "lv", [], ["vt"])
+        for kb in range(4):
+            a, e = NC * kb + (64 if kb == 0 else 0), NC * kb + NC
+            tt(T.dd[:, a:e], T.pc[:, a - NC * kb:NC], T.arep[:, a:e], A.subtract, ["pc", "arep%d" % kb], ["dd%d" % kb])
+            act(T.aw[:, a:e], T.dd[:, a:e], AF.Abs, ["dd%d" % kb], ["aw%d" % kb])
+            if kb:
+                act(T.ab[:, C * kb - C:C * kb], T.dd[:, a:e].indirect(lst(L_ABS, 22)), AF.Abs, ["dd%d" % kb, "L_ABS"], ["ab%d" % kb])
+        if t == 0:
+            quant("qe", 512, T.et[:], ek)
+        for b in range(4):
+            mm("pd%d" % b, "qe", 128 * b, land, NC, ["qe", "qes"])
+        for k in range(3):
+            tt(T.dm[:, C * k:C * k + C], T.aw[:, NC * k:NC * k + 2 * NC].indirect(T.lb[:]), T.ab[:, C * k:C * k + C],
+               A.max, ["aw%d" % k, "aw%d" % (k + 1), "awz", "ab%d" % (k + 1), "lb"], ["dm%d" % k])
+            scan(T.rr[:, 8 + C * k:8 + C * k + C], T.reset[:], T.dm[:, C * k:C * k + C], A.max, A.min,
+                 ["reset", "dm%d" % k], ["rr%d" % k])
+        unpack = lambda b: act(T.dsb[:, NC * b:NC * b + NC], T["pd%d" % b][:, 0:NC], AF.Copy, ["pd%d" % b], ["dsb%d" % b])
+        unpack(0)
+        unpack(1)
+        W = T.wb
+        tt(W[:, 0:24], T.rr[:, 8 + M - 1:1064:M], kw[:, 24:48], A.max, ["rr0", "rr1", "rr2", "pad"], ["W"])
+        tr(T.t1[:], W[:], ["W", "wbz"], ["t1"])
+        s8 = lambda i: T.srt[:, 8 * i:8 * i + 8]
+        act(T.xg[:, 0:256], T.t1[:].indirect(lst(L_ROW, 16)), AF.Copy, ["t1", "L_S"], ["xg0"])
+        cp(T.xg[:, 256:480], T.t1[:].indirect(lst(L_ROW + 16, 14)), ["t1", "L_S"], ["xg1"])
+        tt(s8(0), W[:, 0:8], W[:, 8:16], A.min, ["W"], ["s0"])
+        tr(T.rw[:, 256:480], T.xg[:, 256:480], ["xg1"], ["rw1"])
+        act(T.row[:, 192:C], T.rw[:, 256:480].indirect(lst(L_CMP + 12, 10)), AF.Copy, ["rw1", "L_CB"], ["row1"])
+        tr(T.rw[:, 0:256], T.xg[:, 0:256], ["xg0"], ["rw0"])
+        tt(s8(1), W[:, 0:8], W[:, 8:16], A.max, ["W"], ["s1"])
+        cp(T.row[:, 0:192], T.rw[:, 0:256].indirect(lst(L_CMP, 12)), ["rw0", "L_CA"], ["row0"])
+        tt(s8(2), s8(1), W[:, 16:24], A.min, ["W", "s1"], ["s2"])
+        tt(s8(3), s8(0), W[:, 16:24], A.min, ["W", "s0"], ["low"])
+        tt(T.cand[:, 0:8], s8(0), s8(2), A.max, ["s0", "s2"], ["mid"])
+        tt(s8(4), s8(1), W[:, 16:24], A.max, ["W", "s1"], ["upp"])
+
+        def count(i, key):
+            act(T.junk[:, C * i:C * i + C], T.row[:], AF.Sign, ["row0", "row1", key], ["junk%d" % i, "cnt%d" % i],
+                bias=col(T.cand, i), scale=-1.0, accum_out=col(T.cnt, i))
+        for i in range(8):
+            count(i, "mid")
+        tt(T.nf[:], T.rr[:, 8:1064], T.rr[:, 7:1063], A.is_ge, ["rr0", "rr1", "rr2", "rrz"], ["nf"])
+        for k in range(3):
+            scan(T.st[:, C * k:C * k + C], T.nf[:, C * k:C * k + C], T.c1[:], A.mult, A.max, ["nf", "c1"], ["st%d" % k])
+        cp(T.zi[:, 0:24], T.st[:, M - 1::M], ["st0", "st1", "st2"], ["zi0"])
+        ts(T.zi[:, 24:48], T.zi[:, 0:24], 511, None, A.bitwise_and, None, ["zi0"], ["zi1"])
+        pen, lh, r3 = T.pen, T.lh, T.r3
+        c8 = ["cnt%d" % i for i in range(8)]
+        half = 2 * K - C - 0.5
+        ts(pen[:, 8:16], T.cnt[:, 0:8], half, BIG, A.is_lt, A.mult, c8, ["pen1"])
+        cp(T.lz[:], T.zi[:, 24:48], ["zi1"], ["lz"])
+        tt(lh[:, 32:40], s8(4), pen[:, 8:16], A.min, ["upp", "pen1"], ["lh2"])
+        tt(T.cand[:, 8:16], lh[:, 32:40], s8(3), A.max, ["lh2", "low"], ["nxt"])
+        for i in range(8, 13):
+            count(i, "nxt")
+        for i in range(3):
+            ts(T.cmp[:, C * i:C * i + C], T.row[:], col(T.cand, 13 + i), None, A.is_lt, None, ["row0", "row1", "nxt"], ["cmp%d" % i])
+        ts(pen[:, 0:8], T.cnt[:, 0:8], half, BIG, A.is_lt, A.mult, c8, ["pen0"])
+        scan(T.cms[:], T.keepc[:], T.cmp[:], A.mult, A.add, ["keepc0", "cmp0", "cmp1", "cmp2"], ["cms"])
+        unpack(2)
+        unpack(3)
+        for b in range(4):
+            act(T.zall[:, NC * b:NC * b + NC], T.dsb[:, NC * b:NC * b + NC].indirect(T.lz[:]), AF.Copy,
+                ["dsb%d" % b, "lz"], ["zall%d" % b])
+        ts(pen[:, 21:24], T.cms[:, C - 1::C], K - 0.5, BIG, A.is_lt, A.mult, ["cms"], ["pen3"])
+        ts(pen[:, 16:21], T.cnt[:, 8:13], half, BIG, A.is_lt, A.mult, ["cnt%d" % i for i in range(8, 13)], ["pen2"])
+        pk = ["pen1", "pen2", "pen3"]
+        tt(lh[:, 0:16], T.cand[:], pen[:, 8:24], A.min, ["mid", "nxt"] + pk, ["lh0"])
+        tt(lh[:, 16:32], T.cand[:], pen[:, 8:24], A.max, ["mid", "nxt"] + pk, ["lh1"])
+        red(col(r3, 2), pen[:], A.add, pk + ["pen0"], ["r2"])
+        red(col(r3, 0), lh[:, 0:16], A.max, ["lh0"], ["r0"])
+        red(col(r3, 1), lh[:, 16:32], A.min, ["lh1"], ["r1"])
+        xe, xf = T.xe, T.xf
+        ts(xe[:, 64:96], mk[:, 0:32], col(r3, 2), None, A.mult, None, ["same", "r2"], ["xe2"])
+        ts(xe[:, 0:32], mk[:, 0:32], col(r3, 0), None, A.mult, None, ["same", "r0"], ["xe0"])
+        ts(xe[:, 32:64], mk[:, 96:128], col(r3, 1), None, A.max, None, ["other", "r1"], ["xe1"])
+        tr(xf[:], xe[:], ["xe0", "xe1", "xe2"], ["xf"])
+        red(col(r3, 5), xf[:, 64:96], A.add, ["xf"], ["r5"])
+        red(col(r3, 4), xf[:, 32:64], A.min, ["xf"], ["r4"])
+        red(col(r3, 3), xf[:, 0:32], A.max, ["xf"], ["r3"])
+        ts(col(r3, 6), col(r3, 5), (K - 0.5) * BIG, col(r3, 4), A.is_lt, A.mult, ["r4", "r5"], ["r6"])
+        tt(col(r3, 7), col(r3, 6), col(r3, 3), A.max, ["r6", "r3"], ["tau"])
+        tau = col(r3, 7)
+        p24 = lambda i: T.pw[:, 24 * i:24 * i + 24]
+        ts(T.le[:, 0:24], W[:, 0:24], tau, None, A.is_lt, None, ["W", "tau"], ["lt"])
+        ts(T.le[:, 24:48], W[:, 0:24], tau, None, A.is_equal, None, ["W", "tau"], ["eq"])
+        ts(p24(0), W[:, 0:24], tau, 1000.0, A.is_gt, A.mult, ["W", "tau"], ["p0"])
+        scan(T.cs[:], T.keep24[:], T.le[:], A.mult, A.add, ["keep24", "lt", "eq"], ["cs"])
+        ts(p24(1), W[:, 0:24], tau, 1000.0, A.is_equal, A.mult, ["W", "tau"], ["p1"])
+        ts(xe[:, 0:32], mk[:, 32:64], col(T.cs, 23), None, A.mult, None, ["tri", "cs"], ["xe0"])
+        ts(xe[:, 32:64], mk[:, 32:64], col(T.cs, 47), None, A.mult, None, ["tri", "cs"], ["xe1"])
+        ts(xe[:, 64:96], mk[:, 128:160], col(T.cs, 23), K / 32.0, A.mult, A.add, ["nsame", "cs"], ["xe2"])
+        tr(xf[:], xe[:], ["xe0", "xe1", "xe2"], ["xf"])
+        tt(p24(2), T.cs[:, 0:24], p24(0), A.add, ["cs", "p0"], ["p2"])
+        red(col(r3, 9), xf[:, 32:64], A.add, ["xf"], ["r9"])
+        red(col(r3, 10), xf[:, 64:96], A.add, ["xf"], ["r10"])
+        red(col(r3, 8), xf[:, 0:32], A.add, ["xf"], ["r8"])
+        ts(p24(3), T.cs[:, 24:48], col(r3, 9), col(r3, 10), A.add, A.min, ["cs", "r9", "r10"], ["p3"])
+        ts(p24(4), T.cs[:, 24:48], col(r3, 9), col(r3, 10), A.add, A.is_gt, ["cs", "r9", "r10"], ["p4"])
+        ts(p24(5), p24(2), col(r3, 8), -1.0, A.add, A.add, ["p2", "r8"], ["p5"])
+        tt(p24(6), p24(4), p24(1), A.mult, ["p4", "p1"], ["p6"])
+        tt(p24(7), p24(3), p24(5), A.add, ["p3", "p5"], ["p7"])
+        tt(p24(8), p24(6), p24(7), A.add, ["p6", "p7"], ["p8"])
+        tt(p24(9), p24(8), kw[:, 48:72], A.min, ["p8", "J"], ["p9"])
+        cp(T.lo[:], p24(9), ["p9"], ["lo"])
+        cp(T.win[:].indirect(T.lo[:]), io[:, 0:NC], ["lo", "io"], ["win"])
+        tt(T.em[:], T.win[:, 0:K], T.diag[:, 0:K], A.mult, ["win", "diag"], ["em"])
+        scan(T.es[:], T.keep16[:, 0:K], T.em[:], A.mult, A.add, ["keep16", "em"], ["es"])
+        cp(T.lk[:], T.es[:, 15::16], ["es"], ["lk"])
+        zsrc = lambda b: T.zall[:, NC * b:NC * b + NC].indirect(T.lk[:])
+        for b in (0, 1):
+            cp(T.zt[:, b::4], zsrc(b), ["zall%d" % b, "lk"], ["zt%d" % b])
+        for b in (2, 3):
+            act(T.zt[:, b::4], zsrc(b), AF.Copy, ["zall%d" % b, "lk"], ["zt%d" % b])
+        for b in (2, 3):
+            act(T.f64[:, K * b:K * b + K], xpl(b).indirect(T.lk[:]), AF.Copy, ["xp%d" % b, "lk"], ["f%d" % b])
+        quant("qz", K, T.zt[:], ["zt%d" % b for b in range(4)])
+        for b in (2, 3, 0, 1):
+            mm("pd%d" % b, "qw", 128 * b, "qz", K, ["qw"])
+        for b in (0, 1):
+            cp(T.f64[:, K * b:K * b + K], xpl(b).indirect(T.lk[:]), ["xp%d" % b, "lk"], ["f%d" % b])
+        if t + 1 == R:
+            act(T.oeb[:], T.plc[:].indirect(T.lk[:]), AF.Copy, ["plc", "lk"], ["oeb"])
+            for k in range(8):
+                dma("y", T.oe[k:k + 1, :], T.oeb[16 * k:16 * k + 1, :], "out", ["oeb"], [])
+        for b in (2, 3, 0, 1):
+            tt(wd[:, 544 * b:544 * b + K], T["pd%d" % b][:, 0:K], T.f64[:, K * b:K * b + K], A.add,
+               ["pd%d" % b, "f%d" % b], ["g%d" % b])
+        usrc = lambda b, a, e: wd[:, 544 * b:544 * b + 544].indirect(T.lo[:, a:e])
+        for b, a, e, key in ((2, 0, 24, "xs2"), (3, 0, 24, "xs3"), (1, 16, 24, "xs4")):
+            act(T.xs[:, 64 * a + b:64 * e:4], usrc(b, a, e), AF.Copy, ["g%d" % b, "xp%d" % b, "lo"], [key], scale=0.015625)
+        for b, a, e in ((0, 0, 24), (1, 0, 16)):
+            ts(T.xs[:, 64 * a + b:64 * e:4], usrc(b, a, e), 0.015625, None, A.mult, None, ["g%d" % b, "xp%d" % b, "lo"], ["xs%d" % b])
+        quant("q%d" % (t + 1), NC, T.xs[:], ["xs%d" % b for b in range(5)])
+        if t + 1 < R:
+            send_state(t + 1)
+            pick("sl%d" % (t + 1), 128, "lu%d" % (t + 1), 16, lst(L_16, 8), "L_16")
+            if t == 0:
+                quant("qv", 128, T.vt[:], ["vt"])
+
+    pick("q3n", C, "q3", NC, lst(L_NAT, 22), "L_NAT")
+    dma("y", T.oc[:], T.q3n[:].bitcast(dt.uint8), "out", ["q3n"], [])
+    mm("pa", "qv", 0, "q3n", C, ["qv", "qvs"])
+    for k in range(4):
+        dma("s", T.osc[4 * k:4 * k + 4, :], T.q3ns[32 * k:32 * k + 4, :], "out", ["q3ns"], [])
+    cp(T.yb[:], T.pa[:, 0:C], ["pa"], ["yb"])
+    dma("y", T.y[:], T.yb[:], "out", ["yb"], [])
+    for s in SEMAPHORES:
+        if total.get(s):
+            wait("g", (s, total[s]))

@@ -4,7 +4,9 @@ from concourse.mybir import dt, AluOpType, AxisListType, ActivationFunctionType
 C, K, M, R = 352, 160, 44, 3
 STEP = [3, 1, 5]
 NC = 384
+NR = 360
 BIG = float(2 ** 80)
+FAR = float(2 ** 90)
 Q4, U8, F32, BF, I32, U16 = "float8_e4m3fn_x4", "uint8", "float32", "bfloat16", "int32", "uint16"
 
 SCRATCH = {}
@@ -19,36 +21,34 @@ def _mx(name, n):
     _sb(name + "s", n, U8)
 
 
-for _n, _w in (("qu", 128), ("uc", 16), ("su0", 128), ("su1", 128), ("qv", 128), ("qw", 512), ("qe", 512),
-               ("q0n", 368), ("q3", NC), ("q3n", C), ("qz", K)):
+for _n, _w in (("qu", 128), ("su0", 128), ("su1", 128), ("qv", 128), ("qw", 512), ("qe", 512),
+               ("q0", C), ("land0", C), ("q1", NC), ("land1", NC), ("q2", NC), ("land2", NC),
+               ("q3", NC), ("q3n", C), ("qz", K)):
     _mx(_n, _w)
-for _t in range(R):
-    _mx("q%d" % _t, NC)
-    _mx("land%d" % _t, NC)
-    _mx("lu%d" % _t, 16)
-    _mx("sl%d" % _t, 128)
 for _n, _s, _d in (
-        ("xt", 4 * 368, BF), ("ut", 512, BF), ("vt", 512, BF), ("et", 2048, BF), ("xs", 4 * NC, BF),
+        ("xt", 4 * C + 16, BF), ("ut", 512, BF), ("vt", 512, BF), ("et", 2048, BF), ("xs", 4 * NC, BF),
         ("wd", 4 * 544, BF), ("dsb", 4 * NC, BF), ("zall", 4 * NC, BF), ("zt", 4 * K, BF), ("f64", 4 * K, F32),
-        ("pi", 8, I32), ("kc", 16, F32), ("io5", 512, F32), ("m16", NC, F32), ("sm", 64, F32),
-        ("bt", NC, F32), ("jt", C, F32), ("c1", C, F32), ("plc", NC, F32), ("diag", NC, F32),
-        ("mab", 128, F32), ("keep16", 512, BF), ("reset", C, BF), ("keepc", 3 * C, BF),
-        ("keep24", 48, F32), ("mk", 160, F32), ("kt", 22 * 12, F32), ("ki", 22 * 3, I32),
-        ("kw", 24 * 3, F32), ("lc", 284, U16),
-        ("mm", 512, F32), ("ms", 512, F32), ("aa", 32, F32), ("arep", 4 * NC, F32), ("pos1", NC, BF),
+        ("pi", 8, I32), ("kc", 16, F32), ("io1", 128, F32), ("m16", 448, F32), ("sm", 32, F32),
+        ("bt", NC, F32), ("c0", C, F32), ("c1", C, F32), ("plc", NC, F32), ("val", NC, F32),
+        ("diag", 448, F32), ("dq", K, F32), ("keep16", 448, BF), ("reset", C, BF), ("keepc", 3 * NR, BF),
+        ("ones", 64, F32), ("mk", 160, F32), ("kt", 24 * 12, F32), ("ki", 24 * 3, I32),
+        ("kw", 28 * 5, F32), ("lc", 320, U16),
+        ("tp", NC, F32), ("ps", 72, F32), ("lp", 72, F32), ("xb", NC, F32), ("far", NC, F32),
+        ("prow", 392, F32), ("mm", 448, F32), ("ms", 448, F32), ("sg", 2 * NC, BF),
         ("tc", 8, F32), ("ti", 8, I32), ("bl", 66, F32), ("lb", 22, U16),
-        ("dd", 4 * NC, F32), ("ab", 3 * C, F32), ("aw", 4 * NC, F32), ("dm", 1056, F32), ("rr", 1064, F32),
-        ("nf", 1056, F32), ("st", 1056, F32), ("zi", 48, I32), ("lz", 24, U16), ("wb", 32, F32), ("t1", 32, F32),
-        ("xg", 480, F32), ("rw", 480, F32), ("row", C, F32), ("srt", 40, F32), ("cand", 16, F32), ("cnt", 16, F32),
-        ("junk", 13 * C, BF), ("cmp", 3 * C, BF), ("cms", 3 * C, BF), ("pen", 24, F32), ("lh", 40, F32),
+        ("ab", 28 * M, F32), ("aw", 28 * M, F32), ("dm", 3 * C, F32), ("rr", 32 * M, F32), ("lq", 3 * C + 16, BF),
+        ("st", 3 * C, F32), ("zi", 48, I32), ("lz", 24, U16), ("t1", 32, F32),
+        ("xg", 480, F32), ("srt", 40, F32), ("cand", 16, F32), ("cnt", 16, F32),
+        ("junk", 12 * NR, BF), ("cmp", 4 * NR, BF), ("cms", 4 * NR, BF), ("pen", 24, F32), ("lh", 40, F32),
         ("r3", 16, F32), ("xe", 96, F32), ("xf", 96, F32), ("le", 48, F32), ("cs", 48, F32),
-        ("pw", 24 * 10, F32), ("lo", 24, U16), ("win", 544, F32), ("em", K, F32), ("es", K, F32),
+        ("pw", 24 * 10, F32), ("lo", 24, U16), ("win", 544, F32), ("es", K, F32), ("ei", 32, I32),
         ("lk", 10, U16), ("oeb", K, F32), ("yb", C, F32)):
     _sb(_n, _s, _d)
+SCRATCH["rw"] = ("sbuf", [128, 15, 32], F32)
 for _n in ("pa", "pb", "pc", "pd0", "pd1", "pd2", "pd3"):
     SCRATCH[_n] = ("psum", [128, 512], F32)
 
-SEMAPHORES = ["v", "s", "t", "g", "lx", "lu", "lv", "lw", "out", "u0", "u1", "a0", "a1", "a2", "loc"]
+SEMAPHORES = ["v", "s", "t", "g", "lx", "lu", "lv", "lw", "out", "p0", "p1", "p2", "a0", "a1", "a2", "loc"]
 
 A = AluOpType
 AF = ActivationFunctionType
@@ -65,6 +65,7 @@ def rank_program(g, core, T, topo):
     total = {}
     clock = {}
     wrote, read = {}, {}
+    held = []
 
     def wait(q, ev):
         s, n = ev
@@ -76,6 +77,9 @@ def rank_program(g, core, T, topo):
                 known[q][a] = b
 
     def op(q, fn, r, w, sem=None, inc=1):
+        if held:
+            held[-1].append((q, fn, r, w, sem, inc))
+            return
         need = {}
         evs = [wrote[k] for k in list(r) + list(w) if k in wrote]
         for k in w:
@@ -98,6 +102,18 @@ def rank_program(g, core, T, topo):
             wrote[k] = ev
             read[k] = []
 
+    def listed(*fs):
+        ls = []
+        for f in fs:
+            held.append([])
+            f()
+            ls.append(held.pop())
+        return [l[i] for i in range(max(len(l) for l in ls)) for l in ls if i < len(l)]
+
+    def issue(l, n=None):
+        for _ in range(len(l) if n is None else min(n, len(l))):
+            op(*l.pop(0))
+
     V, S, PE = g.vector, g.scalar, g.tensor
 
     def ts(o, i, s1, s2, o0, o1, r, w):
@@ -115,8 +131,8 @@ def rank_program(g, core, T, topo):
     def ms(o, c, w):
         op("v", lambda: V.memset(o, c), [], w)
 
-    def scan(o, a, b, o0, o1, r, w):
-        op("v", lambda: V.tensor_tensor_scan(o, a, b, 0.0, o0, o1), r, w)
+    def scan(o, a, b, o0, o1, r, w, init=0.0):
+        op("v", lambda: V.tensor_tensor_scan(o, a, b, init, o0, o1), r, w)
 
     def red(o, i, f, r, w):
         op("v", lambda: V.tensor_reduce(o, i, X, f), r, w)
@@ -126,6 +142,9 @@ def rank_program(g, core, T, topo):
 
     def act(o, i, f, r, w, **kw):
         op("s", lambda: S.activation(o, i, f, **kw), r, w)
+
+    def fill(o, n, c, w):
+        act(o, T.m16[:, 0:n], AF.Identity, ["m16"], w, bias=c, scale=0.0)
 
     def quant(name, n, tile, r):
         op("v", lambda: V.quantize_mx(T[name][:, 0:n], T[name + "s"][:, 0:n], tile), r, [name, name + "s"])
@@ -152,275 +171,305 @@ def rank_program(g, core, T, topo):
     def dma(q, o, i, sem, r, w):
         op(q, lambda: eng[q].dma_start(o, i), r, w, sem=sem, inc=16)
 
-    def bits(es):
-        return sum(1 << e for e in es)
-
     askers = [T.cores[(rank - STEP[t]) % N] for t in range(R)]
-    ne = min(len(topo.engines(core, d)) for d in askers)
+    ne = min(len(topo.engines(T.cores[r], T.cores[(r - s) % N])) for r in range(N) for s in STEP)
 
-    def send_state(t):
+    def send(t, dst, src, sem, r, w):
         d = askers[t]
         rid, pid = topo.addr(d, core)
-        mask = bits(topo.engines(core, d)[:ne])
+        mask = sum(1 << e for e in topo.engines(core, d)[:ne])
+        op("g", lambda: g.remote_dma(dst, src, T.sem[sem], T.sem.loc, pid, rid, mask), r, [], inc=0)
+        total["loc"] = total.get("loc", 0) + ne
+        total[sem] = total.get(sem, 0) + ne
+        for k in w:
+            wrote[k] = (sem, total[sem])
+
+    def send_state(t):
         q, l = "q%d" % t, "land%d" % t
-        op("g", lambda: g.remote_dma(T[l][:].bitcast(dt.uint8), T[q][:].bitcast(dt.uint8), T.sem["a%d" % t], T.sem.loc,
-                                     pid, rid, mask), [q], [], inc=0)
-        op("g", lambda: g.remote_dma(T[l + "s"][:], T[q + "s"][:], T.sem["a%d" % t], T.sem.loc, pid, rid, mask),
-           [q + "s"], [], inc=0)
-        total["loc"] = total.get("loc", 0) + 2 * ne
-        total["a%d" % t] = 2 * ne
-        wrote[l] = wrote[l + "s"] = ("a%d" % t, 2 * ne)
+        send(t, T[l][:].bitcast(dt.uint8), T[q][:].bitcast(dt.uint8), "a%d" % t, [q], [])
+        send(t, T[l + "s"][:], T[q + "s"][:], "a%d" % t, [q + "s"], [l, l + "s"])
 
-    def send_u(rounds, sem):
-        per = ne // len(rounds)
-        for sfx in ("", "s"):
-            trs = []
-            for i, t in enumerate(rounds):
-                rid, pid = topo.addr(askers[t], core)
-                es = topo.engines(core, askers[t])[per * i:per * (i + 1)]
-                src, dst = T["uc" + sfx][:], T["lu%d%s" % (t, sfx)][:]
-                if not sfx:
-                    src, dst = src.bitcast(dt.uint8), dst.bitcast(dt.uint8)
-                trs.append(RemoteDMATransfer(dst_ids=[DstId(rid=rid, pnc=pid)], dma_engine_mask=bits(es),
-                                             remote_sem=T.sem[sem], src=src, dst=dst))
-            op("g", lambda: g.remote_dma_fused(trs, local_sem=T.sem.loc), ["uc" + sfx], [], inc=0)
-        total["loc"] = total.get("loc", 0) + 2 * ne
-        total[sem] = 2 * ne
-        for t in rounds:
-            wrote["lu%d" % t] = wrote["lu%ds" % t] = (sem, 2 * ne)
-
-    io, kc, lc, kt, kw, mk = T.io5, T.kc, T.lc, T.kt, T.kw, T.mk
+    io, kc, lc, kt, kw, mk = T.io1, T.kc, T.lc, T.kt, T.kw, T.mk
     col = lambda b, i: b[:, i:i + 1]
-    L_U, L_16, L_S, L_ROW, L_0, L_X, L_ABS, L_SUC, L_NAT, L_CMP = 0, 2, 18, 42, 72, 96, 192, 214, 236, 258
+    L_U0, L_U1, L_B, L_ROW, L_OWN, L_X, L_SUC, L_NAT = 0, 8, 16, 40, 70, 126, 222, 244
     lst = lambda a, n: lc[:, a:a + n]
-    k22 = lambda i: kt[:, 22 * i:22 * i + 22]
+    k22 = lambda i: kt[:, 24 * i:24 * i + 22]
+    w28 = lambda i, a=0, e=28: kw[:, 28 * i + a:28 * i + e]
+
+    def own_lists():
+        ts(col(kc, 1), col(kc, 0), 24.0, -4.0, A.mult, A.add, ["q"], ["q24"])
+        ts(col(kc, 3), col(kc, 0), 0.0, None, A.is_equal, None, ["q"], ["qz0"])
+        ts(w28(0), io[:, 0:28], col(kc, 1), None, A.add, None, ["io", "q24"], ["n"])
+        ts(col(kc, 2), col(kc, 3), float(C), col(kc, 1), A.mult, A.add, ["qz0", "q24"], ["k2"])
+        ts(w28(1), w28(0), float(C), float(NC), A.is_ge, A.mult, ["n"], ["pad"])
+        ts(w28(2, 0, 4), io[:, 0:4], col(kc, 2), None, A.add, None, ["io", "k2"], ["o0a"])
+        cp(w28(2, 4, 28), w28(0, 4, 28), ["n"], ["o0b"])
+        tt(w28(3), w28(2), w28(1), A.max, ["o0a", "o0b", "pad"], ["o0"])
+        ts(lst(L_OWN, 28), w28(3), float(NC), None, A.min, None, ["o0"], ["L_OWN0"])
+
+    def own_lists_state():
+        ts(col(kc, 4), col(kc, 3), -113.0, col(kc, 0), A.mult, A.add, ["qz0", "q"], ["k4"])
+        ts(col(kc, 5), col(kc, 0), -64.0, None, A.add, None, ["q"], ["k5"])
+        ts(col(kc, 4), col(kc, 4), 319.0, None, A.add, None, ["k4"], ["k4"])
+        ts(w28(2, 4, 28), io[:, 4:28], 16.0, col(kc, 5), A.mult, A.add, ["io", "k5"], ["o0b"])
+        ts(w28(2, 0, 4), io[:, 0:4], 16.0, col(kc, 4), A.mult, A.add, ["io", "k4"], ["o0a"])
+        ts(w28(4, 0, 24), w28(2, 4, 28), float(K), None, A.add, None, ["o0b"], ["J"])
+        tt(w28(3), w28(2), w28(1), A.max, ["o0a", "o0b", "pad"], ["o0"])
+        ts(lst(L_OWN + 28, 28), w28(3), float(NC), None, A.min, None, ["o0"], ["L_OWN1"])
 
     def tables():
         k = k22
-        ki = lambda i: T.ki[:, 22 * i:22 * i + 22]
+        ki = lambda i: T.ki[:, 24 * i:24 * i + 22]
         ts(k(0), io[:, 0:22], 16.0, col(kc, 0), A.mult, A.add, ["io", "q"], ["e"])
         ts(k(1), k(0), -21.5, 1.0 / M, A.add, A.mult, ["e"], ["k1"])
-        ts(k(9), k(0), -11.5, 1.0 / 24, A.add, A.mult, ["e"], ["k9"])
+        ts(k(7), k(0), 3.0 * M, None, A.add, None, ["e"], ["base"])
         cp(ki(0), k(1), ["k1"], ["si"])
-        cp(ki(2), k(9), ["k9"], ["ni"])
         cp(k(1), ki(0), ["si"], ["sf"])
         ts(k(2), ki(0), -float(M), None, A.mult, None, ["si"], ["k2t"])
-        ts(k(9), ki(2), -383.0, None, A.mult, None, ["ni"], ["k9"])
-        ts(k(10), k(0), 16.0, None, A.mult, None, ["e"], ["k10"])
         tt(k(2), k(2), k(0), A.add, ["k2t", "e"], ["j"])
+        ts(k(6), k(2), 0.0, float(M), A.is_equal, A.mult, ["j"], ["k6"])
+        ts(k(6), k(6), -1.0, None, A.add, None, ["k6"], ["adj"])
+
+    def natural():
+        k = k22
+        ki = T.ki[:, 48:70]
+        ts(k(9), k(0), -11.5, 1.0 / 24, A.add, A.mult, ["e"], ["k9"])
+        ts(k(10), k(0), 16.0, None, A.mult, None, ["e"], ["k10"])
+        cp(ki, k(9), ["k9"], ["ni"])
+        ts(k(9), ki, -383.0, None, A.mult, None, ["ni"], ["k9"])
         tt(k(9), k(9), k(10), A.add, ["k9", "k10"], ["k9"])
-        ts(k(8), ki(2), 8.0, None, A.mult, None, ["ni"], ["k8"])
-        ts(k(3), k(2), -1.0, 1.0 / 3, A.add, A.mult, ["j"], ["k3"])
-        ts(k(4), k(2), 128.0, None, A.mult, None, ["j"], ["k4"])
-        ts(k(5), k(1), 16.0, None, A.mult, None, ["sf"], ["k5"])
         cp(lst(L_NAT, 22), k(9), ["k9"], ["L_NAT"])
-        tt(k(8), k(8), k(0), A.add, ["k8", "e"], ["k8"])
-        cp(ki(1), k(3), ["k3"], ["ai"])
-        tt(k(4), k(4), k(5), A.add, ["k4", "k5"], ["k4"])
-        ts(k(6), k(2), 0.0, -113.0, A.is_equal, A.mult, ["j"], ["k6"])
-        ts(k(11), ki(1), 3.0, None, A.mult, None, ["ai"], ["k11"])
-        ts(k(3), ki(1), -383.0, None, A.mult, None, ["ai"], ["k3"])
-        tt(k(11), k(11), k(2), A.is_equal, ["k11", "j"], ["k11"])
-        tt(k(4), k(4), k(3), A.add, ["k4", "k3"], ["k4"])
-        ts(k(11), k(11), 383.0, -384.0, A.mult, A.add, ["k11"], ["k11"])
-        cp(lst(L_CMP, 12), kt[:, 176:188], ["k8"], ["L_CA"])
-        ts(lst(L_CMP + 12, 10), kt[:, 188:198], -256.0, None, A.add, None, ["k8"], ["L_CB"])
-        tt(k(6), k(6), k(11), A.add, ["k6", "k11"], ["adj"])
-        ts(k(7), k(4), NC - 16.0, None, A.add, None, ["k4"], ["base"])
-        cp(lst(L_ABS, 22), k(4), ["k4"], ["L_ABS"])
 
     def masks():
         ts(T.pi[:, 2:3], T.pi[:, 0:1], 16, None, A.bitwise_and, None, ["pi0"], ["pi2"])
-        ts(kw[:, 24:48], kw[:, 0:24], float(C), BIG, A.is_ge, A.mult, ["n0"], ["pad"])
+        ms(T.ones[:], 1.0, ["ones"])
         cp(col(kc, 9), T.pi[:, 2:3], ["pi2"], ["h"])
-        ts(kw[:, 48:72], io[:, 0:24], 16.0, col(kc, 0), A.mult, A.add, ["io", "q"], ["J"])
+        ts(T.dq[:], T.diag[:, 0:K], BIG, None, A.mult, None, ["diag"], ["dq"])
         ts(col(kc, 10), col(kc, 9), 16.0, None, A.add, None, ["h"], ["h16"])
         tt(col(kc, 11), col(kc, 9), col(kc, 0), A.add, ["h", "q"], ["r32"])
         ts(mk[:, 0:32], io[:, 0:32], col(kc, 9), None, A.is_ge, None, ["io", "h"], ["mk0"])
         ts(mk[:, 64:96], io[:, 0:32], col(kc, 10), None, A.is_lt, None, ["io", "h16"], ["mk2"])
         ts(mk[:, 32:64], io[:, 0:32], col(kc, 11), None, A.is_gt, None, ["io", "r32"], ["mk1"])
-        ts(kw[:, 48:72], kw[:, 48:72], float(K), None, A.add, None, ["J"], ["J"])
+        ts(mk[:, 128:160], io[:, 0:32], col(kc, 11), -1.0, A.is_lt, A.mult, ["io", "r32"], ["mk4"])
         tt(mk[:, 0:32], mk[:, 0:32], mk[:, 64:96], A.mult, ["mk0", "mk2"], ["same"])
         tt(mk[:, 32:64], mk[:, 32:64], mk[:, 64:96], A.mult, ["mk1", "mk2"], ["tri"])
-        ms(T.keep24[:], 1.0, ["keep24"])
         ts(mk[:, 96:128], mk[:, 0:32], -BIG, BIG, A.mult, A.add, ["same"], ["other"])
-        ts(mk[:, 128:160], mk[:, 0:32], -1.0, None, A.mult, None, ["same"], ["nsame"])
-        ms(T.keep24[:, 0::24], 0.0, ["keep24"])
-        ms(T.keepc[:, 0::C], 0.0, ["keepc0", "keepc1", "keepc2"])
+        tt(mk[:, 128:160], mk[:, 128:160], mk[:, 0:32], A.mult, ["mk4", "same"], ["ntri"])
 
     def successors():
-        k = k22
-        ts(k(5), k(1), 7.0, None, A.is_equal, None, ["sf"], ["k5"])
-        ts(k(8), k(1), 1.0, 48.0, A.add, A.mult, ["sf"], ["k8"])
-        tt(k(10), k(5), k(2), A.add, ["k5", "j"], ["k10"])
-        ts(k(5), k(5), -384.0, 1.0, A.mult, A.add, ["k5"], ["k5"])
-        ts(k(11), k(10), M - 1.0, -float(M), A.is_ge, A.mult, ["k10"], ["k11"])
-        tt(k(8), k(8), k(5), A.add, ["k8", "k5"], ["k8"])
-        tt(k(10), k(10), k(11), A.add, ["k10", "k11"], ["k10"])
-        tt(k(8), k(8), k(10), A.add, ["k8", "k10"], ["k8"])
-        cp(lst(L_SUC, 22), k(8), ["k8"], ["L_SUC"])
-        tt(T.c1[:], T.bt[:].indirect(lst(L_SUC, 22)), T.jt[:], A.add, ["bt", "jt", "L_SUC"], ["c1"])
+        runs = [(T.c1[:, M * s:M * s + M - 1], T.bt[:, 48 * s + 49:48 * s + 48 + M], 65) for s in range(7)]
+        runs += [(T.c1[:, M - 1:7 * M:M], T.bt[:, 48::48], 65 - M), (T.c1[:, 7 * M:C - 2], T.bt[:, 2:M], 66),
+                 (T.c1[:, C - 2:C], T.bt[:, 0:2], 66 - M)]
+        for i, (o, a, c) in enumerate(runs):
+            act(o, a, AF.Identity, ["bt"], ["c1" if i == len(runs) - 1 else "c1_%d" % i], bias=512.0 * c)
 
-    dma("y", T.ut[:], T.u[:], "lu", [], ["ut"])
-    dma("s", T.xt[:, 0:4 * C], T.x[:], "lx", [], ["xt"])
-    iota(T.pi[:, 0:1], [[0, 1]], 0, 1, ["pi0"], f=False)
-    iota(io[:], [[1, 512]], 0, 0, ["io"])
-    iota(T.sm[:, 0:24], [[0, 3], [1, 8]], 0, 0, ["sm0"])
-    iota(T.sm[:, 24:54], [[1, 15], [16, 2]], 0, 0, ["sm1"])
-    iota(T.m16[:], [[0, 24], [1, 16]], 0, 0, ["m16"])
-    ms(T.xt[:, 4 * C:], 0.0, ["xz"])
-    for b in range(4):
-        act(T.et[:, 512 * b:512 * b + 512], io[:], AF.Identity, ["io"], ["et%d" % b], bias=1.0, scale=0.0)
-    ms(T.keep16[:], 1.0, ["keep16"])
-    ms(T.reset[:], 0.0, ["reset"])
-    ms(T.aa[:, 0:4], 0.0, ["aaz"])
-    ms(T.aw[:, 0:64], 0.0, ["awz"])
-    ms(T.wb[:, 24:32], BIG, ["wbz"])
-    ms(T.rr[:, 0:8], 0.0, ["rrz"])
-    ms(T.keep16[:, 0::16], 0.0, ["keep16"])
-    ms(T.reset[:, 0::M], BIG, ["reset"])
-    ts(T.pi[:, 1:2], T.pi[:, 0:1], 15, None, A.bitwise_and, None, ["pi0"], ["pi1"])
-    cp(col(kc, 0), T.pi[:, 1:2], ["pi1"], ["q"])
-    ts(col(kc, 1), col(kc, 0), 24.0, None, A.mult, None, ["q"], ["q24"])
-    ts(col(kc, 2), col(kc, 0), 8.0, -127.0, A.is_ge, A.mult, ["q"], ["k2"])
-    ts(col(kc, 3), col(kc, 0), 0.0, None, A.is_equal, None, ["q"], ["qz0"])
-    ts(col(kc, 4), col(kc, 0), -1.0, None, A.add, None, ["q"], ["qm1"])
-    ts(lst(L_U, 1), col(kc, 0), 16.0, col(kc, 2), A.mult, A.add, ["q", "k2"], ["L_U"])
-    ts(kw[:, 0:24], io[:, 0:24], col(kc, 1), float(C), A.add, A.min, ["io", "q24"], ["n0"])
-    cp(lst(L_16, 16), io[:, 0:16], ["io"], ["L_16"])
-    cp(lst(L_0, 24), kw[:, 0:24], ["n0"], ["L_0"])
-    quant("qu", 128, T.ut[:], ["ut"])
-    pick("uc", 16, "qu", 128, lst(L_U, 1), "L_U", on_s=False)
-    send_u([0], "u0")
-    tables()
-    quant("q0n", 368, T.xt[:], ["xt", "xz"])
-    pick("q0", NC, "q0n", 368, lst(L_0, 24), "L_0")
-    send_state(0)
-    iota(T.bt[:], [[16, 8], [1, 16], [128, 3]], 0, 0, ["bt"])
-    iota(T.jt[:], [[0, 8], [-512, M]], 64 * 512, 0, ["jt"])
-    ek = ["et%d" % b for b in range(4)]
-    op("g", lambda: g.affine_select(T.et[:], T.et[:], [[-1, 4], [1, 512]], A.is_equal, 0.0, 0, -4), ek, ek)
-    send_u([1, 2], "u1")
-    iota(T.plc[:], [[1, 24], [24, 16]], 0, 0, ["plc"])
-    pick("su0", 128, "uc", 16, lst(L_16, 8), "L_16")
-    pick("su1", 128, "uc", 16, lst(L_16 + 8, 8), "L_16")
-    for b in range(3):
-        act(T.keepc[:, C * b:C * b + C], io[:, 0:C], AF.Identity, ["io"], ["keepc%d" % b], bias=1.0, scale=0.0)
-    ts(T.diag[:], T.m16[:], col(kc, 0), None, A.is_equal, None, ["m16", "q"], ["diag"])
-    ts(T.mab[:, 0:64], T.m16[:, 0:64], 14.0, col(kc, 3), A.is_equal, A.mult, ["m16", "qz0"], ["ma"])
-    ts(T.mab[:, 64:128], T.m16[:, 0:64], col(kc, 4), None, A.is_equal, None, ["m16", "qm1"], ["mb"])
-    cp(lst(L_S, 54), T.sm[:, 0:54], ["sm0", "sm1"], ["L_S"])
-    for b in range(4):
-        ts(lst(L_X + 24 * b, 24), kw[:, 0:24], 4.0, float(b), A.mult, A.add, ["n0"], ["L_X%d" % b])
-
-    wd = T.wd
-    xpl = lambda b: wd[:, 544 * b + K:544 * b + 544]
-    for t in range(R):
-        q, land, sl = "q%d" % t, "land%d" % t, "sl%d" % t
-        mm("pa", "su0", 0, q, NC, ["su0", "su0s"])
-        mm("pb", "su1", 0, q, NC, ["su1", "su1s"])
-        tt(T.mm[:, 0:NC], T.pa[:, 0:NC], T.diag[:], A.mult, ["pa", "diag"], ["mm0"])
-        tt(T.mm[:, 384:448], T.pa[:, 192:256], T.mab[:, 0:64], A.mult, ["pa", "ma"], ["mm1"])
-        tt(T.mm[:, 448:512], T.pa[:, 320:384], T.mab[:, 64:128], A.mult, ["pa", "mb"], ["mm2"])
-        scan(T.ms[:], T.keep16[:], T.mm[:], A.mult, A.add, ["keep16", "mm0", "mm1", "mm2"], ["ms"])
-        cp(T.aa[:, 8:32], T.ms[:, 15:384:16], ["ms"], ["aa1"])
-        tt(T.aa[:, 4:8], T.ms[:, 399:448:16], T.ms[:, 463:512:16], A.add, ["ms"], ["aa0"])
-        for kb in (1, 2, 3):
-            act(T.arep[:, NC * kb:NC * kb + NC], T.aa[:, 8 * kb:8 * kb + 8].indirect(lst(L_S, 24)), AF.Copy,
-                ["aa1", "L_S"], ["arep%d" % kb])
-        if t == 0:
-            pick(sl, 128, "lu0", 16, lst(L_16, 8), "L_16")
+    def plane_lists():
+        ts(w28(3, 0, 24), w28(0, 4, 28), float(C), None, A.min, None, ["n", "L_OWN0"], ["n0", "o0"])
         for b in range(4):
-            if t == 0:
-                act(xpl(b), T.xt[:].indirect(lst(L_X + 24 * b, 24)), AF.Copy, ["xt", "xz", "L_X%d" % b], ["xp%d" % b], scale=64.0)
-            else:
-                act(xpl(b), T.xs[:, b::4], AF.Copy, ["xs%d" % b, "xs4"], ["xp%d" % b], scale=64.0)
-        cp(T.arep[:, 64:NC], T.aa[:, 0:8].indirect(lst(L_S + 4, 20)), ["aa0", "aaz", "L_S"], ["arep0"])
-        ts(T.pos1[:], T.pb[:, 0:NC], 0.0, None, A.is_gt, None, ["pb"], ["pos1"])
-        red(col(T.tc, 0), T.pos1[:], A.add, ["pos1"], ["tc0"])
+            ts(lst(L_X + 24 * b, 24), w28(3, 0, 24), 4.0, float(b), A.mult, A.add, ["n0", "o0"], ["L_X%d" % b])
+
+    def resets():
+        ms(T.reset[:, 0::M], BIG, ["reset"])
+        ms(T.rr[:, 24 * M + M - 1::M], BIG, ["rrz"])
+        cp(lst(L_ROW, 30), T.sm[:, 0:30], ["sm"], ["L_ROW"])
+        ts(T.c0[:, M - 1::M], T.c0[:, M - 1::M], -float(C), None, A.add, None, ["c0"], ["c0"])
+        ms(T.lq[:, 0::M], 0.0, ["lqz"])
+        ts(col(T.c0, C - 2), col(T.c0, C - 2), -float(C), None, A.add, None, ["c0"], ["c0"])
+        ms(T.keepc[:, 0::NR], 0.0, ["keepc%d" % b for b in range(3)])
+
+    def delay_list():
         cp(col(T.ti, 0), col(T.tc, 0), ["tc0"], ["ti0"])
         ts(col(T.ti, 1), col(T.ti, 0), 3, None, A.bitwise_and, None, ["ti0"], ["ti1"])
         cp(col(T.tc, 1), col(T.ti, 1), ["ti1"], ["tc1"])
-        ts(col(T.tc, 2), col(T.ti, 1), -16.0, None, A.mult, None, ["ti1"], ["tc2"])
+        ts(col(T.tc, 2), col(T.ti, 1), -float(M), None, A.mult, None, ["ti1"], ["tc2"])
         ts(T.bl[:, 0:22], k22(1), col(T.tc, 1), None, A.is_le, None, ["sf", "tc1"], ["bl0"])
         tt(T.bl[:, 22:44], T.bl[:, 0:22], k22(6), A.mult, ["bl0", "adj"], ["bl1"])
         tt(T.bl[:, 44:66], T.bl[:, 22:44], k22(7), A.add, ["bl1", "base"], ["bl2"])
         ts(T.lb[:], T.bl[:, 44:66], col(T.tc, 2), None, A.add, None, ["bl2", "tc2"], ["lb"])
+
+    def unit_tiles():
+        for b in range(4):
+            ts(T.et[:, 512 * b + b:512 * b + 512:4], io[:], col(kc, 6), None, A.is_equal, None, ["io", "p", "etz"], ["et%d" % b])
+        quant("qe", 512, T.et[:], ["et%d" % b for b in range(4)])
+
+    dma("y", T.ut[:], T.u[:], "lu", [], ["ut"])
+    dma("s", T.xt[:, 0:4 * C], T.x[:], "lx", [], ["xt"])
+    iota(T.pi[:, 0:1], [[0, 1]], 0, 1, ["pi0"], f=False)
+    iota(io[:], [[1, 128]], 0, 0, ["io"])
+    iota(T.m16[:], [[0, 28], [1, 16]], 0, 0, ["m16"])
+    iota(T.sm[:, 0:30], [[1, 15], [16, 2]], 0, 0, ["sm"])
+    iota(T.c0[:], [[1, 8], [8 - 512, M]], 64 * 512 + 9, 0, ["c0"])
+    iota(T.val[:], [[512 + 16, 24], [24 * 512 + 1, 16]], 0, 0, ["val"])
+    ms(T.et[:], 0.0, ["etz"])
+    ts(T.pi[:, 1:2], T.pi[:, 0:1], 15, None, A.bitwise_and, None, ["pi0"], ["pi1"])
+    cp(col(kc, 6), T.pi[:, 0:1], ["pi0"], ["p"])
+    ts(lst(L_U0, 8), io[:, 0:8], 16.0, None, A.mult, None, ["io"], ["L_U0"])
+    ts(lst(L_U1, 8), io[:, 0:8], 16.0, 1.0, A.mult, A.add, ["io"], ["L_U1"])
+    cp(col(kc, 0), T.pi[:, 1:2], ["pi1"], ["q"])
+    cp(lst(L_B, 24), io[:, 0:24], ["io"], ["L_B"])
+    ms(T.xt[:, 4 * C:], 0.0, ["xz"])
+    ms(T.prow[:, C:], FAR, ["prz", "prow"])
+    own_lists()
+    fill(T.keep16[:], 448, 1.0, ["keep16"])
+    fill(T.reset[:], C, 0.0, ["reset"])
+    quant("qu", 128, T.ut[:], ["ut"])
+    pick("su0", 128, "qu", 128, lst(L_U0, 8), "L_U0")
+    ts(T.diag[:], T.m16[:], col(kc, 0), None, A.is_equal, None, ["m16", "q"], ["diag"])
+    quant("q0", C, T.xt[:, 0:4 * C], ["xt"])
+    pick("su1", 128, "qu", 128, lst(L_U1, 8), "L_U1")
+    for b in range(3):
+        fill(T.keepc[:, NR * b:NR * b + NR], NR, 1.0, ["keepc%d" % b])
+
+    wd, rr, rw = T.wd, T.rr, T.rw
+    xpl = lambda b: wd[:, 544 * b + K:544 * b + 544]
+    Wv = lambda a, e: rr[:, M * a + M - 1:M * e:M]
+    row = rw[:, :, 0:24]
+    half = 2 * K - NR - 0.5
+    for t in range(R):
+        q, land = "q%d" % t, "land%d" % t
+        n = C if t == 0 else NC
+        nb = n // 16
+        mm("pa", "su0", 0, q, n, ["su0", "su0s"])
+        mm("pc", "su0", 0, q, n, ["su0", "su0s"])
+        mm("pb", "su1", 0, q, n, ["su1", "su1s"])
+        tr(T.tp[:, 0:n], T.pa[:, 0:n], ["pa"], ["tp"])
+        cp(T.ps[:, 24 * t:24 * t + nb], T.tp[:, 0:n:16], ["tp"], ["ps%d" % t])
+        send(t, T.lp[:, 24 * t:24 * t + nb], T.ps[:, 24 * t:24 * t + nb], "p%d" % t, ["ps%d" % t], ["lp%d" % t])
+        send_state(t)
+        act(T.prow[:, 0:n], T.pc[:, 0:n], AF.Copy, ["pc"], ["prow"])
+        act(T.sg[:, 0:n], T.pb[:, 0:n], AF.Sign, ["pb"], ["sg0"])
+        act(T.sg[:, NC:NC + n], T.sg[:, 0:n], AF.Relu, ["sg0"], ["sg1", "tc0"], accum_out=col(T.tc, 0))
         if t == 0:
-            masks()
+            iota(T.bt[:], [[16, 8], [1 - 3 * 512, 16], [128 - 512, 3]], 0, 0, ["bt"])
+            iota(T.plc[:], [[1, 24], [24, 16]], 0, 0, ["plc"])
+            ms(T.keep16[:, 0::16], 0.0, ["keep16"])
+            plane_lists()
+        if t == 1:
             successors()
-        mm("pc", sl, 0, land, NC, [sl, sl + "s"])
+        own = "L_OWN%d" % min(t, 1)
+        tt(T.mm[:], T.prow[:].indirect(lst(L_OWN + 28 * min(t, 1), 28)), T.diag[:], A.mult, ["prow", "prz", own, "diag"], ["mm"])
+        scan(T.ms[:], T.keep16[:], T.mm[:], A.mult, A.add, ["keep16", "mm"], ["ms"])
         if t == 0:
+            for b in (0, 1):
+                act(xpl(b), T.xt[:].indirect(lst(L_X + 24 * b, 24)), AF.Copy, ["xt", "xz", "L_X%d" % b], ["xp%d" % b], scale=64.0)
+            issue(listed(tables, resets))
+            spare = listed(unit_tiles) + listed(masks, own_lists_state)
+            issue(spare, 4)
+        else:
+            for b in range(4):
+                ts(xpl(b), T.xs[:, b::4], 64.0, None, A.mult, None, ["xs%d" % b, "xs4"], ["xp%d" % b])
+        lw = T.lp[:, 24 * t:24 * t + nb]
+        cuts = ((0, 8), (8, 16), (16, nb))
+        for i, (a, e) in enumerate(cuts):
+            src, key = lw.indirect(lst(L_B + a, e - a)), ["lp%d" % t, "L_B"]
+            if i == 0:
+                cp(T.xb[:, 16 * a:16 * e], src, key, ["xb%d" % i])
+            else:
+                act(T.xb[:, 16 * a:16 * e], src, AF.Copy, key, ["xb%d" % i])
+        for i, (a, e) in enumerate(cuts):
+            tr(T.far[:, 16 * a:16 * e] if t == 0 else T.far[:, i::3], T.xb[:, 16 * a:16 * e], ["xb%d" % i], ["far%d" % i])
+        rows = [("ab", c) for c in range(11)] + [("aw", 10), ("aw", 11)] + [("ab", c) for c in range(11, 19)] + [("aw", 19)]
+        rows += [("ab", c) for c in range(19, 27)] + [("aw", c) for c in range(20, 28)]
+        for buf, c in rows:
+            s = (c - 4) % 8
+            act(T[buf][:, M * c:M * c + M], T.far[:, s:C:8] if t == 0 else T.far[:, 48 * s:48 * s + M], AF.Abs,
+                ["far0", "far1", "far2", "ms"], ["%s%d" % (buf, c)], bias=col(T.ms, 16 * c + 15), scale=-1.0)
+        if t == 0:
+            issue(listed(delay_list, lambda: issue(spare, 3)))
             wait("y", wrote[land])
             dma("y", T.qw[:].bitcast(dt.uint8), T.wc[:], "lw", [], ["qw"])
             dma("y", T.qws[:], T.ws[:], "lw", [], ["qw"])
             dma("y", T.vt[:], T.v[:], "lv", [], ["vt"])
-        for kb in range(4):
-            a, e = NC * kb + (64 if kb == 0 else 0), NC * kb + NC
-            tt(T.dd[:, a:e], T.pc[:, a - NC * kb:NC], T.arep[:, a:e], A.subtract, ["pc", "arep%d" % kb], ["dd%d" % kb])
-            act(T.aw[:, a:e], T.dd[:, a:e], AF.Abs, ["dd%d" % kb], ["aw%d" % kb])
-            if kb:
-                act(T.ab[:, C * kb - C:C * kb], T.dd[:, a:e].indirect(lst(L_ABS, 22)), AF.Abs, ["dd%d" % kb, "L_ABS"], ["ab%d" % kb])
-        if t == 0:
-            quant("qe", 512, T.et[:], ek)
+        elif t == 1:
+            issue(listed(delay_list, natural))
+        else:
+            delay_list()
+            quant("qv", 128, T.vt[:], ["vt"])
         for b in range(4):
-            mm("pd%d" % b, "qe", 128 * b, land, NC, ["qe", "qes"])
-        for k in range(3):
-            tt(T.dm[:, C * k:C * k + C], T.aw[:, NC * k:NC * k + 2 * NC].indirect(T.lb[:]), T.ab[:, C * k:C * k + C],
-               A.max, ["aw%d" % k, "aw%d" % (k + 1), "awz", "ab%d" % (k + 1), "lb"], ["dm%d" % k])
-            scan(T.rr[:, 8 + C * k:8 + C * k + C], T.reset[:], T.dm[:, C * k:C * k + C], A.max, A.min,
+            mm("pd%d" % b, "qe", 128 * b, land, n, ["qe", "qes"])
+        def again(a, e):
+            cp(T.aw[:, M * a:M * e], T.ab[:, M * a:M * e], ["ab%d" % c for c in range(a, e)], ["aw%d" % c for c in range(a, e)])
+
+        def larger(k):
+            tt(T.dm[:, C * k:C * k + C], T.ab[:, C * k:C * k + 11 * M].indirect(T.lb[:]), T.aw[:, C * k + 4 * M:C * k + 12 * M],
+               A.max, ["ab%d" % c for c in range(8 * k, 8 * k + 11)] + ["aw%d" % c for c in range(8 * k + 4, 8 * k + 12)] + ["lb"],
+               ["dm%d" % k])
+
+        def least(k):
+            scan(rr[:, C * k:C * k + C], T.reset[:], T.dm[:, C * k:C * k + C], A.max, A.min,
                  ["reset", "dm%d" % k], ["rr%d" % k])
-        unpack = lambda b: act(T.dsb[:, NC * b:NC * b + NC], T["pd%d" % b][:, 0:NC], AF.Copy, ["pd%d" % b], ["dsb%d" % b])
+        again(4, 10)
+        larger(0)
+        again(12, 15)
+        least(0)
+        again(15, 19)
+        larger(1)
+        least(1)
+        larger(2)
+        least(2)
+        unpack = lambda b: act(T.dsb[:, NC * b:NC * b + n], T["pd%d" % b][:, 0:n], AF.Copy, ["pd%d" % b], ["dsb%d" % b])
         unpack(0)
         unpack(1)
-        W = T.wb
-        tt(W[:, 0:24], T.rr[:, 8 + M - 1:1064:M], kw[:, 24:48], A.max, ["rr0", "rr1", "rr2", "pad"], ["W"])
-        tr(T.t1[:], W[:], ["W", "wbz"], ["t1"])
+        rk = ["rr0", "rr1", "rr2"]
         s8 = lambda i: T.srt[:, 8 * i:8 * i + 8]
-        act(T.xg[:, 0:256], T.t1[:].indirect(lst(L_ROW, 16)), AF.Copy, ["t1", "L_S"], ["xg0"])
-        cp(T.xg[:, 256:480], T.t1[:].indirect(lst(L_ROW + 16, 14)), ["t1", "L_S"], ["xg1"])
-        tt(s8(0), W[:, 0:8], W[:, 8:16], A.min, ["W"], ["s0"])
-        tr(T.rw[:, 256:480], T.xg[:, 256:480], ["xg1"], ["rw1"])
-        act(T.row[:, 192:C], T.rw[:, 256:480].indirect(lst(L_CMP + 12, 10)), AF.Copy, ["rw1", "L_CB"], ["row1"])
-        tr(T.rw[:, 0:256], T.xg[:, 0:256], ["xg0"], ["rw0"])
-        tt(s8(1), W[:, 0:8], W[:, 8:16], A.max, ["W"], ["s1"])
-        cp(T.row[:, 0:192], T.rw[:, 0:256].indirect(lst(L_CMP, 12)), ["rw0", "L_CA"], ["row0"])
-        tt(s8(2), s8(1), W[:, 16:24], A.min, ["W", "s1"], ["s2"])
-        tt(s8(3), s8(0), W[:, 16:24], A.min, ["W", "s0"], ["low"])
+        tr(T.t1[:], Wv(0, 32), rk + ["rrz"], ["t1"])
+        tt(s8(0), Wv(0, 8), Wv(8, 16), A.min, rk, ["s0"])
+        act(T.xg[:, 0:288], T.t1[:].indirect(lst(L_ROW, 18)), AF.Copy, ["t1", "L_ROW"], ["xg0"])
+        cp(T.xg[:, 288:480], T.t1[:].indirect(lst(L_ROW + 18, 12)), ["t1", "L_ROW"], ["xg1"])
+        tt(s8(1), Wv(0, 8), Wv(8, 16), A.max, rk, ["s1"])
+        tr(rw[:, 9:15, :], T.xg[:, 288:480], ["xg1"], ["rw1"])
+        tt(s8(2), s8(1), Wv(16, 24), A.min, rk + ["s1"], ["s2"])
+        tr(rw[:, 0:9, :], T.xg[:, 0:288], ["xg0"], ["rw0"])
         tt(T.cand[:, 0:8], s8(0), s8(2), A.max, ["s0", "s2"], ["mid"])
-        tt(s8(4), s8(1), W[:, 16:24], A.max, ["W", "s1"], ["upp"])
+        rwk = ["rw0", "rw1"]
 
-        def count(i, key):
-            act(T.junk[:, C * i:C * i + C], T.row[:], AF.Sign, ["row0", "row1", key], ["junk%d" % i, "cnt%d" % i],
+        def count(i, j, key):
+            act(T.junk[:, NR * j:NR * j + NR], row, AF.Sign, rwk + [key], ["junk%d" % j, "cnt%d" % i],
                 bias=col(T.cand, i), scale=-1.0, accum_out=col(T.cnt, i))
-        for i in range(8):
-            count(i, "mid")
-        tt(T.nf[:], T.rr[:, 8:1064], T.rr[:, 7:1063], A.is_ge, ["rr0", "rr1", "rr2", "rrz"], ["nf"])
+
+        def less(i, j, key):
+            ts(T.cmp[:, NR * j:NR * j + NR], row, col(T.cand, i), None, A.is_lt, None, rwk + [key], ["cmp%d" % j])
+        for i in range(7):
+            count(i, i, "mid")
+        tt(s8(3), s8(0), Wv(16, 24), A.min, rk + ["s0"], ["low"])
+        tt(s8(4), s8(1), Wv(16, 24), A.max, rk + ["s1"], ["upp"])
+        less(7, 3, "mid")
+        for c in range(24):
+            ts(T.lq[:, M * c + 1:M * c + M], rr[:, M * c:M * c + M - 1], col(rr, M * c + M - 1), None, A.is_le, None,
+               rk + ["lqz"], ["lq%d" % c])
+            if c == 0:
+                scan(T.cms[:, 3 * NR:], T.keepc[:, 0:NR], T.cmp[:, 3 * NR:], A.mult, A.add, ["keepc0", "cmp3"], ["cms3"])
+        cc = "c%d" % min(t, 1)
         for k in range(3):
-            scan(T.st[:, C * k:C * k + C], T.nf[:, C * k:C * k + C], T.c1[:], A.mult, A.max, ["nf", "c1"], ["st%d" % k])
-        cp(T.zi[:, 0:24], T.st[:, M - 1::M], ["st0", "st1", "st2"], ["zi0"])
-        ts(T.zi[:, 24:48], T.zi[:, 0:24], 511, None, A.bitwise_and, None, ["zi0"], ["zi1"])
+            scan(T.st[:, C * k:C * k + C], T.lq[:, C * k:C * k + C], T[cc][:], A.mult, A.max,
+                 ["lq%d" % c for c in range(8 * k, 8 * k + 8)] + [cc], ["st%d" % k])
         pen, lh, r3 = T.pen, T.lh, T.r3
-        c8 = ["cnt%d" % i for i in range(8)]
-        half = 2 * K - C - 0.5
-        ts(pen[:, 8:16], T.cnt[:, 0:8], half, BIG, A.is_lt, A.mult, c8, ["pen1"])
-        cp(T.lz[:], T.zi[:, 24:48], ["zi1"], ["lz"])
-        tt(lh[:, 32:40], s8(4), pen[:, 8:16], A.min, ["upp", "pen1"], ["lh2"])
+        ts(col(pen, 15), col(T.cms, 4 * NR - 1), K - 0.5, BIG, A.is_lt, A.mult, ["cms3"], ["pen1b"])
+        ts(pen[:, 8:15], T.cnt[:, 0:7], half, BIG, A.is_lt, A.mult, ["cnt%d" % i for i in range(7)], ["pen1a"])
+        cp(T.zi[:, 0:24], T.st[:, M - 1::M], ["st0", "st1", "st2"], ["zi0"])
+        tt(lh[:, 32:40], s8(4), pen[:, 8:16], A.min, ["upp", "pen1a", "pen1b"], ["lh2"])
+        ts(T.zi[:, 24:48], T.zi[:, 0:24], 511, None, A.bitwise_and, None, ["zi0"], ["zi1"])
         tt(T.cand[:, 8:16], lh[:, 32:40], s8(3), A.max, ["lh2", "low"], ["nxt"])
+        cp(T.lz[:], T.zi[:, 24:48], ["zi1"], ["lz"])
         for i in range(8, 13):
-            count(i, "nxt")
+            count(i, i - 1, "nxt")
         for i in range(3):
-            ts(T.cmp[:, C * i:C * i + C], T.row[:], col(T.cand, 13 + i), None, A.is_lt, None, ["row0", "row1", "nxt"], ["cmp%d" % i])
-        ts(pen[:, 0:8], T.cnt[:, 0:8], half, BIG, A.is_lt, A.mult, c8, ["pen0"])
-        scan(T.cms[:], T.keepc[:], T.cmp[:], A.mult, A.add, ["keepc0", "cmp0", "cmp1", "cmp2"], ["cms"])
-        unpack(2)
-        unpack(3)
+            less(13 + i, i, "nxt")
+        cp(pen[:, 0:8], pen[:, 8:16], ["pen1a", "pen1b"], ["pen0"])
+        scan(T.cms[:, 0:3 * NR], T.keepc[:, 0:3 * NR], T.cmp[:, 0:3 * NR], A.mult, A.add, ["keepc0", "cmp0", "cmp1", "cmp2"], ["cms"])
+        if t == 0:
+            issue(spare)
+        for b in (2, 3):
+            unpack(b)
         for b in range(4):
-            act(T.zall[:, NC * b:NC * b + NC], T.dsb[:, NC * b:NC * b + NC].indirect(T.lz[:]), AF.Copy,
+            act(T.zall[:, NC * b:NC * b + NC], T.dsb[:, NC * b:NC * b + n].indirect(T.lz[:]), AF.Copy,
                 ["dsb%d" % b, "lz"], ["zall%d" % b])
-        ts(pen[:, 21:24], T.cms[:, C - 1::C], K - 0.5, BIG, A.is_lt, A.mult, ["cms"], ["pen3"])
+        if t == 0:
+            for b in (2, 3):
+                act(xpl(b), T.xt[:].indirect(lst(L_X + 24 * b, 24)), AF.Copy, ["xt", "xz", "L_X%d" % b], ["xp%d" % b], scale=64.0)
+        ts(pen[:, 21:24], T.cms[:, NR - 1:3 * NR:NR], K - 0.5, BIG, A.is_lt, A.mult, ["cms"], ["pen3"])
         ts(pen[:, 16:21], T.cnt[:, 8:13], half, BIG, A.is_lt, A.mult, ["cnt%d" % i for i in range(8, 13)], ["pen2"])
-        pk = ["pen1", "pen2", "pen3"]
+        pk = ["pen1a", "pen1b", "pen2", "pen3"]
         tt(lh[:, 0:16], T.cand[:], pen[:, 8:24], A.min, ["mid", "nxt"] + pk, ["lh0"])
         tt(lh[:, 16:32], T.cand[:], pen[:, 8:24], A.max, ["mid", "nxt"] + pk, ["lh1"])
         red(col(r3, 2), pen[:], A.add, pk + ["pen0"], ["r2"])
@@ -438,31 +487,31 @@ def rank_program(g, core, T, topo):
         tt(col(r3, 7), col(r3, 6), col(r3, 3), A.max, ["r6", "r3"], ["tau"])
         tau = col(r3, 7)
         p24 = lambda i: T.pw[:, 24 * i:24 * i + 24]
-        ts(T.le[:, 0:24], W[:, 0:24], tau, None, A.is_lt, None, ["W", "tau"], ["lt"])
-        ts(T.le[:, 24:48], W[:, 0:24], tau, None, A.is_equal, None, ["W", "tau"], ["eq"])
-        ts(p24(0), W[:, 0:24], tau, 1000.0, A.is_gt, A.mult, ["W", "tau"], ["p0"])
-        scan(T.cs[:], T.keep24[:], T.le[:], A.mult, A.add, ["keep24", "lt", "eq"], ["cs"])
-        ts(p24(1), W[:, 0:24], tau, 1000.0, A.is_equal, A.mult, ["W", "tau"], ["p1"])
-        ts(xe[:, 0:32], mk[:, 32:64], col(T.cs, 23), None, A.mult, None, ["tri", "cs"], ["xe0"])
-        ts(xe[:, 32:64], mk[:, 32:64], col(T.cs, 47), None, A.mult, None, ["tri", "cs"], ["xe1"])
-        ts(xe[:, 64:96], mk[:, 128:160], col(T.cs, 23), K / 32.0, A.mult, A.add, ["nsame", "cs"], ["xe2"])
-        tr(xf[:], xe[:], ["xe0", "xe1", "xe2"], ["xf"])
-        tt(p24(2), T.cs[:, 0:24], p24(0), A.add, ["cs", "p0"], ["p2"])
-        red(col(r3, 9), xf[:, 32:64], A.add, ["xf"], ["r9"])
-        red(col(r3, 10), xf[:, 64:96], A.add, ["xf"], ["r10"])
+        W, cs = Wv(0, 24), T.cs
+        ts(T.le[:, 0:24], W, tau, None, A.is_lt, None, rk + ["tau"], ["lt"])
+        ts(T.le[:, 24:48], W, tau, None, A.is_equal, None, rk + ["tau"], ["eq"])
+        ts(p24(0), W, tau, 1000.0, A.is_gt, A.mult, rk + ["tau"], ["p0"])
+        scan(cs[:], T.ones[:, 0:48], T.le[:], A.mult, A.add, ["ones", "lt", "eq"], ["cs"])
+        ts(p24(1), W, tau, None, A.is_ge, None, rk + ["tau"], ["p1"])
+        ts(xe[:, 0:32], mk[:, 32:64], col(cs, 47), None, A.mult, None, ["tri", "cs"], ["xe0"])
+        ts(xe[:, 32:64], mk[:, 128:160], col(cs, 23), K / 32.0, A.mult, A.add, ["ntri", "cs"], ["xe1"])
+        tt(p24(2), cs[:, 24:48], p24(0), A.add, ["cs", "p0"], ["p2"])
+        tr(xf[:, 0:64], xe[:, 0:64], ["xe0", "xe1"], ["xf"])
+        tt(p24(3), p24(1), w28(4, 0, 24), A.mult, ["p1", "J"], ["p3"])
         red(col(r3, 8), xf[:, 0:32], A.add, ["xf"], ["r8"])
-        ts(p24(3), T.cs[:, 24:48], col(r3, 9), col(r3, 10), A.add, A.min, ["cs", "r9", "r10"], ["p3"])
-        ts(p24(4), T.cs[:, 24:48], col(r3, 9), col(r3, 10), A.add, A.is_gt, ["cs", "r9", "r10"], ["p4"])
-        ts(p24(5), p24(2), col(r3, 8), -1.0, A.add, A.add, ["p2", "r8"], ["p5"])
-        tt(p24(6), p24(4), p24(1), A.mult, ["p4", "p1"], ["p6"])
-        tt(p24(7), p24(3), p24(5), A.add, ["p3", "p5"], ["p7"])
-        tt(p24(8), p24(6), p24(7), A.add, ["p6", "p7"], ["p8"])
-        tt(p24(9), p24(8), kw[:, 48:72], A.min, ["p8", "J"], ["p9"])
+        red(col(r3, 9), xf[:, 32:64], A.add, ["xf"], ["r9"])
+        ts(p24(4), cs[:, 0:24], col(cs, 23), -1.0, A.subtract, A.add, ["cs"], ["p4"])
+        ts(p24(5), p24(2), col(r3, 8), col(r3, 9), A.add, A.is_gt, ["p2", "r8", "r9"], ["p5"])
+        ts(p24(6), cs[:, 24:48], col(r3, 8), col(r3, 9), A.add, A.min, ["cs", "r8", "r9"], ["p6"])
+        tt(p24(7), p24(5), p24(3), A.mult, ["p5", "p3"], ["p7"])
+        tt(p24(8), p24(6), p24(4), A.add, ["p6", "p4"], ["p8"])
+        tt(p24(9), p24(8), p24(7), A.max, ["p7", "p8"], ["p9"])
         cp(T.lo[:], p24(9), ["p9"], ["lo"])
-        cp(T.win[:].indirect(T.lo[:]), io[:, 0:NC], ["lo", "io"], ["win"])
-        tt(T.em[:], T.win[:, 0:K], T.diag[:, 0:K], A.mult, ["win", "diag"], ["em"])
-        scan(T.es[:], T.keep16[:, 0:K], T.em[:], A.mult, A.add, ["keep16", "em"], ["es"])
-        cp(T.lk[:], T.es[:, 15::16], ["es"], ["lk"])
+        cp(T.win[:].indirect(T.lo[:]), T.val[:], ["lo", "val"], ["win"])
+        scan(T.es[:], T.dq[:], T.win[:, 0:K], A.max, A.min, ["dq", "win"], ["es"])
+        cp(T.ei[:, 0:10], T.es[:, 15::16], ["es"], ["ei0"])
+        ts(T.ei[:, 16:26], T.ei[:, 0:10], 511, None, A.bitwise_and, None, ["ei0"], ["ei1"])
+        cp(T.lk[:], T.ei[:, 16:26], ["ei1"], ["lk"])
         zsrc = lambda b: T.zall[:, NC * b:NC * b + NC].indirect(T.lk[:])
         for b in (0, 1):
             cp(T.zt[:, b::4], zsrc(b), ["zall%d" % b, "lk"], ["zt%d" % b])
@@ -473,30 +522,24 @@ def rank_program(g, core, T, topo):
         quant("qz", K, T.zt[:], ["zt%d" % b for b in range(4)])
         for b in (2, 3, 0, 1):
             mm("pd%d" % b, "qw", 128 * b, "qz", K, ["qw"])
-        for b in (0, 1):
-            cp(T.f64[:, K * b:K * b + K], xpl(b).indirect(T.lk[:]), ["xp%d" % b, "lk"], ["f%d" % b])
-        if t + 1 == R:
-            act(T.oeb[:], T.plc[:].indirect(T.lk[:]), AF.Copy, ["plc", "lk"], ["oeb"])
-            for k in range(8):
-                dma("y", T.oe[k:k + 1, :], T.oeb[16 * k:16 * k + 1, :], "out", ["oeb"], [])
         for b in (2, 3, 0, 1):
+            if b in (2, 1):
+                h = b % 2
+                cp(T.f64[:, K * h:K * h + K], xpl(h).indirect(T.lk[:]), ["xp%d" % h, "lk"], ["f%d" % h])
             tt(wd[:, 544 * b:544 * b + K], T["pd%d" % b][:, 0:K], T.f64[:, K * b:K * b + K], A.add,
                ["pd%d" % b, "f%d" % b], ["g%d" % b])
         usrc = lambda b, a, e: wd[:, 544 * b:544 * b + 544].indirect(T.lo[:, a:e])
-        for b, a, e, key in ((2, 0, 24, "xs2"), (3, 0, 24, "xs3"), (1, 16, 24, "xs4")):
+        for b, a, e, key in ((2, 0, 24, "xs2"), (3, 0, 24, "xs3"), (1, 10, 24, "xs4")):
             act(T.xs[:, 64 * a + b:64 * e:4], usrc(b, a, e), AF.Copy, ["g%d" % b, "xp%d" % b, "lo"], [key], scale=0.015625)
-        for b, a, e in ((0, 0, 24), (1, 0, 16)):
+        for b, a, e in ((0, 0, 24), (1, 0, 10)):
             ts(T.xs[:, 64 * a + b:64 * e:4], usrc(b, a, e), 0.015625, None, A.mult, None, ["g%d" % b, "xp%d" % b, "lo"], ["xs%d" % b])
         quant("q%d" % (t + 1), NC, T.xs[:], ["xs%d" % b for b in range(5)])
-        if t + 1 < R:
-            send_state(t + 1)
-            pick("sl%d" % (t + 1), 128, "lu%d" % (t + 1), 16, lst(L_16, 8), "L_16")
-            if t == 0:
-                quant("qv", 128, T.vt[:], ["vt"])
 
     pick("q3n", C, "q3", NC, lst(L_NAT, 22), "L_NAT")
     dma("y", T.oc[:], T.q3n[:].bitcast(dt.uint8), "out", ["q3n"], [])
     mm("pa", "qv", 0, "q3n", C, ["qv", "qvs"])
+    act(T.oeb[:], T.plc[:].indirect(T.lk[:]), AF.Copy, ["plc", "lk"], ["oeb"])
+    dma("s", T.oe[:], T.oeb[0:128:16, :], "out", ["oeb"], [])
     for k in range(4):
         dma("s", T.osc[4 * k:4 * k + 4, :], T.q3ns[32 * k:32 * k + 4, :], "out", ["q3ns"], [])
     cp(T.yb[:], T.pa[:, 0:C], ["pa"], ["yb"])

@@ -5,6 +5,7 @@ C, K, M, R = 352, 160, 44, 3
 STEP = [3, 1, 5]
 NC = 384
 NR = 360
+NS = 16
 BIG = float(2 ** 80)
 FAR = float(2 ** 90)
 Q4, U8, F32, BF, I32, U16 = "float8_e4m3fn_x4", "uint8", "float32", "bfloat16", "int32", "uint16"
@@ -28,10 +29,10 @@ for _n, _w in (("qu", 128), ("su0", 128), ("su1", 128), ("qv", 128), ("qw", 512)
 for _n, _s, _d in (
         ("xt", 4 * C + 16, BF), ("ut", 512, BF), ("vt", 512, BF), ("et", 2048, BF), ("xs", 4 * NC, BF),
         ("wd", 4 * 544, BF), ("dsb", 4 * NC, BF), ("zall", 4 * NC, BF), ("zt", 4 * K, BF), ("f64", 4 * K, F32),
-        ("pi", 8, I32), ("kc", 16, F32), ("io1", 128, F32), ("m16", 448, F32), ("sm", 32, F32),
+        ("pi", 8, I32), ("kc", 16, F32), ("io1", 32, F32), ("sm", 32, F32),
         ("bt", NC, F32), ("c0", C, F32), ("c1", C, F32), ("plc", NC, F32), ("val", NC, F32),
-        ("diag", 448, F32), ("dq", K, F32), ("keep16", 448, BF), ("reset", C, BF), ("keepc", 3 * NR, BF),
-        ("ones", 64, F32), ("mk", 160, F32), ("kt", 24 * 12, F32), ("ki", 24 * 3, I32),
+        ("diag", 448, F32), ("keep16", 448, BF), ("reset", C, BF),
+        ("ones", 512, BF), ("mk", 160, F32), ("kt", 24 * 12, F32), ("ki", 24 * 3, I32),
         ("kw", 28 * 5, F32), ("lc", 320, U16),
         ("tp", NC, F32), ("ps", 72, F32), ("lp", 72, F32), ("xb", NC, F32), ("far", NC, F32),
         ("prow", 392, F32), ("mm", 448, F32), ("ms", 448, F32), ("sg", 2 * NC, BF),
@@ -39,16 +40,16 @@ for _n, _s, _d in (
         ("ab", 28 * M, F32), ("aw", 28 * M, F32), ("dm", 3 * C, F32), ("rr", 32 * M, F32), ("lq", 3 * C + 16, BF),
         ("st", 3 * C, F32), ("zi", 48, I32), ("lz", 24, U16), ("t1", 32, F32),
         ("xg", 480, F32), ("srt", 40, F32), ("cand", 16, F32), ("cnt", 16, F32),
-        ("junk", 12 * NR, BF), ("cmp", 4 * NR, BF), ("cms", 4 * NR, BF), ("pen", 24, F32), ("lh", 40, F32),
+        ("junk", 12 * NR, BF), ("cmp", 5 * NR, BF), ("cms", 5 * NR, BF), ("pen", 24, F32), ("lh", 40, F32),
         ("r3", 16, F32), ("xe", 96, F32), ("xf", 96, F32), ("le", 48, F32), ("cs", 48, F32),
-        ("pw", 24 * 10, F32), ("lo", 24, U16), ("win", 544, F32), ("es", K, F32), ("ei", 32, I32),
-        ("lk", 10, U16), ("oeb", K, F32), ("yb", C, F32)):
+        ("pw", 24 * 10, F32), ("lo", 24, U16), ("win", 560, F32), ("es", K + 192, F32),
+        ("lk", 16, U16), ("oeb", K, F32), ("yb", C, F32)):
     _sb(_n, _s, _d)
 SCRATCH["rw"] = ("sbuf", [128, 15, 32], F32)
-for _n in ("pa", "pb", "pc", "pd0", "pd1", "pd2", "pd3"):
+for _n in ("pa", "pb", "pc", "pe", "pd0", "pd1", "pd2", "pd3"):
     SCRATCH[_n] = ("psum", [128, 512], F32)
 
-SEMAPHORES = ["v", "s", "t", "g", "lx", "lu", "lv", "lw", "out", "p0", "p1", "p2", "a0", "a1", "a2", "loc"]
+SEMAPHORES = ["v", "s", "t", "g", "lx", "lz", "lu", "lv", "lw", "out", "p0", "p1", "p2", "a0", "a1", "a2", "loc"]
 
 A = AluOpType
 AF = ActivationFunctionType
@@ -144,23 +145,19 @@ def rank_program(g, core, T, topo):
         op("s", lambda: S.activation(o, i, f, **kw), r, w)
 
     def fill(o, n, c, w):
-        act(o, T.m16[:, 0:n], AF.Identity, ["m16"], w, bias=c, scale=0.0)
+        act(o, T.ones[:, 0:n], AF.Copy, ["ones"], w, scale=c)
 
-    def quant(name, n, tile, r):
-        op("v", lambda: V.quantize_mx(T[name][:, 0:n], T[name + "s"][:, 0:n], tile), r, [name, name + "s"])
+    def quant(name, a, e, tile, r, key=None):
+        op("v", lambda: V.quantize_mx(T[name][:, a:e], T[name + "s"][:, a:e], tile[:, 4 * a:4 * e]), r, [key or name])
 
-    def mm(ps, lhs, l0, rhs, n, r):
-        op("t", lambda: PE.matmul_mx(T[ps][:, 0:n], T[lhs][:, l0:l0 + 128], T[lhs + "s"][:, l0:l0 + 128],
-                                     T[rhs][:, 0:n], T[rhs + "s"][:, 0:n], True, True),
-           r + [rhs, rhs + "s"], [ps])
+    def mm(ps, lhs, l0, rhs, a, e, r):
+        op("t", lambda: PE.matmul_mx(T[ps][:, 0:e - a], T[lhs][:, l0:l0 + 128], T[lhs + "s"][:, l0:l0 + 128],
+                                     T[rhs][:, a:e], T[rhs + "s"][:, a:e], True, True), r, [ps])
 
-    def pick(dst, n, src, w, off, okey, on_s=True):
-        op("v", lambda: V.tensor_copy(T[dst][:, 0:n].bitcast(dt.uint32), T[src][:, 0:w].bitcast(dt.uint32).indirect(off)),
-           [src, okey], [dst])
-        if on_s:
-            act(T[dst + "s"][:, 0:n], T[src + "s"][:, 0:w].indirect(off), AF.Copy, [src + "s", okey], [dst + "s"])
-        else:
-            cp(T[dst + "s"][:, 0:n], T[src + "s"][:, 0:w].indirect(off), [src + "s", okey], [dst + "s"])
+    def pick(dst, a, e, src, w, off, okey, key):
+        op("v", lambda: V.tensor_copy(T[dst][:, a:e].bitcast(dt.uint32), T[src][:, 0:w].bitcast(dt.uint32).indirect(off)),
+           [src, okey], [key])
+        act(T[dst + "s"][:, a:e], T[src + "s"][:, 0:w].indirect(off), AF.Copy, [src, okey], [key + "s"])
 
     def iota(o, pat, base, cm, w, f=True):
         if f:
@@ -184,14 +181,10 @@ def rank_program(g, core, T, topo):
         for k in w:
             wrote[k] = (sem, total[sem])
 
-    def send_state(t):
-        q, l = "q%d" % t, "land%d" % t
-        send(t, T[l][:].bitcast(dt.uint8), T[q][:].bitcast(dt.uint8), "a%d" % t, [q], [])
-        send(t, T[l + "s"][:], T[q + "s"][:], "a%d" % t, [q + "s"], [l, l + "s"])
 
     io, kc, lc, kt, kw, mk = T.io1, T.kc, T.lc, T.kt, T.kw, T.mk
     col = lambda b, i: b[:, i:i + 1]
-    L_U0, L_U1, L_B, L_ROW, L_OWN, L_X, L_SUC, L_NAT = 0, 8, 16, 40, 70, 126, 222, 244
+    L_U0, L_U1, L_B, L_ROW, L_OWN, L_X, L_K, L_NAT = 0, 8, 16, 40, 70, 126, 222, 244
     lst = lambda a, n: lc[:, a:a + n]
     k22 = lambda i: kt[:, 24 * i:24 * i + 22]
     w28 = lambda i, a=0, e=28: kw[:, 28 * i + a:28 * i + e]
@@ -242,9 +235,7 @@ def rank_program(g, core, T, topo):
 
     def masks():
         ts(T.pi[:, 2:3], T.pi[:, 0:1], 16, None, A.bitwise_and, None, ["pi0"], ["pi2"])
-        ms(T.ones[:], 1.0, ["ones"])
         cp(col(kc, 9), T.pi[:, 2:3], ["pi2"], ["h"])
-        ts(T.dq[:], T.diag[:, 0:K], BIG, None, A.mult, None, ["diag"], ["dq"])
         ts(col(kc, 10), col(kc, 9), 16.0, None, A.add, None, ["h"], ["h16"])
         tt(col(kc, 11), col(kc, 9), col(kc, 0), A.add, ["h", "q"], ["r32"])
         ts(mk[:, 0:32], io[:, 0:32], col(kc, 9), None, A.is_ge, None, ["io", "h"], ["mk0"])
@@ -256,26 +247,43 @@ def rank_program(g, core, T, topo):
         ts(mk[:, 96:128], mk[:, 0:32], -BIG, BIG, A.mult, A.add, ["same"], ["other"])
         tt(mk[:, 128:160], mk[:, 128:160], mk[:, 0:32], A.mult, ["mk4", "same"], ["ntri"])
 
+    def turn_list():
+        ts(T.pi[:, 3:4], T.pi[:, 0:1], 1, None, A.bitwise_and, None, ["pi0"], ["pi3"])
+        ts(T.pi[:, 4:5], T.pi[:, 0:1], 4, 1, A.arith_shift_right, A.bitwise_and, ["pi0"], ["pi4"])
+        ts(col(kc, 12), col(kc, 0), 9.0, 16.0, A.min, A.mult, ["q"], ["k12"])
+        tt(col(kc, 13), T.pi[:, 3:4], T.pi[:, 4:5], A.not_equal, ["pi3", "pi4"], ["k13"])
+        ts(lst(L_K, 1), col(kc, 13), K + 16.0, col(kc, 12), A.mult, A.add, ["k12", "k13"], ["L_K"])
+
     def successors():
         runs = [(T.c1[:, M * s:M * s + M - 1], T.bt[:, 48 * s + 49:48 * s + 48 + M], 65) for s in range(7)]
         runs += [(T.c1[:, M - 1:7 * M:M], T.bt[:, 48::48], 65 - M), (T.c1[:, 7 * M:C - 2], T.bt[:, 2:M], 66),
                  (T.c1[:, C - 2:C], T.bt[:, 0:2], 66 - M)]
         for i, (o, a, c) in enumerate(runs):
-            act(o, a, AF.Identity, ["bt"], ["c1" if i == len(runs) - 1 else "c1_%d" % i], bias=512.0 * c)
+            act(o, a, AF.Identity, ["bt"], ["c1" if i == len(runs) - 1 else "c1_%d" % i], bias=c / 128.0, scale=1 / 65536.0)
 
     def plane_lists():
         ts(w28(3, 0, 24), w28(0, 4, 28), float(C), None, A.min, None, ["n", "L_OWN0"], ["n0", "o0"])
         for b in range(4):
             ts(lst(L_X + 24 * b, 24), w28(3, 0, 24), 4.0, float(b), A.mult, A.add, ["n0", "o0"], ["L_X%d" % b])
 
-    def resets():
-        ms(T.reset[:, 0::M], BIG, ["reset"])
-        ms(T.rr[:, 24 * M + M - 1::M], BIG, ["rrz"])
-        cp(lst(L_ROW, 30), T.sm[:, 0:30], ["sm"], ["L_ROW"])
-        ts(T.c0[:, M - 1::M], T.c0[:, M - 1::M], -float(C), None, A.add, None, ["c0"], ["c0"])
-        ms(T.lq[:, 0::M], 0.0, ["lqz"])
-        ts(col(T.c0, C - 2), col(T.c0, C - 2), -float(C), None, A.add, None, ["c0"], ["c0"])
-        ms(T.keepc[:, 0::NR], 0.0, ["keepc%d" % b for b in range(3)])
+    def fills():
+        fill(T.keep16[:], 448, 1.0, ["keep16"])
+        fill(T.reset[:], C, 0.0, ["reset"])
+        fill(T.keep16[:, 0::16], 28, 0.0, ["keep16"])
+        fill(T.reset[:, 0::M], 8, BIG, ["reset"])
+        fill(T.win[:, 0:192], 192, 0.0, ["win"])
+        fill(T.rr[:, 24 * M + M - 1::M], 8, BIG, ["rrz"])
+        fill(T.lq[:, 0::M], 25, -1.0, ["lqz"])
+
+    def diagonal():
+        for a in (16, 32, 64, 128, 256):
+            e = min(2 * a, 448)
+            act(T.diag[:, a:e], T.diag[:, 0:e - a], AF.Copy, ["diag"], ["diag"])
+
+    def first_successors():
+        act(T.c0[:], T.c0[:], AF.Copy, ["c0"], ["c0"], scale=1 / 65536.0)
+        for a in (T.c0[:, M - 1::M], col(T.c0, C - 2)):
+            act(a, a, AF.Identity, ["c0"], ["c0"], bias=-C / 65536.0)
 
     def delay_list():
         cp(col(T.ti, 0), col(T.tc, 0), ["tc0"], ["ti0"])
@@ -287,62 +295,69 @@ def rank_program(g, core, T, topo):
         tt(T.bl[:, 44:66], T.bl[:, 22:44], k22(7), A.add, ["bl1", "base"], ["bl2"])
         ts(T.lb[:], T.bl[:, 44:66], col(T.tc, 2), None, A.add, None, ["bl2", "tc2"], ["lb"])
 
-    def unit_tiles():
-        for b in range(4):
-            ts(T.et[:, 512 * b + b:512 * b + 512:4], io[:], col(kc, 6), None, A.is_equal, None, ["io", "p", "etz"], ["et%d" % b])
-        quant("qe", 512, T.et[:], ["et%d" % b for b in range(4)])
+    def unit_tile(b):
+        op("g", lambda: g.affine_select(T.et[:, 512 * b:512 * b + 512], T.ones[:], [[-4, 128], [-1, 4]], A.is_equal, 0.0, b, 4),
+           ["ones"], ["et%d" % b])
 
     dma("y", T.ut[:], T.u[:], "lu", [], ["ut"])
-    dma("s", T.xt[:, 0:4 * C], T.x[:], "lx", [], ["xt"])
+    dma("s", T.xt[:, 0:4 * C - 512], T.x[:, 0:4 * C - 512], "lx", [], ["xta"])
+    dma("s", T.xt[:, 4 * C - 512:4 * C], T.x[:, 4 * C - 512:], "lz", [], ["xtb"])
     iota(T.pi[:, 0:1], [[0, 1]], 0, 1, ["pi0"], f=False)
-    iota(io[:], [[1, 128]], 0, 0, ["io"])
-    iota(T.m16[:], [[0, 28], [1, 16]], 0, 0, ["m16"])
+    iota(io[:], [[1, 32]], 0, 0, ["io"])
+    ms(T.ones[:], 1.0, ["ones"])
+    unit_tile(0)
+    unit_tile(1)
     iota(T.sm[:, 0:30], [[1, 15], [16, 2]], 0, 0, ["sm"])
-    iota(T.c0[:], [[1, 8], [8 - 512, M]], 64 * 512 + 9, 0, ["c0"])
-    iota(T.val[:], [[512 + 16, 24], [24 * 512 + 1, 16]], 0, 0, ["val"])
-    ms(T.et[:], 0.0, ["etz"])
     ts(T.pi[:, 1:2], T.pi[:, 0:1], 15, None, A.bitwise_and, None, ["pi0"], ["pi1"])
-    cp(col(kc, 6), T.pi[:, 0:1], ["pi0"], ["p"])
-    ts(lst(L_U0, 8), io[:, 0:8], 16.0, None, A.mult, None, ["io"], ["L_U0"])
-    ts(lst(L_U1, 8), io[:, 0:8], 16.0, 1.0, A.mult, A.add, ["io"], ["L_U1"])
-    cp(col(kc, 0), T.pi[:, 1:2], ["pi1"], ["q"])
-    cp(lst(L_B, 24), io[:, 0:24], ["io"], ["L_B"])
     ms(T.xt[:, 4 * C:], 0.0, ["xz"])
     ms(T.prow[:, C:], FAR, ["prz", "prow"])
-    own_lists()
-    fill(T.keep16[:], 448, 1.0, ["keep16"])
-    fill(T.reset[:], C, 0.0, ["reset"])
-    quant("qu", 128, T.ut[:], ["ut"])
-    pick("su0", 128, "qu", 128, lst(L_U0, 8), "L_U0")
-    ts(T.diag[:], T.m16[:], col(kc, 0), None, A.is_equal, None, ["m16", "q"], ["diag"])
-    quant("q0", C, T.xt[:, 0:4 * C], ["xt"])
-    pick("su1", 128, "qu", 128, lst(L_U1, 8), "L_U1")
-    for b in range(3):
-        fill(T.keepc[:, NR * b:NR * b + NR], NR, 1.0, ["keepc%d" % b])
+    cp(col(kc, 0), T.pi[:, 1:2], ["pi1"], ["q"])
+    ts(lst(L_U0, 8), io[:, 0:8], 16.0, None, A.mult, None, ["io"], ["L_U0"])
+    ts(T.diag[:, 0:16], io[:, 0:16], col(kc, 0), None, A.is_equal, None, ["io", "q"], ["diag"])
+    ts(lst(L_U1, 8), io[:, 0:8], 16.0, 1.0, A.mult, A.add, ["io"], ["L_U1"])
+    cp(lst(L_B, 24), io[:, 0:24], ["io"], ["L_B"])
+    issue(listed(own_lists, masks, turn_list))
+    issue(listed(fills, diagonal))
+    quant("qu", 0, 128, T.ut, ["ut"])
+    pick("su0", 0, 128, "qu", 128, lst(L_U0, 8), "L_U0", "su0")
+    quant("q0", 0, C - 128, T.xt, ["xta"], "qa")
+    quant("q0", C - 128, C, T.xt, ["xtb"], "qb")
+    pick("su1", 0, 128, "qu", 128, lst(L_U1, 8), "L_U1", "su1")
 
     wd, rr, rw = T.wd, T.rr, T.rw
     xpl = lambda b: wd[:, 544 * b + K:544 * b + 544]
     Wv = lambda a, e: rr[:, M * a + M - 1:M * e:M]
     row = rw[:, :, 0:24]
+
+    def first_planes(a, e):
+        for b in range(a, e):
+            act(xpl(b), T.xt[:].indirect(lst(L_X + 24 * b, 24)), AF.Copy, ["xta", "xtb", "xz", "L_X%d" % b], ["xp%d" % b], scale=64.0)
     half = 2 * K - NR - 0.5
     for t in range(R):
         q, land = "q%d" % t, "land%d" % t
         n = C if t == 0 else NC
         nb = n // 16
-        mm("pa", "su0", 0, q, n, ["su0", "su0s"])
-        mm("pc", "su0", 0, q, n, ["su0", "su0s"])
-        mm("pb", "su1", 0, q, n, ["su1", "su1s"])
-        tr(T.tp[:, 0:n], T.pa[:, 0:n], ["pa"], ["tp"])
-        cp(T.ps[:, 24 * t:24 * t + nb], T.tp[:, 0:n:16], ["tp"], ["ps%d" % t])
+        h = n - 128
+        mm("pa", "su0", 0, q, 0, h, ["su0", "su0s", "qa"])
+        mm("pe", "su0", 0, q, h, n, ["su0", "su0s", "qb"])
+        mm("pc", "su0", 0, q, 0, n, ["su0", "su0s", "qa", "qb"])
+        mm("pb", "su1", 0, q, 0, n, ["su1", "su1s", "qa", "qb"])
+        tr(T.tp[:, 0:h], T.pa[:, 0:h], ["pa"], ["tpa"])
+        tr(T.tp[:, h:n], T.pe[:, 0:128], ["pe"], ["tpb"])
+        cp(T.ps[:, 24 * t:24 * t + nb], T.tp[:, 0:n:16], ["tpa", "tpb"], ["ps%d" % t])
+        send(t, T[land + "s"][:], T[q + "s"][:], "a%d" % t, ["qa", "qb"], [])
         send(t, T.lp[:, 24 * t:24 * t + nb], T.ps[:, 24 * t:24 * t + nb], "p%d" % t, ["ps%d" % t], ["lp%d" % t])
-        send_state(t)
+        send(t, T[land][:].bitcast(dt.uint8), T[q][:].bitcast(dt.uint8), "a%d" % t, ["qa", "qb"], [land])
         act(T.prow[:, 0:n], T.pc[:, 0:n], AF.Copy, ["pc"], ["prow"])
         act(T.sg[:, 0:n], T.pb[:, 0:n], AF.Sign, ["pb"], ["sg0"])
         act(T.sg[:, NC:NC + n], T.sg[:, 0:n], AF.Relu, ["sg0"], ["sg1", "tc0"], accum_out=col(T.tc, 0))
         if t == 0:
+            unit_tile(2)
+            unit_tile(3)
+            iota(T.c0[:], [[1, 8], [8 - 512, M]], 64 * 512 + 9, 0, ["c0"])
+            iota(T.val[:], [[1, NC]], 0, 0, ["val"])
             iota(T.bt[:], [[16, 8], [1 - 3 * 512, 16], [128 - 512, 3]], 0, 0, ["bt"])
             iota(T.plc[:], [[1, 24], [24, 16]], 0, 0, ["plc"])
-            ms(T.keep16[:, 0::16], 0.0, ["keep16"])
             plane_lists()
         if t == 1:
             successors()
@@ -350,13 +365,15 @@ def rank_program(g, core, T, topo):
         tt(T.mm[:], T.prow[:].indirect(lst(L_OWN + 28 * min(t, 1), 28)), T.diag[:], A.mult, ["prow", "prz", own, "diag"], ["mm"])
         scan(T.ms[:], T.keep16[:], T.mm[:], A.mult, A.add, ["keep16", "mm"], ["ms"])
         if t == 0:
-            for b in (0, 1):
-                act(xpl(b), T.xt[:].indirect(lst(L_X + 24 * b, 24)), AF.Copy, ["xt", "xz", "L_X%d" % b], ["xp%d" % b], scale=64.0)
-            issue(listed(tables, resets))
-            spare = listed(unit_tiles) + listed(masks, own_lists_state)
-            issue(spare, 4)
+            first_planes(0, 3)
+            issue(listed(tables, own_lists_state))
+            cp(lst(L_ROW, 30), T.sm[:, 0:30], ["sm"], ["L_ROW"])
+        delay = listed(delay_list)
+        if t == 0:
+            issue(delay, 4)
         else:
             for b in range(4):
+                issue(delay, 1)
                 ts(xpl(b), T.xs[:, b::4], 64.0, None, A.mult, None, ["xs%d" % b, "xs4"], ["xp%d" % b])
         lw = T.lp[:, 24 * t:24 * t + nb]
         cuts = ((0, 8), (8, 16), (16, nb))
@@ -368,25 +385,28 @@ def rank_program(g, core, T, topo):
                 act(T.xb[:, 16 * a:16 * e], src, AF.Copy, key, ["xb%d" % i])
         for i, (a, e) in enumerate(cuts):
             tr(T.far[:, 16 * a:16 * e] if t == 0 else T.far[:, i::3], T.xb[:, 16 * a:16 * e], ["xb%d" % i], ["far%d" % i])
-        rows = [("ab", c) for c in range(11)] + [("aw", 10), ("aw", 11)] + [("ab", c) for c in range(11, 19)] + [("aw", 19)]
-        rows += [("ab", c) for c in range(19, 27)] + [("aw", c) for c in range(20, 28)]
+        rows = [("ab", c) for c in list(range(4, 12)) + list(range(4)) + list(range(12, 27))] + [("aw", c) for c in range(24, 28)]
         for buf, c in rows:
             s = (c - 4) % 8
             act(T[buf][:, M * c:M * c + M], T.far[:, s:C:8] if t == 0 else T.far[:, 48 * s:48 * s + M], AF.Abs,
                 ["far0", "far1", "far2", "ms"], ["%s%d" % (buf, c)], bias=col(T.ms, 16 * c + 15), scale=-1.0)
         if t == 0:
-            issue(listed(delay_list, lambda: issue(spare, 3)))
+            issue(delay, 1)
+            quant("qe", 0, 512, T.et, ["et%d" % b for b in range(4)])
+            issue(delay)
+            first_successors()
             wait("y", wrote[land])
             dma("y", T.qw[:].bitcast(dt.uint8), T.wc[:], "lw", [], ["qw"])
             dma("y", T.qws[:], T.ws[:], "lw", [], ["qw"])
             dma("y", T.vt[:], T.v[:], "lv", [], ["vt"])
         elif t == 1:
-            issue(listed(delay_list, natural))
+            issue(listed(lambda: issue(delay), natural))
         else:
-            delay_list()
-            quant("qv", 128, T.vt[:], ["vt"])
+            issue(delay)
+            quant("qv", 0, 128, T.vt, ["vt"])
         for b in range(4):
-            mm("pd%d" % b, "qe", 128 * b, land, n, ["qe", "qes"])
+            mm("pd%d" % b, "qe", 128 * b, land, 0, n, ["qe", land])
+
         def again(a, e):
             cp(T.aw[:, M * a:M * e], T.ab[:, M * a:M * e], ["ab%d" % c for c in range(a, e)], ["aw%d" % c for c in range(a, e)])
 
@@ -398,29 +418,39 @@ def rank_program(g, core, T, topo):
         def least(k):
             scan(rr[:, C * k:C * k + C], T.reset[:], T.dm[:, C * k:C * k + C], A.max, A.min,
                  ["reset", "dm%d" % k], ["rr%d" % k])
-        again(4, 10)
+        again(4, 9)
+        again(9, 12)
         larger(0)
-        again(12, 15)
+        again(12, 16)
         least(0)
-        again(15, 19)
+        again(16, 20)
         larger(1)
+        again(20, 24)
         least(1)
-        larger(2)
-        least(2)
-        unpack = lambda b: act(T.dsb[:, NC * b:NC * b + n], T["pd%d" % b][:, 0:n], AF.Copy, ["pd%d" % b], ["dsb%d" % b])
-        unpack(0)
-        unpack(1)
         rk = ["rr0", "rr1", "rr2"]
         s8 = lambda i: T.srt[:, 8 * i:8 * i + 8]
+        larger(2)
+        tt(s8(0), Wv(0, 8), Wv(8, 16), A.min, rk[0:2], ["s0"])
+        tt(s8(1), Wv(0, 8), Wv(8, 16), A.max, rk[0:2], ["s1"])
+        least(2)
+
+        def before(c):
+            o, a, m = T.lq[:, M * c + 1:M * c + M], rr[:, M * c:M * c + M - 1], col(rr, M * c + M - 1)
+            if c < NS:
+                act(o, a, AF.Sign, ["rr%d" % (c // 8), "lqz"], ["lq%d" % c], bias=m, scale=-1.0)
+            else:
+                ts(o, a, m, -1.0, A.is_gt, A.mult, ["rr%d" % (c // 8), "lqz"], ["lq%d" % c])
+        for c in range(NS):
+            before(c)
         tr(T.t1[:], Wv(0, 32), rk + ["rrz"], ["t1"])
-        tt(s8(0), Wv(0, 8), Wv(8, 16), A.min, rk, ["s0"])
+        tt(s8(2), s8(1), Wv(16, 24), A.min, rk + ["s1"], ["s2"])
         act(T.xg[:, 0:288], T.t1[:].indirect(lst(L_ROW, 18)), AF.Copy, ["t1", "L_ROW"], ["xg0"])
         cp(T.xg[:, 288:480], T.t1[:].indirect(lst(L_ROW + 18, 12)), ["t1", "L_ROW"], ["xg1"])
-        tt(s8(1), Wv(0, 8), Wv(8, 16), A.max, rk, ["s1"])
-        tr(rw[:, 9:15, :], T.xg[:, 288:480], ["xg1"], ["rw1"])
-        tt(s8(2), s8(1), Wv(16, 24), A.min, rk + ["s1"], ["s2"])
-        tr(rw[:, 0:9, :], T.xg[:, 0:288], ["xg0"], ["rw0"])
         tt(T.cand[:, 0:8], s8(0), s8(2), A.max, ["s0", "s2"], ["mid"])
+        tr(rw[:, 9:15, :], T.xg[:, 288:480], ["xg1"], ["rw1"])
+        tt(s8(3), s8(0), Wv(16, 24), A.min, rk + ["s0"], ["low"])
+        tr(rw[:, 0:9, :], T.xg[:, 0:288], ["xg0"], ["rw0"])
+        tt(s8(4), s8(1), Wv(16, 24), A.max, rk + ["s1"], ["upp"])
         rwk = ["rw0", "rw1"]
 
         def count(i, j, key):
@@ -429,49 +459,58 @@ def rank_program(g, core, T, topo):
 
         def less(i, j, key):
             ts(T.cmp[:, NR * j:NR * j + NR], row, col(T.cand, i), None, A.is_lt, None, rwk + [key], ["cmp%d" % j])
-        for i in range(7):
+
+        def tally(j, key):
+            a = T.cmp[:, NR * j:NR * j + NR]
+            scan(T.cms[:, NR * j:NR * j + NR], a, a, A.add, A.max, ["cmp%d" % j], [key])
+        for i in (0, 1, 2, 3, 5, 6):
             count(i, i, "mid")
-        tt(s8(3), s8(0), Wv(16, 24), A.min, rk + ["s0"], ["low"])
-        tt(s8(4), s8(1), Wv(16, 24), A.max, rk + ["s1"], ["upp"])
-        less(7, 3, "mid")
-        for c in range(24):
-            ts(T.lq[:, M * c + 1:M * c + M], rr[:, M * c:M * c + M - 1], col(rr, M * c + M - 1), None, A.is_le, None,
-               rk + ["lqz"], ["lq%d" % c])
-            if c == 0:
-                scan(T.cms[:, 3 * NR:], T.keepc[:, 0:NR], T.cmp[:, 3 * NR:], A.mult, A.add, ["keepc0", "cmp3"], ["cms3"])
+        less(4, 3, "mid")
+        less(7, 4, "mid")
         cc = "c%d" % min(t, 1)
-        for k in range(3):
-            scan(T.st[:, C * k:C * k + C], T.lq[:, C * k:C * k + C], T[cc][:], A.mult, A.max,
+
+        def first(k):
+            scan(T.st[:, C * k:C * k + C], T.lq[:, C * k:C * k + C], T[cc][:], A.add, A.max,
                  ["lq%d" % c for c in range(8 * k, 8 * k + 8)] + [cc], ["st%d" % k])
+        for c in range(NS, 24):
+            before(c)
+            if c == NS:
+                tally(3, "cms4")
+                tally(4, "cms3")
         pen, lh, r3 = T.pen, T.lh, T.r3
-        ts(col(pen, 15), col(T.cms, 4 * NR - 1), K - 0.5, BIG, A.is_lt, A.mult, ["cms3"], ["pen1b"])
-        ts(pen[:, 8:15], T.cnt[:, 0:7], half, BIG, A.is_lt, A.mult, ["cnt%d" % i for i in range(7)], ["pen1a"])
-        cp(T.zi[:, 0:24], T.st[:, M - 1::M], ["st0", "st1", "st2"], ["zi0"])
-        tt(lh[:, 32:40], s8(4), pen[:, 8:16], A.min, ["upp", "pen1a", "pen1b"], ["lh2"])
-        ts(T.zi[:, 24:48], T.zi[:, 0:24], 511, None, A.bitwise_and, None, ["zi0"], ["zi1"])
-        tt(T.cand[:, 8:16], lh[:, 32:40], s8(3), A.max, ["lh2", "low"], ["nxt"])
-        cp(T.lz[:], T.zi[:, 24:48], ["zi1"], ["lz"])
+        ts(pen[:, 12:16:3], T.cms[:, 4 * NR - 1::NR], K - 0.5, BIG, A.is_lt, A.mult, ["cms3"], ["pen1b"])
+        first(0)
+        ts(pen[:, 8:12], T.cnt[:, 0:4], half, BIG, A.is_lt, A.mult, ["cnt%d" % i for i in range(4)], ["pen1a"])
+        first(1)
+        tt(lh[:, 32:37], T.srt[:, 32:37], pen[:, 8:13], A.min, ["upp", "pen1a", "pen1b"], ["lh2"])
+        tt(T.cand[:, 8:13], lh[:, 32:37], T.srt[:, 24:29], A.max, ["lh2", "low"], ["nxt"])
         for i in range(8, 13):
             count(i, i - 1, "nxt")
+        ts(pen[:, 13:15], T.cnt[:, 5:7], half, BIG, A.is_lt, A.mult, ["cnt5", "cnt6"], ["pen1c"])
+        first(2)
+        tt(lh[:, 37:40], T.srt[:, 37:40], pen[:, 13:16], A.min, ["upp", "pen1c", "pen1b"], ["lh3"])
+        cp(pen[:, 0:8], pen[:, 8:16], ["pen1a", "pen1b", "pen1c"], ["pen0"])
+        ts(T.zi[:, 0:24], T.st[:, M - 1::M], 65536.0, None, A.mult, None, ["st0", "st1", "st2"], ["zi0"])
+        tt(T.cand[:, 13:16], lh[:, 37:40], T.srt[:, 29:32], A.max, ["lh3", "low"], ["nxu"])
+        ts(T.zi[:, 24:48], T.zi[:, 0:24], 511, None, A.bitwise_and, None, ["zi0"], ["zi1"])
         for i in range(3):
-            less(13 + i, i, "nxt")
-        cp(pen[:, 0:8], pen[:, 8:16], ["pen1a", "pen1b"], ["pen0"])
-        scan(T.cms[:, 0:3 * NR], T.keepc[:, 0:3 * NR], T.cmp[:, 0:3 * NR], A.mult, A.add, ["keepc0", "cmp0", "cmp1", "cmp2"], ["cms"])
-        if t == 0:
-            issue(spare)
-        for b in (2, 3):
-            unpack(b)
+            less(13 + i, i, "nxu")
+        cp(T.lz[:], T.zi[:, 24:48], ["zi1"], ["lz"])
+        for j in range(3):
+            tally(j, "cms%d" % j if j < 2 else "cms")
+        for b in range(4):
+            act(T.dsb[:, NC * b:NC * b + n], T["pd%d" % b][:, 0:n], AF.Copy, ["pd%d" % b], ["dsb%d" % b])
+
+        ts(pen[:, 16:21], T.cnt[:, 8:13], half, BIG, A.is_lt, A.mult, ["cnt%d" % i for i in range(8, 13)], ["pen2"])
+        ts(pen[:, 21:24], T.cms[:, NR - 1:3 * NR:NR], K - 0.5, BIG, A.is_lt, A.mult, ["cms"], ["pen3"])
         for b in range(4):
             act(T.zall[:, NC * b:NC * b + NC], T.dsb[:, NC * b:NC * b + n].indirect(T.lz[:]), AF.Copy,
                 ["dsb%d" % b, "lz"], ["zall%d" % b])
         if t == 0:
-            for b in (2, 3):
-                act(xpl(b), T.xt[:].indirect(lst(L_X + 24 * b, 24)), AF.Copy, ["xt", "xz", "L_X%d" % b], ["xp%d" % b], scale=64.0)
-        ts(pen[:, 21:24], T.cms[:, NR - 1:3 * NR:NR], K - 0.5, BIG, A.is_lt, A.mult, ["cms"], ["pen3"])
-        ts(pen[:, 16:21], T.cnt[:, 8:13], half, BIG, A.is_lt, A.mult, ["cnt%d" % i for i in range(8, 13)], ["pen2"])
-        pk = ["pen1a", "pen1b", "pen2", "pen3"]
-        tt(lh[:, 0:16], T.cand[:], pen[:, 8:24], A.min, ["mid", "nxt"] + pk, ["lh0"])
-        tt(lh[:, 16:32], T.cand[:], pen[:, 8:24], A.max, ["mid", "nxt"] + pk, ["lh1"])
+            first_planes(3, 4)
+        pk = ["pen1a", "pen1b", "pen1c", "pen2", "pen3"]
+        tt(lh[:, 0:16], T.cand[:], pen[:, 8:24], A.min, ["mid", "nxt", "nxu"] + pk, ["lh0"])
+        tt(lh[:, 16:32], T.cand[:], pen[:, 8:24], A.max, ["mid", "nxt", "nxu"] + pk, ["lh1"])
         red(col(r3, 2), pen[:], A.add, pk + ["pen0"], ["r2"])
         red(col(r3, 0), lh[:, 0:16], A.max, ["lh0"], ["r0"])
         red(col(r3, 1), lh[:, 16:32], A.min, ["lh1"], ["r1"])
@@ -491,7 +530,7 @@ def rank_program(g, core, T, topo):
         ts(T.le[:, 0:24], W, tau, None, A.is_lt, None, rk + ["tau"], ["lt"])
         ts(T.le[:, 24:48], W, tau, None, A.is_equal, None, rk + ["tau"], ["eq"])
         ts(p24(0), W, tau, 1000.0, A.is_gt, A.mult, rk + ["tau"], ["p0"])
-        scan(cs[:], T.ones[:, 0:48], T.le[:], A.mult, A.add, ["ones", "lt", "eq"], ["cs"])
+        scan(cs[:], T.le[:], T.le[:], A.add, A.max, ["lt", "eq"], ["cs"])
         ts(p24(1), W, tau, None, A.is_ge, None, rk + ["tau"], ["p1"])
         ts(xe[:, 0:32], mk[:, 32:64], col(cs, 47), None, A.mult, None, ["tri", "cs"], ["xe0"])
         ts(xe[:, 32:64], mk[:, 128:160], col(cs, 23), K / 32.0, A.mult, A.add, ["ntri", "cs"], ["xe1"])
@@ -507,43 +546,48 @@ def rank_program(g, core, T, topo):
         tt(p24(8), p24(6), p24(4), A.add, ["p6", "p4"], ["p8"])
         tt(p24(9), p24(8), p24(7), A.max, ["p7", "p8"], ["p9"])
         cp(T.lo[:], p24(9), ["p9"], ["lo"])
-        cp(T.win[:].indirect(T.lo[:]), T.val[:], ["lo", "val"], ["win"])
-        scan(T.es[:], T.dq[:], T.win[:, 0:K], A.max, A.min, ["dq", "win"], ["es"])
-        cp(T.ei[:, 0:10], T.es[:, 15::16], ["es"], ["ei0"])
-        ts(T.ei[:, 16:26], T.ei[:, 0:10], 511, None, A.bitwise_and, None, ["ei0"], ["ei1"])
-        cp(T.lk[:], T.ei[:, 16:26], ["ei1"], ["lk"])
-        zsrc = lambda b: T.zall[:, NC * b:NC * b + NC].indirect(T.lk[:])
+        cp(T.win[:, 16:].indirect(T.lo[:]), T.val[:], ["lo", "val"], ["win"])
+        tr(T.es[:, 0:K], T.win[:, 16:16 + K], ["win"], ["es0"])
+        tr(T.es[:, K:], T.win[:, 0:192], ["win"], ["es1"])
+        cp(T.lk[:], T.es[:].indirect(lst(L_K, 1)), ["es0", "es1", "L_K"], ["lk"])
+        lk = T.lk[:, 0:10]
+        zsrc = lambda b: T.zall[:, NC * b:NC * b + NC].indirect(lk)
         for b in (0, 1):
             cp(T.zt[:, b::4], zsrc(b), ["zall%d" % b, "lk"], ["zt%d" % b])
         for b in (2, 3):
             act(T.zt[:, b::4], zsrc(b), AF.Copy, ["zall%d" % b, "lk"], ["zt%d" % b])
-        for b in (2, 3):
-            act(T.f64[:, K * b:K * b + K], xpl(b).indirect(T.lk[:]), AF.Copy, ["xp%d" % b, "lk"], ["f%d" % b])
-        quant("qz", K, T.zt[:], ["zt%d" % b for b in range(4)])
+        for b in (2, 3, 1):
+            act(T.f64[:, K * b:K * b + K], xpl(b).indirect(lk), AF.Copy, ["xp%d" % b, "lk"], ["f%d" % b])
+        quant("qz", 0, K, T.zt, ["zt%d" % b for b in range(4)])
         for b in (2, 3, 0, 1):
-            mm("pd%d" % b, "qw", 128 * b, "qz", K, ["qw"])
+            mm("pd%d" % b, "qw", 128 * b, "qz", 0, K, ["qw", "qz"])
+        cp(T.f64[:, 0:K], xpl(0).indirect(lk), ["xp0", "lk"], ["f0"])
         for b in (2, 3, 0, 1):
-            if b in (2, 1):
-                h = b % 2
-                cp(T.f64[:, K * h:K * h + K], xpl(h).indirect(T.lk[:]), ["xp%d" % h, "lk"], ["f%d" % h])
             tt(wd[:, 544 * b:544 * b + K], T["pd%d" % b][:, 0:K], T.f64[:, K * b:K * b + K], A.add,
                ["pd%d" % b, "f%d" % b], ["g%d" % b])
         usrc = lambda b, a, e: wd[:, 544 * b:544 * b + 544].indirect(T.lo[:, a:e])
-        for b, a, e, key in ((2, 0, 24, "xs2"), (3, 0, 24, "xs3"), (1, 10, 24, "xs4")):
+        for b, a, e, key in ((2, 0, 24, "xs2"), (3, 0, 24, "xs3"), (1, 16, 24, "xs4")):
             act(T.xs[:, 64 * a + b:64 * e:4], usrc(b, a, e), AF.Copy, ["g%d" % b, "xp%d" % b, "lo"], [key], scale=0.015625)
-        for b, a, e in ((0, 0, 24), (1, 0, 10)):
+        for b, a, e in ((0, 0, 24), (1, 0, 16)):
             ts(T.xs[:, 64 * a + b:64 * e:4], usrc(b, a, e), 0.015625, None, A.mult, None, ["g%d" % b, "xp%d" % b, "lo"], ["xs%d" % b])
-        quant("q%d" % (t + 1), NC, T.xs[:], ["xs%d" % b for b in range(5)])
+        if t + 1 < R:
+            quant("q%d" % (t + 1), 0, NC - 128, T.xs, ["xs%d" % b for b in range(4)], "qa")
+            quant("q%d" % (t + 1), NC - 128, NC, T.xs, ["xs%d" % b for b in range(5)], "qb")
+        else:
+            quant("q3", 0, NC, T.xs, ["xs%d" % b for b in range(5)])
 
-    pick("q3n", C, "q3", NC, lst(L_NAT, 22), "L_NAT")
-    dma("y", T.oc[:], T.q3n[:].bitcast(dt.uint8), "out", ["q3n"], [])
-    mm("pa", "qv", 0, "q3n", C, ["qv", "qvs"])
-    act(T.oeb[:], T.plc[:].indirect(T.lk[:]), AF.Copy, ["plc", "lk"], ["oeb"])
+    runs = ((0, K, "pa"), (K, C, "pe"))
+    for a, e, ps in runs:
+        pick("q3n", a, e, "q3", NC, lst(L_NAT + a // 16, (e - a) // 16), "L_NAT", "n" + ps)
+        dma("y", T.oc[:, 4 * a:4 * e], T.q3n[:, a:e].bitcast(dt.uint8), "out", ["n" + ps], [])
+        mm(ps, "qv", 0, "q3n", a, e, ["qv", "n" + ps, "n" + ps + "s"])
+    act(T.oeb[:], T.plc[:].indirect(T.lk[:, 0:10]), AF.Copy, ["plc", "lk"], ["oeb"])
+    for a, e, ps in runs:
+        cp(T.yb[:, a:e], T[ps][:, 0:e - a], [ps], ["y" + ps])
+        dma("y", T.y[:, a:e], T.yb[:, a:e], "out", ["y" + ps], [])
     dma("s", T.oe[:], T.oeb[0:128:16, :], "out", ["oeb"], [])
     for k in range(4):
-        dma("s", T.osc[4 * k:4 * k + 4, :], T.q3ns[32 * k:32 * k + 4, :], "out", ["q3ns"], [])
-    cp(T.yb[:], T.pa[:, 0:C], ["pa"], ["yb"])
-    dma("y", T.y[:], T.yb[:], "out", ["yb"], [])
+        dma("s", T.osc[4 * k:4 * k + 4, :], T.q3ns[32 * k:32 * k + 4, :], "out", ["npas", "npes"], [])
     for s in SEMAPHORES:
         if total.get(s):
             wait("g", (s, total[s]))

@@ -5,7 +5,9 @@ C, K, M, R = 352, 160, 44, 3
 STEP = [3, 1, 5]
 NC = 384
 NR = 360
-NS = 16
+NS = (12, 11, 11)
+FIRST = ((0, 192, "pa"), (192, C, "pe"))
+LATER = ((0, 128, "pa"), (128, 256, "pd0"), (256, NC, "pe"))
 BIG = float(2 ** 80)
 FAR = float(2 ** 90)
 Q4, U8, F32, BF, I32, U16 = "float8_e4m3fn_x4", "uint8", "float32", "bfloat16", "int32", "uint16"
@@ -30,17 +32,17 @@ for _n, _s, _d in (
         ("xt", 4 * C + 16, BF), ("ut", 512, BF), ("vt", 512, BF), ("et", 2048, BF), ("xs", 4 * NC, BF),
         ("wd", 4 * 544, BF), ("dsb", 4 * NC, BF), ("zall", 4 * NC, BF), ("zt", 4 * K, BF), ("f64", 4 * K, F32),
         ("pi", 8, I32), ("kc", 16, F32), ("io1", 32, F32), ("sm", 32, F32),
-        ("bt", NC, F32), ("c0", C, F32), ("c1", C, F32), ("plc", NC, F32), ("val", NC, F32),
+        ("sr", 72, F32), ("keepc", 3 * NR, BF), ("plc", NC, F32), ("val", NC, F32),
         ("diag", 448, F32), ("keep16", 448, BF), ("reset", C, BF),
         ("ones", 512, BF), ("mk", 160, F32), ("kt", 24 * 12, F32), ("ki", 24 * 3, I32),
         ("kw", 28 * 5, F32), ("lc", 320, U16),
         ("tp", NC, F32), ("ps", 72, F32), ("lp", 72, F32), ("xb", NC, F32), ("far", NC, F32),
         ("prow", 392, F32), ("mm", 448, F32), ("ms", 448, F32), ("sg", 2 * NC, BF),
         ("tc", 8, F32), ("ti", 8, I32), ("bl", 66, F32), ("lb", 22, U16),
-        ("ab", 28 * M, F32), ("aw", 28 * M, F32), ("dm", 3 * C, F32), ("rr", 32 * M, F32), ("lq", 3 * C + 16, BF),
-        ("st", 3 * C, F32), ("zi", 48, I32), ("lz", 24, U16), ("t1", 32, F32),
+        ("ab", 28 * M, F32), ("aw", 28 * M, F32), ("dm", 3 * C, F32), ("rr", 32 * M, F32), ("lq", 3 * C, BF),
+        ("jm", 24, F32), ("zf", 96 + 4 * M, F32), ("lz", 24, U16), ("t1", 32, F32),
         ("xg", 480, F32), ("srt", 40, F32), ("cand", 16, F32), ("cnt", 16, F32),
-        ("junk", 12 * NR, BF), ("cmp", 5 * NR, BF), ("cms", 5 * NR, BF), ("pen", 24, F32), ("lh", 40, F32),
+        ("junk", 13 * NR, BF), ("cmp", 6 * NR, BF), ("cms", 6 * NR, BF), ("pen", 24, F32), ("lh", 40, F32),
         ("r3", 16, F32), ("xe", 96, F32), ("xf", 96, F32), ("le", 48, F32), ("cs", 48, F32),
         ("pw", 24 * 10, F32), ("lo", 24, U16), ("win", 560, F32), ("es", K + 192, F32),
         ("lk", 16, U16), ("oeb", K, F32), ("yb", C, F32)):
@@ -49,7 +51,7 @@ SCRATCH["rw"] = ("sbuf", [128, 15, 32], F32)
 for _n in ("pa", "pb", "pc", "pe", "pd0", "pd1", "pd2", "pd3"):
     SCRATCH[_n] = ("psum", [128, 512], F32)
 
-SEMAPHORES = ["v", "s", "t", "g", "lx", "lz", "lu", "lv", "lw", "out", "p0", "p1", "p2", "a0", "a1", "a2", "loc"]
+SEMAPHORES = ["v", "s", "t", "g", "lx", "lz", "lu", "lv", "lw", "p0", "p1", "p2", "a0", "a1", "a2", "loc", "out"]
 
 A = AluOpType
 AF = ActivationFunctionType
@@ -200,13 +202,14 @@ def rank_program(g, core, T, topo):
         tt(w28(3), w28(2), w28(1), A.max, ["o0a", "o0b", "pad"], ["o0"])
         ts(lst(L_OWN, 28), w28(3), float(NC), None, A.min, None, ["o0"], ["L_OWN0"])
 
+    def own_columns():
+        ts(w28(2, 4, 28), io[:, 0:24], 16.0, col(kc, 0), A.mult, A.add, ["io", "q"], ["o0b"])
+        ts(w28(4, 0, 24), w28(2, 4, 28), float(K), None, A.add, None, ["o0b"], ["J"])
+
     def own_lists_state():
         ts(col(kc, 4), col(kc, 3), -113.0, col(kc, 0), A.mult, A.add, ["qz0", "q"], ["k4"])
-        ts(col(kc, 5), col(kc, 0), -64.0, None, A.add, None, ["q"], ["k5"])
-        ts(col(kc, 4), col(kc, 4), 319.0, None, A.add, None, ["k4"], ["k4"])
-        ts(w28(2, 4, 28), io[:, 4:28], 16.0, col(kc, 5), A.mult, A.add, ["io", "k5"], ["o0b"])
-        ts(w28(2, 0, 4), io[:, 0:4], 16.0, col(kc, 4), A.mult, A.add, ["io", "k4"], ["o0a"])
-        ts(w28(4, 0, 24), w28(2, 4, 28), float(K), None, A.add, None, ["o0b"], ["J"])
+        ts(w28(2, 0, 4), io[:, 20:24], 16.0, -1.0, A.mult, A.add, ["io"], ["o0a"])
+        ts(w28(2, 0, 4), w28(2, 0, 4), col(kc, 4), None, A.add, None, ["o0a", "k4"], ["o0a"])
         tt(w28(3), w28(2), w28(1), A.max, ["o0a", "o0b", "pad"], ["o0"])
         ts(lst(L_OWN + 28, 28), w28(3), float(NC), None, A.min, None, ["o0"], ["L_OWN1"])
 
@@ -254,13 +257,6 @@ def rank_program(g, core, T, topo):
         tt(col(kc, 13), T.pi[:, 3:4], T.pi[:, 4:5], A.not_equal, ["pi3", "pi4"], ["k13"])
         ts(lst(L_K, 1), col(kc, 13), K + 16.0, col(kc, 12), A.mult, A.add, ["k12", "k13"], ["L_K"])
 
-    def successors():
-        runs = [(T.c1[:, M * s:M * s + M - 1], T.bt[:, 48 * s + 49:48 * s + 48 + M], 65) for s in range(7)]
-        runs += [(T.c1[:, M - 1:7 * M:M], T.bt[:, 48::48], 65 - M), (T.c1[:, 7 * M:C - 2], T.bt[:, 2:M], 66),
-                 (T.c1[:, C - 2:C], T.bt[:, 0:2], 66 - M)]
-        for i, (o, a, c) in enumerate(runs):
-            act(o, a, AF.Identity, ["bt"], ["c1" if i == len(runs) - 1 else "c1_%d" % i], bias=c / 128.0, scale=1 / 65536.0)
-
     def plane_lists():
         ts(w28(3, 0, 24), w28(0, 4, 28), float(C), None, A.min, None, ["n", "L_OWN0"], ["n0", "o0"])
         for b in range(4):
@@ -273,17 +269,11 @@ def rank_program(g, core, T, topo):
         fill(T.reset[:, 0::M], 8, BIG, ["reset"])
         fill(T.win[:, 0:192], 192, 0.0, ["win"])
         fill(T.rr[:, 24 * M + M - 1::M], 8, BIG, ["rrz"])
-        fill(T.lq[:, 0::M], 25, -1.0, ["lqz"])
 
     def diagonal():
         for a in (16, 32, 64, 128, 256):
             e = min(2 * a, 448)
             act(T.diag[:, a:e], T.diag[:, 0:e - a], AF.Copy, ["diag"], ["diag"])
-
-    def first_successors():
-        act(T.c0[:], T.c0[:], AF.Copy, ["c0"], ["c0"], scale=1 / 65536.0)
-        for a in (T.c0[:, M - 1::M], col(T.c0, C - 2)):
-            act(a, a, AF.Identity, ["c0"], ["c0"], bias=-C / 65536.0)
 
     def delay_list():
         cp(col(T.ti, 0), col(T.tc, 0), ["tc0"], ["ti0"])
@@ -300,34 +290,37 @@ def rank_program(g, core, T, topo):
            ["ones"], ["et%d" % b])
 
     dma("y", T.ut[:], T.u[:], "lu", [], ["ut"])
-    dma("s", T.xt[:, 0:4 * C - 512], T.x[:, 0:4 * C - 512], "lx", [], ["xta"])
-    dma("s", T.xt[:, 4 * C - 512:4 * C], T.x[:, 4 * C - 512:], "lz", [], ["xtb"])
+    dma("s", T.xt[:, 0:768], T.x[:, 0:768], "lx", [], ["xta"])
+    dma("y", T.xt[:, 768:4 * C], T.x[:, 768:], "lz", [], ["xtb"])
     iota(T.pi[:, 0:1], [[0, 1]], 0, 1, ["pi0"], f=False)
     iota(io[:], [[1, 32]], 0, 0, ["io"])
     ms(T.ones[:], 1.0, ["ones"])
     unit_tile(0)
-    unit_tile(1)
     iota(T.sm[:, 0:30], [[1, 15], [16, 2]], 0, 0, ["sm"])
     ts(T.pi[:, 1:2], T.pi[:, 0:1], 15, None, A.bitwise_and, None, ["pi0"], ["pi1"])
     ms(T.xt[:, 4 * C:], 0.0, ["xz"])
-    ms(T.prow[:, C:], FAR, ["prz", "prow"])
+    ms(T.prow[:, C:], FAR, ["prz"])
     cp(col(kc, 0), T.pi[:, 1:2], ["pi1"], ["q"])
     ts(lst(L_U0, 8), io[:, 0:8], 16.0, None, A.mult, None, ["io"], ["L_U0"])
     ts(T.diag[:, 0:16], io[:, 0:16], col(kc, 0), None, A.is_equal, None, ["io", "q"], ["diag"])
     ts(lst(L_U1, 8), io[:, 0:8], 16.0, 1.0, A.mult, A.add, ["io"], ["L_U1"])
     cp(lst(L_B, 24), io[:, 0:24], ["io"], ["L_B"])
-    issue(listed(own_lists, masks, turn_list))
+    issue(listed(own_lists, turn_list))
+    late = listed(masks)
     issue(listed(fills, diagonal))
     quant("qu", 0, 128, T.ut, ["ut"])
+    quant("q0", 0, 192, T.xt, ["xta"], "qpa")
+    quant("q0", 192, C, T.xt, ["xtb"], "qpe")
     pick("su0", 0, 128, "qu", 128, lst(L_U0, 8), "L_U0", "su0")
-    quant("q0", 0, C - 128, T.xt, ["xta"], "qa")
-    quant("q0", C - 128, C, T.xt, ["xtb"], "qb")
-    pick("su1", 0, 128, "qu", 128, lst(L_U1, 8), "L_U1", "su1")
 
     wd, rr, rw = T.wd, T.rr, T.rw
     xpl = lambda b: wd[:, 544 * b + K:544 * b + 544]
     Wv = lambda a, e: rr[:, M * a + M - 1:M * e:M]
     row = rw[:, :, 0:24]
+
+    def planes(a, e):
+        for b in range(a, e):
+            ts(xpl(b), T.xs[:, b::4], 64.0, None, A.mult, None, ["xs%d" % b, "xs4"], ["xp%d" % b])
 
     def first_planes(a, e):
         for b in range(a, e):
@@ -337,75 +330,99 @@ def rank_program(g, core, T, topo):
         q, land = "q%d" % t, "land%d" % t
         n = C if t == 0 else NC
         nb = n // 16
-        h = n - 128
-        mm("pa", "su0", 0, q, 0, h, ["su0", "su0s", "qa"])
-        mm("pe", "su0", 0, q, h, n, ["su0", "su0s", "qb"])
-        mm("pc", "su0", 0, q, 0, n, ["su0", "su0s", "qa", "qb"])
-        mm("pb", "su1", 0, q, 0, n, ["su1", "su1s", "qa", "qb"])
-        tr(T.tp[:, 0:h], T.pa[:, 0:h], ["pa"], ["tpa"])
-        tr(T.tp[:, h:n], T.pe[:, 0:128], ["pe"], ["tpb"])
-        cp(T.ps[:, 24 * t:24 * t + nb], T.tp[:, 0:n:16], ["tpa", "tpb"], ["ps%d" % t])
-        send(t, T[land + "s"][:], T[q + "s"][:], "a%d" % t, ["qa", "qb"], [])
+        parts = (FIRST, LATER)[min(t, 1)]
+        qk = ["q" + ps for a, e, ps in parts]
+        again_in = ("pc", "pd1", "pd2")
+        turned = [lambda a=a, e=e, ps=ps: mm(ps, "qu", 0, q, a, e, ["qu", "q" + ps]) for a, e, ps in parts]
+        spread = [lambda a=a, e=e, ps=ps, pb=pb: mm(pb, "su0", 0, q, a, e, ["su0", "su0s", "q" + ps])
+                  for (a, e, ps), pb in zip(parts, again_in)]
+        for f in turned + spread:
+            f()
+        for a, e, ps in parts:
+            tr(T.tp[:, a:e], T[ps][:, 0:e - a], [ps], ["tp" + ps])
+        cp(T.ps[:, 24 * t:24 * t + nb], T.tp[:, 0:n:16], ["tp" + ps for a, e, ps in parts], ["ps%d" % t])
+        if t == 0:
+            pick("su1", 0, 128, "qu", 128, lst(L_U1, 8), "L_U1", "su1")
+        mm("pb", "su1", 0, q, 0, n, ["su1", "su1s"] + qk)
+        h = FIRST[0][1] if t == 0 else 0
+        if t == 0:
+            send(t, T.land0s[:, 0:h], T.q0s[:, 0:h], "a0", qk[0:1], [])
         send(t, T.lp[:, 24 * t:24 * t + nb], T.ps[:, 24 * t:24 * t + nb], "p%d" % t, ["ps%d" % t], ["lp%d" % t])
-        send(t, T[land][:].bitcast(dt.uint8), T[q][:].bitcast(dt.uint8), "a%d" % t, ["qa", "qb"], [land])
-        act(T.prow[:, 0:n], T.pc[:, 0:n], AF.Copy, ["pc"], ["prow"])
+        for i, ((a, e, ps), pb) in enumerate(zip(parts, again_in)):
+            act(T.prow[:, a:e], T[pb][:, 0:e - a], AF.Copy, [pb, "prz"], ["prow%d" % i])
+        if t == 0:
+            issue(listed(plane_lists, tables))
+            first_planes(0, 1)
         act(T.sg[:, 0:n], T.pb[:, 0:n], AF.Sign, ["pb"], ["sg0"])
         act(T.sg[:, NC:NC + n], T.sg[:, 0:n], AF.Relu, ["sg0"], ["sg1", "tc0"], accum_out=col(T.tc, 0))
         if t == 0:
+            unit_tile(1)
+        send(t, T[land][:].bitcast(dt.uint8), T[q][:].bitcast(dt.uint8), "a%d" % t, qk + ["tc0"] * min(t, 1), [])
+        send(t, T[land + "s"][:, h:], T[q + "s"][:, h:], "a%d" % t, qk, [land])
+        if t == 0:
             unit_tile(2)
             unit_tile(3)
-            iota(T.c0[:], [[1, 8], [8 - 512, M]], 64 * 512 + 9, 0, ["c0"])
+            for b in range(3):
+                op("g", lambda: g.affine_select(T.keepc[:, NR * b:NR * b + NR], T.ones[:, 0:NR], [[1, NR]], A.not_equal, 0.0, 0, 0),
+                   ["ones"], ["keepc" if b == 2 else "keepc%d" % b])
+            iota(T.sr[:, 0:24], [[0, 3], [1, 8]], 9, 0, ["sr0"])
+            iota(T.sr[:, 24:48], [[0, 3], [48, 8]], 49, 0, ["sr1"])
             iota(T.val[:], [[1, NC]], 0, 0, ["val"])
-            iota(T.bt[:], [[16, 8], [1 - 3 * 512, 16], [128 - 512, 3]], 0, 0, ["bt"])
             iota(T.plc[:], [[1, 24], [24, 16]], 0, 0, ["plc"])
-            plane_lists()
         if t == 1:
-            successors()
+            fill(T.sr[:, 31:48:8], 3, 2.0, ["sr1"])
         own = "L_OWN%d" % min(t, 1)
-        tt(T.mm[:], T.prow[:].indirect(lst(L_OWN + 28 * min(t, 1), 28)), T.diag[:], A.mult, ["prow", "prz", own, "diag"], ["mm"])
+        tt(T.mm[:], T.prow[:].indirect(lst(L_OWN + 28 * min(t, 1), 28)), T.diag[:], A.mult,
+           ["prow0", "prow1", "prow2", "prz", own, "diag"], ["mm"])
         scan(T.ms[:], T.keep16[:], T.mm[:], A.mult, A.add, ["keep16", "mm"], ["ms"])
         if t == 0:
-            first_planes(0, 3)
-            issue(listed(tables, own_lists_state))
-            cp(lst(L_ROW, 30), T.sm[:, 0:30], ["sm"], ["L_ROW"])
+            first_planes(1, 3)
+
+        def unit_codes(b):
+            if t == 0:
+                quant("qe", 128 * b, 128 * b + 128, T.et, ["et%d" % b], "qe%d" % b)
+            mm("pd%d" % b, "qe", 128 * b, land, 0, n, ["qe%d" % b, land])
         delay = listed(delay_list)
         if t == 0:
-            issue(delay, 4)
+            issue(delay, 1)
+            ts(wd[:, 544 * 3 + K:544 * 3 + K + 192], T.xt[:].indirect(lst(L_X + 72, 12)), 64.0, None, A.mult, None,
+               ["xta", "xtb", "xz", "L_X3"], ["xp3"])
+            issue(listed(lambda: issue(delay, 3), own_columns))
         else:
-            for b in range(4):
-                issue(delay, 1)
-                ts(xpl(b), T.xs[:, b::4], 64.0, None, A.mult, None, ["xs%d" % b, "xs4"], ["xp%d" % b])
+            issue(delay, 1)
+            planes(0, 1)
+            issue(delay, 1)
         lw = T.lp[:, 24 * t:24 * t + nb]
         cuts = ((0, 8), (8, 16), (16, nb))
-        for i, (a, e) in enumerate(cuts):
+        for i, (a, e) in enumerate(((0, 8), (8, 16), (16, 20), (20, nb))):
             src, key = lw.indirect(lst(L_B + a, e - a)), ["lp%d" % t, "L_B"]
-            if i == 0:
+            if i % 2 == 0:
                 cp(T.xb[:, 16 * a:16 * e], src, key, ["xb%d" % i])
             else:
                 act(T.xb[:, 16 * a:16 * e], src, AF.Copy, key, ["xb%d" % i])
         for i, (a, e) in enumerate(cuts):
-            tr(T.far[:, 16 * a:16 * e] if t == 0 else T.far[:, i::3], T.xb[:, 16 * a:16 * e], ["xb%d" % i], ["far%d" % i])
-        rows = [("ab", c) for c in list(range(4, 12)) + list(range(4)) + list(range(12, 27))] + [("aw", c) for c in range(24, 28)]
-        for buf, c in rows:
-            s = (c - 4) % 8
-            act(T[buf][:, M * c:M * c + M], T.far[:, s:C:8] if t == 0 else T.far[:, 48 * s:48 * s + M], AF.Abs,
-                ["far0", "far1", "far2", "ms"], ["%s%d" % (buf, c)], bias=col(T.ms, 16 * c + 15), scale=-1.0)
+            tr(T.far[:, 16 * a:16 * e] if t == 0 else T.far[:, i::3], T.xb[:, 16 * a:16 * e], ["xb%d" % i, "xb%d" % (i + i // 2)], ["far%d" % i])
+        issue(delay if t else late, 2)
+        phase = lambda s: T.far[:, s:C:8] if t == 0 else T.far[:, 48 * s:48 * s + M]
+        fk = ["far0", "far1", "far2", "ms"]
+        issue(delay, 1)
+        for c in range(4):
+            ts(T.zf[:, 96 + M * c:96 + M * c + M], phase(c + 4), col(T.ms, 16 * c + 15), None, A.subtract, None, fk, ["dd%d" % c])
+            issue(delay, c % 2)
+        for buf, c in [("ab", c) for c in range(4, 27)] + [("aw", c) for c in range(24, 28)]:
+            act(T[buf][:, M * c:M * c + M], phase((c - 4) % 8), AF.Abs, fk, ["%s%d" % (buf, c)], bias=col(T.ms, 16 * c + 15), scale=-1.0)
+            if c == 11:
+                act(T.ab[:, 0:4 * M], T.zf[:, 96:], AF.Abs, ["dd%d" % i for i in range(4)], ["ab%d" % i for i in range(4)])
         if t == 0:
-            issue(delay, 1)
-            quant("qe", 0, 512, T.et, ["et%d" % b for b in range(4)])
+            cp(lst(L_ROW, 30), T.sm[:, 0:30], ["sm"], ["L_ROW"])
             issue(delay)
-            first_successors()
             wait("y", wrote[land])
             dma("y", T.qw[:].bitcast(dt.uint8), T.wc[:], "lw", [], ["qw"])
             dma("y", T.qws[:], T.ws[:], "lw", [], ["qw"])
             dma("y", T.vt[:], T.v[:], "lv", [], ["vt"])
-        elif t == 1:
-            issue(listed(lambda: issue(delay), natural))
         else:
+            planes(1, 2)
             issue(delay)
-            quant("qv", 0, 128, T.vt, ["vt"])
-        for b in range(4):
-            mm("pd%d" % b, "qe", 128 * b, land, 0, n, ["qe", land])
 
         def again(a, e):
             cp(T.aw[:, M * a:M * e], T.ab[:, M * a:M * e], ["ab%d" % c for c in range(a, e)], ["aw%d" % c for c in range(a, e)])
@@ -418,12 +435,16 @@ def rank_program(g, core, T, topo):
         def least(k):
             scan(rr[:, C * k:C * k + C], T.reset[:], T.dm[:, C * k:C * k + C], A.max, A.min,
                  ["reset", "dm%d" % k], ["rr%d" % k])
+        issue(late, 2)
         again(4, 9)
+        issue(late, 1)
         again(9, 12)
+        issue(late, 2)
         larger(0)
         again(12, 16)
         least(0)
         again(16, 20)
+        issue(late, 2)
         larger(1)
         again(20, 24)
         least(1)
@@ -433,25 +454,37 @@ def rank_program(g, core, T, topo):
         tt(s8(0), Wv(0, 8), Wv(8, 16), A.min, rk[0:2], ["s0"])
         tt(s8(1), Wv(0, 8), Wv(8, 16), A.max, rk[0:2], ["s1"])
         least(2)
+        issue(late, 2)
+        if t:
+            planes(3, 4)
 
         def before(c):
-            o, a, m = T.lq[:, M * c + 1:M * c + M], rr[:, M * c:M * c + M - 1], col(rr, M * c + M - 1)
-            if c < NS:
-                act(o, a, AF.Sign, ["rr%d" % (c // 8), "lqz"], ["lq%d" % c], bias=m, scale=-1.0)
-            else:
-                ts(o, a, m, -1.0, A.is_gt, A.mult, ["rr%d" % (c // 8), "lqz"], ["lq%d" % c])
-        for c in range(NS):
+            act(T.lq[:, M * c:M * c + M - 1], rr[:, M * c:M * c + M - 1], AF.Sign, ["rr%d" % (c // 8)], ["lq%d" % c, "jm%d" % c],
+                bias=col(rr, M * c + M - 1), scale=-1.0, accum_out=col(T.jm, c))
+        if t == 0:
+            act(T.sr[:, 0:24], T.sr[:, 0:24], AF.Copy, ["sr0"], ["sr0"], scale=0.125)
+        ns = NS[t]
+        for c in range(ns):
             before(c)
+
+        def successor_list():
+            i = min(t, 1)
+            tt(T.zf[:, 0:24], T.sr[:, 24 * i:24 * i + 24], T.jm[:], A.subtract, ["jm%d" % c for c in range(24)] + ["sr%d" % i], ["z0"])
+            ts(T.lz[:], T.zf[:, 0:24], (8.0, 1.0)[i], None, A.mult, None, ["z0"], ["lz"])
+        spare = listed(successor_list)
         tr(T.t1[:], Wv(0, 32), rk + ["rrz"], ["t1"])
         tt(s8(2), s8(1), Wv(16, 24), A.min, rk + ["s1"], ["s2"])
-        act(T.xg[:, 0:288], T.t1[:].indirect(lst(L_ROW, 18)), AF.Copy, ["t1", "L_ROW"], ["xg0"])
-        cp(T.xg[:, 288:480], T.t1[:].indirect(lst(L_ROW + 18, 12)), ["t1", "L_ROW"], ["xg1"])
-        tt(T.cand[:, 0:8], s8(0), s8(2), A.max, ["s0", "s2"], ["mid"])
-        tr(rw[:, 9:15, :], T.xg[:, 288:480], ["xg1"], ["rw1"])
         tt(s8(3), s8(0), Wv(16, 24), A.min, rk + ["s0"], ["low"])
-        tr(rw[:, 0:9, :], T.xg[:, 0:288], ["xg0"], ["rw0"])
+        cut = (0, 6, 10, 15)
+        act(T.xg[:, 0:192], T.t1[:].indirect(lst(L_ROW, 12)), AF.Copy, ["t1", "L_ROW"], ["xg0"])
+        act(T.xg[:, 192:320], T.t1[:].indirect(lst(L_ROW + 12, 8)), AF.Copy, ["t1", "L_ROW"], ["xg1"])
+        cp(T.xg[:, 320:480], T.t1[:].indirect(lst(L_ROW + 20, 10)), ["t1", "L_ROW"], ["xg2"])
+        tt(T.cand[:, 0:8], s8(0), s8(2), A.max, ["s0", "s2"], ["mid"])
         tt(s8(4), s8(1), Wv(16, 24), A.max, rk + ["s1"], ["upp"])
-        rwk = ["rw0", "rw1"]
+        for i in (2, 0, 1):
+            tr(rw[:, cut[i]:cut[i + 1], :], T.xg[:, 32 * cut[i]:32 * cut[i + 1]], ["xg%d" % i], ["rw%d" % i])
+        issue(late)
+        rwk = ["rw0", "rw1", "rw2"]
 
         def count(i, j, key):
             act(T.junk[:, NR * j:NR * j + NR], row, AF.Sign, rwk + [key], ["junk%d" % j, "cnt%d" % i],
@@ -460,70 +493,91 @@ def rank_program(g, core, T, topo):
         def less(i, j, key):
             ts(T.cmp[:, NR * j:NR * j + NR], row, col(T.cand, i), None, A.is_lt, None, rwk + [key], ["cmp%d" % j])
 
-        def tally(j, key):
-            a = T.cmp[:, NR * j:NR * j + NR]
-            scan(T.cms[:, NR * j:NR * j + NR], a, a, A.add, A.max, ["cmp%d" % j], [key])
-        for i in (0, 1, 2, 3, 5, 6):
-            count(i, i, "mid")
-        less(4, 3, "mid")
-        less(7, 4, "mid")
-        cc = "c%d" % min(t, 1)
-
-        def first(k):
-            scan(T.st[:, C * k:C * k + C], T.lq[:, C * k:C * k + C], T[cc][:], A.add, A.max,
-                 ["lq%d" % c for c in range(8 * k, 8 * k + 8)] + [cc], ["st%d" % k])
-        for c in range(NS, 24):
-            before(c)
-            if c == NS:
-                tally(3, "cms4")
-                tally(4, "cms3")
+        def tally(a, e):
+            scan(T.cms[:, NR * a:NR * e], T.keepc[:, 0:NR * (e - a)], T.cmp[:, NR * a:NR * e], A.mult, A.add,
+                 ["keepc"] + ["cmp%d" % j for j in range(a, e)], ["cms%d" % j for j in range(a, e)])
         pen, lh, r3 = T.pen, T.lh, T.r3
-        ts(pen[:, 12:16:3], T.cms[:, 4 * NR - 1::NR], K - 0.5, BIG, A.is_lt, A.mult, ["cms3"], ["pen1b"])
-        first(0)
-        ts(pen[:, 8:12], T.cnt[:, 0:4], half, BIG, A.is_lt, A.mult, ["cnt%d" % i for i in range(4)], ["pen1a"])
-        first(1)
-        tt(lh[:, 32:37], T.srt[:, 32:37], pen[:, 8:13], A.min, ["upp", "pen1a", "pen1b"], ["lh2"])
-        tt(T.cand[:, 8:13], lh[:, 32:37], T.srt[:, 24:29], A.max, ["lh2", "low"], ["nxt"])
-        for i in range(8, 13):
-            count(i, i - 1, "nxt")
-        ts(pen[:, 13:15], T.cnt[:, 5:7], half, BIG, A.is_lt, A.mult, ["cnt5", "cnt6"], ["pen1c"])
-        first(2)
-        tt(lh[:, 37:40], T.srt[:, 37:40], pen[:, 13:16], A.min, ["upp", "pen1c", "pen1b"], ["lh3"])
-        cp(pen[:, 0:8], pen[:, 8:16], ["pen1a", "pen1b", "pen1c"], ["pen0"])
-        ts(T.zi[:, 0:24], T.st[:, M - 1::M], 65536.0, None, A.mult, None, ["st0", "st1", "st2"], ["zi0"])
-        tt(T.cand[:, 13:16], lh[:, 37:40], T.srt[:, 29:32], A.max, ["lh3", "low"], ["nxu"])
-        ts(T.zi[:, 24:48], T.zi[:, 0:24], 511, None, A.bitwise_and, None, ["zi0"], ["zi1"])
-        for i in range(3):
-            less(13 + i, i, "nxu")
-        cp(T.lz[:], T.zi[:, 24:48], ["zi1"], ["lz"])
-        for j in range(3):
-            tally(j, "cms%d" % j if j < 2 else "cms")
-        for b in range(4):
-            act(T.dsb[:, NC * b:NC * b + n], T["pd%d" % b][:, 0:n], AF.Copy, ["pd%d" % b], ["dsb%d" % b])
+        big = lambda a: 2 * BIG if a < 8 else BIG
+        by_sign = lambda a, e, key: ts(pen[:, 8 + a:8 + e], T.cnt[:, a:e], half, big(a), A.is_lt, A.mult,
+                                       ["cnt%d" % i for i in range(a, e)], [key])
+        by_sum = lambda a, j, e, key: ts(pen[:, 8 + a:8 + a + e - j], T.cms[:, NR * j + NR - 1:NR * e:NR], K - 0.5, big(a),
+                                         A.is_lt, A.mult, ["cms%d" % i for i in range(j, e)], [key])
+        for i in (0, 1, 2, 6, 7):
+            count(i, i, "mid")
+        for i in (3, 4, 5):
+            less(i, i, "mid")
+        tally(3, 5)
+        tally(5, 6)
+        by_sign(0, 3, "pen1a")
+        by_sum(3, 3, 6, "pen1b")
 
-        ts(pen[:, 16:21], T.cnt[:, 8:13], half, BIG, A.is_lt, A.mult, ["cnt%d" % i for i in range(8, 13)], ["pen2"])
-        ts(pen[:, 21:24], T.cms[:, NR - 1:3 * NR:NR], K - 0.5, BIG, A.is_lt, A.mult, ["cms"], ["pen3"])
-        for b in range(4):
-            act(T.zall[:, NC * b:NC * b + NC], T.dsb[:, NC * b:NC * b + n].indirect(T.lz[:]), AF.Copy,
-                ["dsb%d" % b, "lz"], ["zall%d" % b])
+        def unpack(b, i):
+            e = min(128 * i + 128, n)
+            o = T.dsb[:, NC * b + 128 * i:NC * b + e] if t == 0 else T.dsb[:, NC * b + i:NC * b + NC:3]
+            if b < 3:
+                cp(o, T["pd%d" % b][:, 128 * i:e], ["pd%d" % b], ["dsb%d%d" % (b, i)])
+            else:
+                act(o, T["pd%d" % b][:, 128 * i:e], AF.Copy, ["pd%d" % b], ["dsb%d%d" % (b, i)])
+        if t:
+            for b in (2, 0, 1, 3):
+                unit_codes(b)
+        between = (lambda i: unpack(2, i) if i < 3 else None) if t else unit_codes
+        between(0)
+        tt(lh[:, 32:38], T.srt[:, 32:38], pen[:, 8:14], A.min, ["upp", "pen1a", "pen1b"], ["lh2"])
+        between(1)
+        tt(T.cand[:, 8:14], lh[:, 32:38], T.srt[:, 24:30], A.max, ["lh2", "low"], ["nxt"])
+        for i in range(8, 13):
+            count(i, i, "nxt")
+        between(2)
+        by_sign(6, 8, "pen1c")
+        less(13, 0, "nxt")
+        tt(lh[:, 38:40], T.srt[:, 38:40], pen[:, 14:16], A.min, ["upp", "pen1c"], ["lh3"])
+        tally(0, 1)
+        tt(T.cand[:, 14:16], lh[:, 38:40], T.srt[:, 30:32], A.max, ["lh3", "low"], ["nxu"])
+        between(3)
+        less(14, 1, "nxu")
+        less(15, 2, "nxu")
+        tally(1, 2)
+        tally(2, 3)
+        for c in range(ns, 24):
+            before(c)
         if t == 0:
-            first_planes(3, 4)
+            for b in (2, 3):
+                act(T.dsb[:, NC * b:NC * b + C], T["pd%d" % b][:, 0:C], AF.Copy, ["pd%d" % b], ["dsb%d%d" % (b, i) for i in range(3)])
+        else:
+            for i in range(3):
+                unpack(3, i)
+
+        unpack(0, 0)
+        by_sum(13, 0, 3, "pen3")
+        unpack(0, 1)
+        by_sign(8, 13, "pen2")
+        unpack(0, 2)
         pk = ["pen1a", "pen1b", "pen1c", "pen2", "pen3"]
         tt(lh[:, 0:16], T.cand[:], pen[:, 8:24], A.min, ["mid", "nxt", "nxu"] + pk, ["lh0"])
         tt(lh[:, 16:32], T.cand[:], pen[:, 8:24], A.max, ["mid", "nxt", "nxu"] + pk, ["lh1"])
-        red(col(r3, 2), pen[:], A.add, pk + ["pen0"], ["r2"])
+        op("v", lambda: V.tensor_reduce(col(r3, 2), pen[:, 8:24], X, A.add, negate=True), pk, ["r2"])
         red(col(r3, 0), lh[:, 0:16], A.max, ["lh0"], ["r0"])
         red(col(r3, 1), lh[:, 16:32], A.min, ["lh1"], ["r1"])
         xe, xf = T.xe, T.xf
-        ts(xe[:, 64:96], mk[:, 0:32], col(r3, 2), None, A.mult, None, ["same", "r2"], ["xe2"])
+        ts(xe[:, 64:96], mk[:, 0:32], col(r3, 2), (K - 0.5) * BIG / 32, A.mult, A.add, ["same", "r2"], ["xe2"])
         ts(xe[:, 0:32], mk[:, 0:32], col(r3, 0), None, A.mult, None, ["same", "r0"], ["xe0"])
         ts(xe[:, 32:64], mk[:, 96:128], col(r3, 1), None, A.max, None, ["other", "r1"], ["xe1"])
+        unpack(1, 0)
         tr(xf[:], xe[:], ["xe0", "xe1", "xe2"], ["xf"])
+        unpack(1, 1)
         red(col(r3, 5), xf[:, 64:96], A.add, ["xf"], ["r5"])
         red(col(r3, 4), xf[:, 32:64], A.min, ["xf"], ["r4"])
         red(col(r3, 3), xf[:, 0:32], A.max, ["xf"], ["r3"])
-        ts(col(r3, 6), col(r3, 5), (K - 0.5) * BIG, col(r3, 4), A.is_lt, A.mult, ["r4", "r5"], ["r6"])
-        tt(col(r3, 7), col(r3, 6), col(r3, 3), A.max, ["r6", "r3"], ["tau"])
+        unpack(1, 2)
+        ts(col(r3, 7), col(r3, 5), col(r3, 3), col(r3, 4), A.max, A.min, ["r3", "r4", "r5"], ["tau"])
+        dk = ["dsb%d%d" % (b, i) for b in range(4) for i in range(3)]
+        if t == 0:
+            for b in range(4):
+                act(T.dsb[:, NC * b + C:NC * b + C + 9], T.dsb[:, NC * b:NC * b + 9], AF.Copy, dk, ["ring%d" % b])
+        else:
+            for i in range(2):
+                act(T.dsb[:, M + i::48], T.dsb[:, i::48], AF.Copy, dk, ["ring%d" % (3 * i)])
         tau = col(r3, 7)
         p24 = lambda i: T.pw[:, 24 * i:24 * i + 24]
         W, cs = Wv(0, 24), T.cs
@@ -532,9 +586,16 @@ def rank_program(g, core, T, topo):
         ts(p24(0), W, tau, 1000.0, A.is_gt, A.mult, rk + ["tau"], ["p0"])
         scan(cs[:], T.le[:], T.le[:], A.add, A.max, ["lt", "eq"], ["cs"])
         ts(p24(1), W, tau, None, A.is_ge, None, rk + ["tau"], ["p1"])
+        issue(spare, 1)
         ts(xe[:, 0:32], mk[:, 32:64], col(cs, 47), None, A.mult, None, ["tri", "cs"], ["xe0"])
         ts(xe[:, 32:64], mk[:, 128:160], col(cs, 23), K / 32.0, A.mult, A.add, ["ntri", "cs"], ["xe1"])
         tt(p24(2), cs[:, 24:48], p24(0), A.add, ["cs", "p0"], ["p2"])
+        issue(spare)
+        for b in range(4):
+            act(T.zall[:, NC * b:NC * b + NC], T.dsb[:, NC * b:NC * b + (C + 9, NC)[min(t, 1)]].indirect(T.lz[:]), AF.Copy,
+                dk + ["ring0", "ring3", "lz"], ["zall%d" % b])
+        if t == 0:
+            act(wd[:, 544 * 3 + K + 192:], T.xt[:].indirect(lst(L_X + 84, 12)), AF.Copy, ["xta", "xtb", "xz", "L_X3"], ["xp3"], scale=64.0)
         tr(xf[:, 0:64], xe[:, 0:64], ["xe0", "xe1"], ["xf"])
         tt(p24(3), p24(1), w28(4, 0, 24), A.mult, ["p1", "J"], ["p3"])
         red(col(r3, 8), xf[:, 0:32], A.add, ["xf"], ["r8"])
@@ -542,14 +603,25 @@ def rank_program(g, core, T, topo):
         ts(p24(4), cs[:, 0:24], col(cs, 23), -1.0, A.subtract, A.add, ["cs"], ["p4"])
         ts(p24(5), p24(2), col(r3, 8), col(r3, 9), A.add, A.is_gt, ["p2", "r8", "r9"], ["p5"])
         ts(p24(6), cs[:, 24:48], col(r3, 8), col(r3, 9), A.add, A.min, ["cs", "r8", "r9"], ["p6"])
+        spare = listed((own_lists_state, natural, lambda: quant("qv", 0, 128, T.vt, ["vt"]))[t])
+        issue(spare, t == 1)
         tt(p24(7), p24(5), p24(3), A.mult, ["p5", "p3"], ["p7"])
         tt(p24(8), p24(6), p24(4), A.add, ["p6", "p4"], ["p8"])
+        issue(spare, 1)
         tt(p24(9), p24(8), p24(7), A.max, ["p7", "p8"], ["p9"])
+        issue(spare, 1)
         cp(T.lo[:], p24(9), ["p9"], ["lo"])
+        issue(spare, 1)
         cp(T.win[:, 16:].indirect(T.lo[:]), T.val[:], ["lo", "val"], ["win"])
+        if t:
+            planes(2, 3)
+        else:
+            issue(spare, 1)
         tr(T.es[:, 0:K], T.win[:, 16:16 + K], ["win"], ["es0"])
         tr(T.es[:, K:], T.win[:, 0:192], ["win"], ["es1"])
+        issue(spare, 1)
         cp(T.lk[:], T.es[:].indirect(lst(L_K, 1)), ["es0", "es1", "L_K"], ["lk"])
+        issue(spare)
         lk = T.lk[:, 0:10]
         zsrc = lambda b: T.zall[:, NC * b:NC * b + NC].indirect(lk)
         for b in (0, 1):
@@ -570,13 +642,11 @@ def rank_program(g, core, T, topo):
             act(T.xs[:, 64 * a + b:64 * e:4], usrc(b, a, e), AF.Copy, ["g%d" % b, "xp%d" % b, "lo"], [key], scale=0.015625)
         for b, a, e in ((0, 0, 24), (1, 0, 16)):
             ts(T.xs[:, 64 * a + b:64 * e:4], usrc(b, a, e), 0.015625, None, A.mult, None, ["g%d" % b, "xp%d" % b, "lo"], ["xs%d" % b])
-        if t + 1 < R:
-            quant("q%d" % (t + 1), 0, NC - 128, T.xs, ["xs%d" % b for b in range(4)], "qa")
-            quant("q%d" % (t + 1), NC - 128, NC, T.xs, ["xs%d" % b for b in range(5)], "qb")
-        else:
-            quant("q3", 0, NC, T.xs, ["xs%d" % b for b in range(5)])
+        for a, e, ps in LATER if t + 1 < R else ((0, 256, "pa"), LATER[2]):
+            quant("q%d" % (t + 1), a, e, T.xs, ["xs%d" % b for b in range(4 if e < NC else 5)], "q" + ps)
+    wrote["q3"] = wrote["qpe"]
 
-    runs = ((0, K, "pa"), (K, C, "pe"))
+    runs = ((0, C - 128, "pa"), (C - 128, C, "pe"))
     for a, e, ps in runs:
         pick("q3n", a, e, "q3", NC, lst(L_NAT + a // 16, (e - a) // 16), "L_NAT", "n" + ps)
         dma("y", T.oc[:, 4 * a:4 * e], T.q3n[:, a:e].bitcast(dt.uint8), "out", ["n" + ps], [])

from concourse.bass import DstId, RemoteDMATransfer
from concourse.mybir import dt, AluOpType, AxisListType, ActivationFunctionType

C, K, M, R = 352, 160, 44, 3
STEP = [3, 1, 5]
NC = 384
NR = 360
NS = (12, 11, 11)
FIRST = ((0, 192, "pa"), (192, C, "pe"))
LATER = ((0, 128, "pa"), (128, 256, "pd0"), (256, NC, "pe"))
BIG = float(2 ** 80)
FAR = float(2 ** 90)
Q4, U8, F32, BF, I32, U16 = "float8_e4m3fn_x4", "uint8", "float32", "bfloat16", "int32", "uint16"

SCRATCH = {}


def _sb(name, n, dtype):
    SCRATCH[name] = ("sbuf", [128, n], dtype)


def _mx(name, n):
    _sb(name, n, Q4)
    _sb(name + "s", n, U8)


for _n, _w in (("qu", 128), ("su0", 128), ("su1", 128), ("qv", 128), ("qw", 512), ("qe", 512),
               ("q0", C), ("land0", C), ("q1", NC), ("land1", NC), ("q2", NC), ("land2", NC),
               ("q3", NC), ("q3n", C), ("qz", K)):
    _mx(_n, _w)
for _n, _s, _d in (
        ("xt", 4 * C + 16, BF), ("ut", 512, BF), ("vt", 512, BF), ("et", 2048, BF), ("xs", 4 * NC, BF),
        ("wd", 4 * 544, BF), ("dsb", 4 * NC, BF), ("zall", 4 * NC, BF), ("zt", 4 * K, BF), ("f64", 4 * K, F32),
        ("pi", 8, I32), ("kc", 16, F32), ("io1", 32, F32), ("sm", 32, F32),
        ("sr", 72, F32), ("keepc", 3 * NR, BF), ("plc", NC, F32), ("val", NC, F32),
        ("diag", 448, F32), ("keep16", 448, BF), ("reset", C, BF),
        ("ones", 512, BF), ("mk", 160, F32), ("kt", 24 * 12, F32), ("ki", 24 * 3, I32),
        ("kw", 28 * 5, F32), ("lc", 320, U16),
        ("tp", NC, F32), ("ps", 72, F32), ("lp", 72, F32), ("xb", NC, F32), ("far", NC, F32),
        ("prow", 392, F32), ("mm", 448, F32), ("ms", 448, F32), ("sg", 2 * NC, BF),
        ("tc", 8, F32), ("ti", 8, I32), ("bl", 66, F32), ("lb", 22, U16),
        ("ab", 28 * M, F32), ("aw", 28 * M, F32), ("dm", 3 * C, F32), ("rr", 32 * M, F32), ("lq", 3 * C, BF),
        ("jm", 24, F32), ("zf", 96 + 4 * M, F32), ("lz", 24, U16), ("t1", 32, F32),
        ("xg", 480, F32), ("srt", 40, F32), ("cand", 16, F32), ("cnt", 16, F32),
        ("junk", 13 * NR, BF), ("cmp", 6 * NR, BF), ("cms", 6 * NR, BF), ("pen", 24, F32), ("lh", 40, F32),
        ("r3", 16, F32), ("xe", 96, F32), ("xf", 96, F32), ("le", 48, F32), ("cs", 48, F32),
        ("pw", 24 * 10, F32), ("lo", 24, U16), ("win", 560, F32), ("es", K + 192, F32),
        ("lk", 16, U16), ("oeb", K, F32), ("yb", C, F32)):
    _sb(_n, _s, _d)
SCRATCH["rw"] = ("sbuf", [128, 15, 32], F32)
for _n in ("pa", "pb", "pc", "pe", "pd0", "pd1", "pd2", "pd3"):
    SCRATCH[_n] = ("psum", [128, 512], F32)

SEMAPHORES = ["v", "s", "t", "g", "lx", "lz", "lu", "lv", "lw", "p0", "p1", "p2", "a0", "a1", "a2", "loc", "out"]

A = AluOpType
AF = ActivationFunctionType
X = AxisListType.X


def rank_program(g, core, T, topo):
    rank = T.rank_of(core)
    if rank is None:
        return
    N = len(T.cores)
    eng = {"v": g.vector, "s": g.scalar, "t": g.tensor, "g": g, "y": g.sync}
    known = {q: {} for q in eng}
    total = {}
    clock = {}
    wrote, read = {}, {}
    held = []

    def wait(q, ev):
        s, n = ev
        if known[q].get(s, 0) >= n:
            return
        eng[q].wait_ge(T.sem[s], n)
        for a, b in list(clock.get(ev, {}).items()) + [ev]:
            if known[q].get(a, 0) < b:
                known[q][a] = b

    def op(q, fn, r, w, sem=None, inc=1):
        if held:
            held[-1].append((q, fn, r, w, sem, inc))
            return
        need = {}
        evs = [wrote[k] for k in list(r) + list(w) if k in wrote]
        for k in w:
            evs += read.get(k, [])
        for s, n in evs:
            need[s] = max(need.get(s, 0), n)
        for s, n in need.items():
            wait(q, (s, n))
        ins = fn()
        if inc == 0:
            return
        s = sem or q
        ins.then_inc(T.sem[s], inc)
        total[s] = total.get(s, 0) + inc
        ev = (s, total[s])
        clock[ev] = dict(known[q])
        for k in r:
            read.setdefault(k, []).append(ev)
        for k in w:
            wrote[k] = ev
            read[k] = []

    def listed(*fs):
        ls = []
        for f in fs:
            held.append([])
            f()
            ls.append(held.pop())
        return [l[i] for i in range(max(len(l) for l in ls)) for l in ls if i < len(l)]

    def issue(l, n=None):
        for _ in range(len(l) if n is None else min(n, len(l))):
            op(*l.pop(0))

    V, S, PE = g.vector, g.scalar, g.tensor

    def ts(o, i, s1, s2, o0, o1, r, w):
        if o1 is None:
            op("v", lambda: V.tensor_scalar(o, i, s1, None, o0), r, w)
        else:
            op("v", lambda: V.tensor_scalar(o, i, s1, s2, o0, o1), r, w)

    def tt(o, a, b, f, r, w):
        op("v", lambda: V.tensor_tensor(o, a, b, f), r, w)

    def cp(o, i, r, w):
        op("v", lambda: V.tensor_copy(o, i), r, w)

    def ms(o, c, w):
        op("v", lambda: V.memset(o, c), [], w)

    def scan(o, a, b, o0, o1, r, w, init=0.0):
        op("v", lambda: V.tensor_tensor_scan(o, a, b, init, o0, o1), r, w)

    def red(o, i, f, r, w):
        op("v", lambda: V.tensor_reduce(o, i, X, f), r, w)

    def tr(o, i, r, w):
        op("v", lambda: V.transpose(o, i), r, w)

    def act(o, i, f, r, w, **kw):
        op("s", lambda: S.activation(o, i, f, **kw), r, w)

    def fill(o, n, c, w):
        act(o, T.ones[:, 0:n], AF.Copy, ["ones"], w, scale=c)

    def quant(name, a, e, tile, r, key=None):
        op("v", lambda: V.quantize_mx(T[name][:, a:e], T[name + "s"][:, a:e], tile[:, 4 * a:4 * e]), r, [key or name])

    def mm(ps, lhs, l0, rhs, a, e, r):
        op("t", lambda: PE.matmul_mx(T[ps][:, 0:e - a], T[lhs][:, l0:l0 + 128], T[lhs + "s"][:, l0:l0 + 128],
                                     T[rhs][:, a:e], T[rhs + "s"][:, a:e], True, True), r, [ps])

    def pick(dst, a, e, src, w, off, okey, key):
        op("v", lambda: V.tensor_copy(T[dst][:, a:e].bitcast(dt.uint32), T[src][:, 0:w].bitcast(dt.uint32).indirect(off)),
           [src, okey], [key])
        act(T[dst + "s"][:, a:e], T[src + "s"][:, 0:w].indirect(off), AF.Copy, [src, okey], [key + "s"])

    def iota(o, pat, base, cm, w, f=True):
        if f:
            op("g", lambda: g.iota(o, pat, base, cm, allow_small_or_imprecise_dtypes=True), [], w)
        else:
            op("g", lambda: g.iota(o, pat, base, cm), [], w)

    def dma(q, o, i, sem, r, w):
        op(q, lambda: eng[q].dma_start(o, i), r, w, sem=sem, inc=16)

    askers = [T.cores[(rank - STEP[t]) % N] for t in range(R)]
    ne = min(len(topo.engines(T.cores[r], T.cores[(r - s) % N])) for r in range(N) for s in STEP)

    def send(t, dst, src, sem, r, w):
        d = askers[t]
        rid, pid = topo.addr(d, core)
        mask = sum(1 << e for e in topo.engines(core, d)[:ne])
        op("g", lambda: g.remote_dma(dst, src, T.sem[sem], T.sem.loc, pid, rid, mask), r, [], inc=0)
        total["loc"] = total.get("loc", 0) + ne
        total[sem] = total.get(sem, 0) + ne
        for k in w:
            wrote[k] = (sem, total[sem])


    io, kc, lc, kt, kw, mk = T.io1, T.kc, T.lc, T.kt, T.kw, T.mk
    col = lambda b, i: b[:, i:i + 1]
    L_U0, L_U1, L_B, L_ROW, L_OWN, L_X, L_K, L_NAT = 0, 8, 16, 40, 70, 126, 222, 244
    lst = lambda a, n: lc[:, a:a + n]
    k22 = lambda i: kt[:, 24 * i:24 * i + 22]
    w28 = lambda i, a=0, e=28: kw[:, 28 * i + a:28 * i + e]

    def own_lists():
        ts(col(kc, 1), col(kc, 0), 24.0, -4.0, A.mult, A.add, ["q"], ["q24"])
        ts(col(kc, 3), col(kc, 0), 0.0, None, A.is_equal, None, ["q"], ["qz0"])
        ts(w28(0), io[:, 0:28], col(kc, 1), None, A.add, None, ["io", "q24"], ["n"])
        ts(col(kc, 2), col(kc, 3), float(C), col(kc, 1), A.mult, A.add, ["qz0", "q24"], ["k2"])
        ts(w28(1), w28(0), float(C), float(NC), A.is_ge, A.mult, ["n"], ["pad"])
        ts(w28(2, 0, 4), io[:, 0:4], col(kc, 2), None, A.add, None, ["io", "k2"], ["o0a"])
        cp(w28(2, 4, 28), w28(0, 4, 28), ["n"], ["o0b"])
        tt(w28(3), w28(2), w28(1), A.max, ["o0a", "o0b", "pad"], ["o0"])
        ts(lst(L_OWN, 28), w28(3), float(NC), None, A.min, None, ["o0"], ["L_OWN0"])

    def own_columns():
        ts(w28(2, 4, 28), io[:, 0:24], 16.0, col(kc, 0), A.mult, A.add, ["io", "q"], ["o0b"])
        ts(w28(4, 0, 24), w28(2, 4, 28), float(K), None, A.add, None, ["o0b"], ["J"])

    def own_lists_state():
        ts(col(kc, 4), col(kc, 3), -113.0, col(kc, 0), A.mult, A.add, ["qz0", "q"], ["k4"])
        ts(w28(2, 0, 4), io[:, 20:24], 16.0, -1.0, A.mult, A.add, ["io"], ["o0a"])
        ts(w28(2, 0, 4), w28(2, 0, 4), col(kc, 4), None, A.add, None, ["o0a", "k4"], ["o0a"])
        tt(w28(3), w28(2), w28(1), A.max, ["o0a", "o0b", "pad"], ["o0"])
        ts(lst(L_OWN + 28, 28), w28(3), float(NC), None, A.min, None, ["o0"], ["L_OWN1"])

    def tables():
        k = k22
        ki = lambda i: T.ki[:, 24 * i:24 * i + 22]
        ts(k(0), io[:, 0:22], 16.0, col(kc, 0), A.mult, A.add, ["io", "q"], ["e"])
        ts(k(1), k(0), -21.5, 1.0 / M, A.add, A.mult, ["e"], ["k1"])
        ts(k(7), k(0), 3.0 * M, None, A.add, None, ["e"], ["base"])
        cp(ki(0), k(1), ["k1"], ["si"])
        cp(k(1), ki(0), ["si"], ["sf"])
        ts(k(2), ki(0), -float(M), None, A.mult, None, ["si"], ["k2t"])
        tt(k(2), k(2), k(0), A.add, ["k2t", "e"], ["j"])
        ts(k(6), k(2), 0.0, float(M), A.is_equal, A.mult, ["j"], ["k6"])
        ts(k(6), k(6), -1.0, None, A.add, None, ["k6"], ["adj"])

    def natural():
        k = k22
        ki = T.ki[:, 48:70]
        ts(k(9), k(0), -11.5, 1.0 / 24, A.add, A.mult, ["e"], ["k9"])
        ts(k(10), k(0), 16.0, None, A.mult, None, ["e"], ["k10"])
        cp(ki, k(9), ["k9"], ["ni"])
        ts(k(9), ki, -383.0, None, A.mult, None, ["ni"], ["k9"])
        tt(k(9), k(9), k(10), A.add, ["k9", "k10"], ["k9"])
        cp(lst(L_NAT, 22), k(9), ["k9"], ["L_NAT"])

    def masks():
        ts(T.pi[:, 2:3], T.pi[:, 0:1], 16, None, A.bitwise_and, None, ["pi0"], ["pi2"])
        cp(col(kc, 9), T.pi[:, 2:3], ["pi2"], ["h"])
        ts(col(kc, 10), col(kc, 9), 16.0, None, A.add, None, ["h"], ["h16"])
        tt(col(kc, 11), col(kc, 9), col(kc, 0), A.add, ["h", "q"], ["r32"])
        ts(mk[:, 0:32], io[:, 0:32], col(kc, 9), None, A.is_ge, None, ["io", "h"], ["mk0"])
        ts(mk[:, 64:96], io[:, 0:32], col(kc, 10), None, A.is_lt, None, ["io", "h16"], ["mk2"])
        ts(mk[:, 32:64], io[:, 0:32], col(kc, 11), None, A.is_gt, None, ["io", "r32"], ["mk1"])
        ts(mk[:, 128:160], io[:, 0:32], col(kc, 11), -1.0, A.is_lt, A.mult, ["io", "r32"], ["mk4"])
        tt(mk[:, 0:32], mk[:, 0:32], mk[:, 64:96], A.mult, ["mk0", "mk2"], ["same"])
        tt(mk[:, 32:64], mk[:, 32:64], mk[:, 64:96], A.mult, ["mk1", "mk2"], ["tri"])
        ts(mk[:, 96:128], mk[:, 0:32], -BIG, BIG, A.mult, A.add, ["same"], ["other"])
        tt(mk[:, 128:160], mk[:, 128:160], mk[:, 0:32], A.mult, ["mk4", "same"], ["ntri"])

    def turn_list():
        ts(T.pi[:, 3:4], T.pi[:, 0:1], 1, None, A.bitwise_and, None, ["pi0"], ["pi3"])
        ts(T.pi[:, 4:5], T.pi[:, 0:1], 4, 1, A.arith_shift_right, A.bitwise_and, ["pi0"], ["pi4"])
        ts(col(kc, 12), col(kc, 0), 9.0, 16.0, A.min, A.mult, ["q"], ["k12"])
        tt(col(kc, 13), T.pi[:, 3:4], T.pi[:, 4:5], A.not_equal, ["pi3", "pi4"], ["k13"])
        ts(lst(L_K, 1), col(kc, 13), K + 16.0, col(kc, 12), A.mult, A.add, ["k12", "k13"], ["L_K"])

    def plane_lists():
        ts(w28(3, 0, 24), w28(0, 4, 28), float(C), None, A.min, None, ["n", "L_OWN0"], ["n0", "o0"])
        for b in range(4):
            ts(lst(L_X + 24 * b, 24), w28(3, 0, 24), 4.0, float(b), A.mult, A.add, ["n0", "o0"], ["L_X%d" % b])

    def fills():
        fill(T.keep16[:], 448, 1.0, ["keep16"])
        fill(T.reset[:], C, 0.0, ["reset"])
        fill(T.keep16[:, 0::16], 28, 0.0, ["keep16"])
        fill(T.reset[:, 0::M], 8, BIG, ["reset"])
        fill(T.win[:, 0:192], 192, 0.0, ["win"])
        fill(T.rr[:, 24 * M + M - 1::M], 8, BIG, ["rrz"])

    def diagonal():
        for a in (16, 32, 64, 128, 256):
            e = min(2 * a, 448)
            act(T.diag[:, a:e], T.diag[:, 0:e - a], AF.Copy, ["diag"], ["diag"])

    def delay_list():
        cp(col(T.ti, 0), col(T.tc, 0), ["tc0"], ["ti0"])
        ts(col(T.ti, 1), col(T.ti, 0), 3, None, A.bitwise_and, None, ["ti0"], ["ti1"])
        cp(col(T.tc, 1), col(T.ti, 1), ["ti1"], ["tc1"])
        ts(col(T.tc, 2), col(T.ti, 1), -float(M), None, A.mult, None, ["ti1"], ["tc2"])
        ts(T.bl[:, 0:22], k22(1), col(T.tc, 1), None, A.is_le, None, ["sf", "tc1"], ["bl0"])
        tt(T.bl[:, 22:44], T.bl[:, 0:22], k22(6), A.mult, ["bl0", "adj"], ["bl1"])
        tt(T.bl[:, 44:66], T.bl[:, 22:44], k22(7), A.add, ["bl1", "base"], ["bl2"])
        ts(T.lb[:], T.bl[:, 44:66], col(T.tc, 2), None, A.add, None, ["bl2", "tc2"], ["lb"])

    def unit_tile(b):
        op("g", lambda: g.affine_select(T.et[:, 512 * b:512 * b + 512], T.ones[:], [[-4, 128], [-1, 4]], A.is_equal, 0.0, b, 4),
           ["ones"], ["et%d" % b])

    dma("y", T.ut[:], T.u[:], "lu", [], ["ut"])
    dma("s", T.xt[:, 0:768], T.x[:, 0:768], "lx", [], ["xta"])
    dma("y", T.xt[:, 768:4 * C], T.x[:, 768:], "lz", [], ["xtb"])
    iota(T.pi[:, 0:1], [[0, 1]], 0, 1, ["pi0"], f=False)
    iota(io[:], [[1, 32]], 0, 0, ["io"])
    ms(T.ones[:], 1.0, ["ones"])
    unit_tile(0)
    iota(T.sm[:, 0:30], [[1, 15], [16, 2]], 0, 0, ["sm"])
    ts(T.pi[:, 1:2], T.pi[:, 0:1], 15, None, A.bitwise_and, None, ["pi0"], ["pi1"])
    ms(T.xt[:, 4 * C:], 0.0, ["xz"])
    ms(T.prow[:, C:], FAR, ["prz"])
    cp(col(kc, 0), T.pi[:, 1:2], ["pi1"], ["q"])
    ts(lst(L_U0, 8), io[:, 0:8], 16.0, None, A.mult, None, ["io"], ["L_U0"])
    ts(T.diag[:, 0:16], io[:, 0:16], col(kc, 0), None, A.is_equal, None, ["io", "q"], ["diag"])
    ts(lst(L_U1, 8), io[:, 0:8], 16.0, 1.0, A.mult, A.add, ["io"], ["L_U1"])
    cp(lst(L_B, 24), io[:, 0:24], ["io"], ["L_B"])
    issue(listed(own_lists, turn_list))
    late = listed(masks)
    issue(listed(fills, diagonal))
    quant("qu", 0, 128, T.ut, ["ut"])
    quant("q0", 0, 192, T.xt, ["xta"], "qpa")
    quant("q0", 192, C, T.xt, ["xtb"], "qpe")
    pick("su0", 0, 128, "qu", 128, lst(L_U0, 8), "L_U0", "su0")

    wd, rr, rw = T.wd, T.rr, T.rw
    xpl = lambda b: wd[:, 544 * b + K:544 * b + 544]
    Wv = lambda a, e: rr[:, M * a + M - 1:M * e:M]
    row = rw[:, :, 0:24]

    def planes(a, e):
        for b in range(a, e):
            ts(xpl(b), T.xs[:, b::4], 64.0, None, A.mult, None, ["xs%d" % b, "xs4"], ["xp%d" % b])

    def first_planes(a, e):
        for b in range(a, e):
            act(xpl(b), T.xt[:].indirect(lst(L_X + 24 * b, 24)), AF.Copy, ["xta", "xtb", "xz", "L_X%d" % b], ["xp%d" % b], scale=64.0)
    half = 2 * K - NR - 0.5
    for t in range(R):
        q, land = "q%d" % t, "land%d" % t
        n = C if t == 0 else NC
        nb = n // 16
        parts = (FIRST, LATER)[min(t, 1)]
        qk = ["q" + ps for a, e, ps in parts]
        again_in = ("pc", "pd1", "pd2")
        turned = [lambda a=a, e=e, ps=ps: mm(ps, "qu", 0, q, a, e, ["qu", "q" + ps]) for a, e, ps in parts]
        spread = [lambda a=a, e=e, ps=ps, pb=pb: mm(pb, "su0", 0, q, a, e, ["su0", "su0s", "q" + ps])
                  for (a, e, ps), pb in zip(parts, again_in)]
        for f in turned + spread:
            f()
        for a, e, ps in parts:
            tr(T.tp[:, a:e], T[ps][:, 0:e - a], [ps], ["tp" + ps])
        cp(T.ps[:, 24 * t:24 * t + nb], T.tp[:, 0:n:16], ["tp" + ps for a, e, ps in parts], ["ps%d" % t])
        if t == 0:
            pick("su1", 0, 128, "qu", 128, lst(L_U1, 8), "L_U1", "su1")
        mm("pb", "su1", 0, q, 0, n, ["su1", "su1s"] + qk)
        h = FIRST[0][1] if t == 0 else 0
        if t == 0:
            send(t, T.land0s[:, 0:h], T.q0s[:, 0:h], "a0", qk[0:1], [])
        send(t, T.lp[:, 24 * t:24 * t + nb], T.ps[:, 24 * t:24 * t + nb], "p%d" % t, ["ps%d" % t], ["lp%d" % t])
        for i, ((a, e, ps), pb) in enumerate(zip(parts, again_in)):
            act(T.prow[:, a:e], T[pb][:, 0:e - a], AF.Copy, [pb, "prz"], ["prow%d" % i])
        if t == 0:
            issue(listed(plane_lists, tables))
            first_planes(0, 1)
        act(T.sg[:, 0:n], T.pb[:, 0:n], AF.Sign, ["pb"], ["sg0"])
        act(T.sg[:, NC:NC + n], T.sg[:, 0:n], AF.Relu, ["sg0"], ["sg1", "tc0"], accum_out=col(T.tc, 0))
        if t == 0:
            unit_tile(1)
        send(t, T[land][:].bitcast(dt.uint8), T[q][:].bitcast(dt.uint8), "a%d" % t, qk + ["tc0"] * min(t, 1), [])
        send(t, T[land + "s"][:, h:], T[q + "s"][:, h:], "a%d" % t, qk, [land])
        if t == 0:
            unit_tile(2)
            unit_tile(3)
            for b in range(3):
                op("g", lambda: g.affine_select(T.keepc[:, NR * b:NR * b + NR], T.ones[:, 0:NR], [[1, NR]], A.not_equal, 0.0, 0, 0),
                   ["ones"], ["keepc" if b == 2 else "keepc%d" % b])
            iota(T.sr[:, 0:24], [[0, 3], [1, 8]], 9, 0, ["sr0"])
            iota(T.sr[:, 24:48], [[0, 3], [48, 8]], 49, 0, ["sr1"])
            iota(T.val[:], [[1, NC]], 0, 0, ["val"])
            iota(T.plc[:], [[1, 24], [24, 16]], 0, 0, ["plc"])
        if t == 1:
            fill(T.sr[:, 31:48:8], 3, 2.0, ["sr1"])
        own = "L_OWN%d" % min(t, 1)
        tt(T.mm[:], T.prow[:].indirect(lst(L_OWN + 28 * min(t, 1), 28)), T.diag[:], A.mult,
           ["prow0", "prow1", "prow2", "prz", own, "diag"], ["mm"])
        scan(T.ms[:], T.keep16[:], T.mm[:], A.mult, A.add, ["keep16", "mm"], ["ms"])
        if t == 0:
            first_planes(1, 3)

        def unit_codes(b):
            if t == 0:
                quant("qe", 128 * b, 128 * b + 128, T.et, ["et%d" % b], "qe%d" % b)
            mm("pd%d" % b, "qe", 128 * b, land, 0, n, ["qe%d" % b, land])
        delay = listed(delay_list)
        if t == 0:
            issue(delay, 1)
            ts(wd[:, 544 * 3 + K:544 * 3 + K + 192], T.xt[:].indirect(lst(L_X + 72, 12)), 64.0, None, A.mult, None,
               ["xta", "xtb", "xz", "L_X3"], ["xp3"])
            issue(listed(lambda: issue(delay, 3), own_columns))
        else:
            issue(delay, 1)
            planes(0, 1)
            issue(delay, 1)
        lw = T.lp[:, 24 * t:24 * t + nb]
        cuts = ((0, 8), (8, 16), (16, nb))
        for i, (a, e) in enumerate(((0, 8), (8, 16), (16, 20), (20, nb))):
            src, key = lw.indirect(lst(L_B + a, e - a)), ["lp%d" % t, "L_B"]
            if i % 2 == 0:
                cp(T.xb[:, 16 * a:16 * e], src, key, ["xb%d" % i])
            else:
                act(T.xb[:, 16 * a:16 * e], src, AF.Copy, key, ["xb%d" % i])
        for i, (a, e) in enumerate(cuts):
            tr(T.far[:, 16 * a:16 * e] if t == 0 else T.far[:, i::3], T.xb[:, 16 * a:16 * e], ["xb%d" % i, "xb%d" % (i + i // 2)], ["far%d" % i])
        issue(delay if t else late, 2)
        phase = lambda s: T.far[:, s:C:8] if t == 0 else T.far[:, 48 * s:48 * s + M]
        fk = ["far0", "far1", "far2", "ms"]
        issue(delay, 1)
        for c in range(4):
            ts(T.zf[:, 96 + M * c:96 + M * c + M], phase(c + 4), col(T.ms, 16 * c + 15), None, A.subtract, None, fk, ["dd%d" % c])
            issue(delay, c % 2)
        for buf, c in [("ab", c) for c in range(4, 27)] + [("aw", c) for c in range(24, 28)]:
            act(T[buf][:, M * c:M * c + M], phase((c - 4) % 8), AF.Abs, fk, ["%s%d" % (buf, c)], bias=col(T.ms, 16 * c + 15), scale=-1.0)
            if c == 11:
                act(T.ab[:, 0:4 * M], T.zf[:, 96:], AF.Abs, ["dd%d" % i for i in range(4)], ["ab%d" % i for i in range(4)])
        if t == 0:
            cp(lst(L_ROW, 30), T.sm[:, 0:30], ["sm"], ["L_ROW"])
            issue(delay)
            wait("y", wrote[land])
            dma("y", T.qw[:].bitcast(dt.uint8), T.wc[:], "lw", [], ["qw"])
            dma("y", T.qws[:], T.ws[:], "lw", [], ["qw"])
            dma("y", T.vt[:], T.v[:], "lv", [], ["vt"])
        else:
            planes(1, 2)
            issue(delay)

        def again(a, e):
            cp(T.aw[:, M * a:M * e], T.ab[:, M * a:M * e], ["ab%d" % c for c in range(a, e)], ["aw%d" % c for c in range(a, e)])

        def larger(k):
            tt(T.dm[:, C * k:C * k + C], T.ab[:, C * k:C * k + 11 * M].indirect(T.lb[:]), T.aw[:, C * k + 4 * M:C * k + 12 * M],
               A.max, ["ab%d" % c for c in range(8 * k, 8 * k + 11)] + ["aw%d" % c for c in range(8 * k + 4, 8 * k + 12)] + ["lb"],
               ["dm%d" % k])

        def least(k):
            scan(rr[:, C * k:C * k + C], T.reset[:], T.dm[:, C * k:C * k + C], A.max, A.min,
                 ["reset", "dm%d" % k], ["rr%d" % k])
        issue(late, 2)
        again(4, 9)
        issue(late, 1)
        again(9, 12)
        issue(late, 2)
        larger(0)
        again(12, 16)
        least(0)
        again(16, 20)
        issue(late, 2)
        larger(1)
        again(20, 24)
        least(1)
        rk = ["rr0", "rr1", "rr2"]
        s8 = lambda i: T.srt[:, 8 * i:8 * i + 8]
        larger(2)
        tt(s8(0), Wv(0, 8), Wv(8, 16), A.min, rk[0:2], ["s0"])
        tt(s8(1), Wv(0, 8), Wv(8, 16), A.max, rk[0:2], ["s1"])
        least(2)
        issue(late, 2)
        if t:
            planes(3, 4)

        def before(c):
            act(T.lq[:, M * c:M * c + M - 1], rr[:, M * c:M * c + M - 1], AF.Sign, ["rr%d" % (c // 8)], ["lq%d" % c, "jm%d" % c],
                bias=col(rr, M * c + M - 1), scale=-1.0, accum_out=col(T.jm, c))
        if t == 0:
            act(T.sr[:, 0:24], T.sr[:, 0:24], AF.Copy, ["sr0"], ["sr0"], scale=0.125)
        ns = NS[t]
        for c in range(ns):
            before(c)

        def successor_list():
            i = min(t, 1)
            tt(T.zf[:, 0:24], T.sr[:, 24 * i:24 * i + 24], T.jm[:], A.subtract, ["jm%d" % c for c in range(24)] + ["sr%d" % i], ["z0"])
            ts(T.lz[:], T.zf[:, 0:24], (8.0, 1.0)[i], None, A.mult, None, ["z0"], ["lz"])
        spare = listed(successor_list)
        tr(T.t1[:], Wv(0, 32), rk + ["rrz"], ["t1"])
        tt(s8(2), s8(1), Wv(16, 24), A.min, rk + ["s1"], ["s2"])
        tt(s8(3), s8(0), Wv(16, 24), A.min, rk + ["s0"], ["low"])
        cut = (0, 6, 10, 15)
        act(T.xg[:, 0:192], T.t1[:].indirect(lst(L_ROW, 12)), AF.Copy, ["t1", "L_ROW"], ["xg0"])
        act(T.xg[:, 192:320], T.t1[:].indirect(lst(L_ROW + 12, 8)), AF.Copy, ["t1", "L_ROW"], ["xg1"])
        cp(T.xg[:, 320:480], T.t1[:].indirect(lst(L_ROW + 20, 10)), ["t1", "L_ROW"], ["xg2"])
        tt(T.cand[:, 0:8], s8(0), s8(2), A.max, ["s0", "s2"], ["mid"])
        tt(s8(4), s8(1), Wv(16, 24), A.max, rk + ["s1"], ["upp"])
        for i in (2, 0, 1):
            tr(rw[:, cut[i]:cut[i + 1], :], T.xg[:, 32 * cut[i]:32 * cut[i + 1]], ["xg%d" % i], ["rw%d" % i])
        issue(late)
        rwk = ["rw0", "rw1", "rw2"]

        def count(i, j, key):
            act(T.junk[:, NR * j:NR * j + NR], row, AF.Sign, rwk + [key], ["junk%d" % j, "cnt%d" % i],
                bias=col(T.cand, i), scale=-1.0, accum_out=col(T.cnt, i))

        def less(i, j, key):
            ts(T.cmp[:, NR * j:NR * j + NR], row, col(T.cand, i), None, A.is_lt, None, rwk + [key], ["cmp%d" % j])

        def tally(a, e):
            scan(T.cms[:, NR * a:NR * e], T.keepc[:, 0:NR * (e - a)], T.cmp[:, NR * a:NR * e], A.mult, A.add,
                 ["keepc"] + ["cmp%d" % j for j in range(a, e)], ["cms%d" % j for j in range(a, e)])
        pen, lh, r3 = T.pen, T.lh, T.r3
        big = lambda a: 2 * BIG if a < 8 else BIG
        by_sign = lambda a, e, key: ts(pen[:, 8 + a:8 + e], T.cnt[:, a:e], half, big(a), A.is_lt, A.mult,
                                       ["cnt%d" % i for i in range(a, e)], [key])
        by_sum = lambda a, j, e, key: ts(pen[:, 8 + a:8 + a + e - j], T.cms[:, NR * j + NR - 1:NR * e:NR], K - 0.5, big(a),
                                         A.is_lt, A.mult, ["cms%d" % i for i in range(j, e)], [key])
        for i in (0, 1, 2, 6, 7):
            count(i, i, "mid")
        for i in (3, 4, 5):
            less(i, i, "mid")
        tally(3, 5)
        tally(5, 6)
        by_sign(0, 3, "pen1a")
        by_sum(3, 3, 6, "pen1b")

        def unpack(b, i):
            e = min(128 * i + 128, n)
            o = T.dsb[:, NC * b + 128 * i:NC * b + e] if t == 0 else T.dsb[:, NC * b + i:NC * b + NC:3]
            if b < 3:
                cp(o, T["pd%d" % b][:, 128 * i:e], ["pd%d" % b], ["dsb%d%d" % (b, i)])
            else:
                act(o, T["pd%d" % b][:, 128 * i:e], AF.Copy, ["pd%d" % b], ["dsb%d%d" % (b, i)])
        if t:
            for b in (2, 0, 1, 3):
                unit_codes(b)
        between = (lambda i: unpack(2, i) if i < 3 else None) if t else unit_codes
        between(0)
        tt(lh[:, 32:38], T.srt[:, 32:38], pen[:, 8:14], A.min, ["upp", "pen1a", "pen1b"], ["lh2"])
        between(1)
        tt(T.cand[:, 8:14], lh[:, 32:38], T.srt[:, 24:30], A.max, ["lh2", "low"], ["nxt"])
        for i in range(8, 13):
            count(i, i, "nxt")
        between(2)
        by_sign(6, 8, "pen1c")
        less(13, 0, "nxt")
        tt(lh[:, 38:40], T.srt[:, 38:40], pen[:, 14:16], A.min, ["upp", "pen1c"], ["lh3"])
        tally(0, 1)
        tt(T.cand[:, 14:16], lh[:, 38:40], T.srt[:, 30:32], A.max, ["lh3", "low"], ["nxu"])
        between(3)
        less(14, 1, "nxu")
        less(15, 2, "nxu")
        tally(1, 2)
        tally(2, 3)
        for c in range(ns, 24):
            before(c)
        if t == 0:
            for b in (2, 3):
                act(T.dsb[:, NC * b:NC * b + C], T["pd%d" % b][:, 0:C], AF.Copy, ["pd%d" % b], ["dsb%d%d" % (b, i) for i in range(3)])
        else:
            for i in range(3):
                unpack(3, i)

        unpack(0, 0)
        by_sum(13, 0, 3, "pen3")
        unpack(0, 1)
        by_sign(8, 13, "pen2")
        unpack(0, 2)
        pk = ["pen1a", "pen1b", "pen1c", "pen2", "pen3"]
        tt(lh[:, 0:16], T.cand[:], pen[:, 8:24], A.min, ["mid", "nxt", "nxu"] + pk, ["lh0"])
        tt(lh[:, 16:32], T.cand[:], pen[:, 8:24], A.max, ["mid", "nxt", "nxu"] + pk, ["lh1"])
        op("v", lambda: V.tensor_reduce(col(r3, 2), pen[:, 8:24], X, A.add, negate=True), pk, ["r2"])
        red(col(r3, 0), lh[:, 0:16], A.max, ["lh0"], ["r0"])
        red(col(r3, 1), lh[:, 16:32], A.min, ["lh1"], ["r1"])
        xe, xf = T.xe, T.xf
        ts(xe[:, 64:96], mk[:, 0:32], col(r3, 2), (K - 0.5) * BIG / 32, A.mult, A.add, ["same", "r2"], ["xe2"])
        ts(xe[:, 0:32], mk[:, 0:32], col(r3, 0), None, A.mult, None, ["same", "r0"], ["xe0"])
        ts(xe[:, 32:64], mk[:, 96:128], col(r3, 1), None, A.max, None, ["other", "r1"], ["xe1"])
        unpack(1, 0)
        tr(xf[:], xe[:], ["xe0", "xe1", "xe2"], ["xf"])
        unpack(1, 1)
        red(col(r3, 5), xf[:, 64:96], A.add, ["xf"], ["r5"])
        red(col(r3, 4), xf[:, 32:64], A.min, ["xf"], ["r4"])
        red(col(r3, 3), xf[:, 0:32], A.max, ["xf"], ["r3"])
        unpack(1, 2)
        ts(col(r3, 7), col(r3, 5), col(r3, 3), col(r3, 4), A.max, A.min, ["r3", "r4", "r5"], ["tau"])
        dk = ["dsb%d%d" % (b, i) for b in range(4) for i in range(3)]
        if t == 0:
            for b in range(4):
                act(T.dsb[:, NC * b + C:NC * b + C + 9], T.dsb[:, NC * b:NC * b + 9], AF.Copy, dk, ["ring%d" % b])
        else:
            for i in range(2):
                act(T.dsb[:, M + i::48], T.dsb[:, i::48], AF.Copy, dk, ["ring%d" % (3 * i)])
        tau = col(r3, 7)
        p24 = lambda i: T.pw[:, 24 * i:24 * i + 24]
        W, cs = Wv(0, 24), T.cs
        ts(T.le[:, 0:24], W, tau, None, A.is_lt, None, rk + ["tau"], ["lt"])
        ts(T.le[:, 24:48], W, tau, None, A.is_equal, None, rk + ["tau"], ["eq"])
        ts(p24(0), W, tau, 1000.0, A.is_gt, A.mult, rk + ["tau"], ["p0"])
        scan(cs[:], T.le[:], T.le[:], A.add, A.max, ["lt", "eq"], ["cs"])
        ts(p24(1), W, tau, None, A.is_ge, None, rk + ["tau"], ["p1"])
        issue(spare, 1)
        ts(xe[:, 0:32], mk[:, 32:64], col(cs, 47), None, A.mult, None, ["tri", "cs"], ["xe0"])
        ts(xe[:, 32:64], mk[:, 128:160], col(cs, 23), K / 32.0, A.mult, A.add, ["ntri", "cs"], ["xe1"])
        tt(p24(2), cs[:, 24:48], p24(0), A.add, ["cs", "p0"], ["p2"])
        issue(spare)
        for b in range(4):
            act(T.zall[:, NC * b:NC * b + NC], T.dsb[:, NC * b:NC * b + (C + 9, NC)[min(t, 1)]].indirect(T.lz[:]), AF.Copy,
                dk + ["ring0", "ring3", "lz"], ["zall%d" % b])
        if t == 0:
            act(wd[:, 544 * 3 + K + 192:], T.xt[:].indirect(lst(L_X + 84, 12)), AF.Copy, ["xta", "xtb", "xz", "L_X3"], ["xp3"], scale=64.0)
        tr(xf[:, 0:64], xe[:, 0:64], ["xe0", "xe1"], ["xf"])
        tt(p24(3), p24(1), w28(4, 0, 24), A.mult, ["p1", "J"], ["p3"])
        red(col(r3, 8), xf[:, 0:32], A.add, ["xf"], ["r8"])
        red(col(r3, 9), xf[:, 32:64], A.add, ["xf"], ["r9"])
        ts(p24(4), cs[:, 0:24], col(cs, 23), -1.0, A.subtract, A.add, ["cs"], ["p4"])
        ts(p24(5), p24(2), col(r3, 8), col(r3, 9), A.add, A.is_gt, ["p2", "r8", "r9"], ["p5"])
        ts(p24(6), cs[:, 24:48], col(r3, 8), col(r3, 9), A.add, A.min, ["cs", "r8", "r9"], ["p6"])
        spare = listed((own_lists_state, natural, lambda: quant("qv", 0, 128, T.vt, ["vt"]))[t])
        issue(spare, t == 1)
        tt(p24(7), p24(5), p24(3), A.mult, ["p5", "p3"], ["p7"])
        tt(p24(8), p24(6), p24(4), A.add, ["p6", "p4"], ["p8"])
        issue(spare, 1)
        tt(p24(9), p24(8), p24(7), A.max, ["p7", "p8"], ["p9"])
        issue(spare, 1)
        cp(T.lo[:], p24(9), ["p9"], ["lo"])
        issue(spare, 1)
        cp(T.win[:, 16:].indirect(T.lo[:]), T.val[:], ["lo", "val"], ["win"])
        if t:
            planes(2, 3)
        else:
            issue(spare, 1)
        tr(T.es[:, 0:K], T.win[:, 16:16 + K], ["win"], ["es0"])
        tr(T.es[:, K:], T.win[:, 0:192], ["win"], ["es1"])
        issue(spare, 1)
        cp(T.lk[:], T.es[:].indirect(lst(L_K, 1)), ["es0", "es1", "L_K"], ["lk"])
        issue(spare)
        lk = T.lk[:, 0:10]
        zsrc = lambda b: T.zall[:, NC * b:NC * b + NC].indirect(lk)
        for b in (0, 1):
            cp(T.zt[:, b::4], zsrc(b), ["zall%d" % b, "lk"], ["zt%d" % b])
        for b in (2, 3):
            act(T.zt[:, b::4], zsrc(b), AF.Copy, ["zall%d" % b, "lk"], ["zt%d" % b])
        for b in (2, 3, 1):
            act(T.f64[:, K * b:K * b + K], xpl(b).indirect(lk), AF.Copy, ["xp%d" % b, "lk"], ["f%d" % b])
        quant("qz", 0, K, T.zt, ["zt%d" % b for b in range(4)])
        for b in (2, 3, 0, 1):
            mm("pd%d" % b, "qw", 128 * b, "qz", 0, K, ["qw", "qz"])
        cp(T.f64[:, 0:K], xpl(0).indirect(lk), ["xp0", "lk"], ["f0"])
        for b in (2, 3, 0, 1):
            tt(wd[:, 544 * b:544 * b + K], T["pd%d" % b][:, 0:K], T.f64[:, K * b:K * b + K], A.add,
               ["pd%d" % b, "f%d" % b], ["g%d" % b])
        usrc = lambda b, a, e: wd[:, 544 * b:544 * b + 544].indirect(T.lo[:, a:e])
        for b, a, e, key in ((2, 0, 24, "xs2"), (3, 0, 24, "xs3"), (1, 16, 24, "xs4")):
            act(T.xs[:, 64 * a + b:64 * e:4], usrc(b, a, e), AF.Copy, ["g%d" % b, "xp%d" % b, "lo"], [key], scale=0.015625)
        for b, a, e in ((0, 0, 24), (1, 0, 16)):
            ts(T.xs[:, 64 * a + b:64 * e:4], usrc(b, a, e), 0.015625, None, A.mult, None, ["g%d" % b, "xp%d" % b, "lo"], ["xs%d" % b])
        for a, e, ps in LATER if t + 1 < R else ((0, 256, "pa"), LATER[2]):
            quant("q%d" % (t + 1), a, e, T.xs, ["xs%d" % b for b in range(4 if e < NC else 5)], "q" + ps)
    wrote["q3"] = wrote["qpe"]

    runs = ((0, C - 128, "pa"), (C - 128, C, "pe"))
    for a, e, ps in runs:
        pick("q3n", a, e, "q3", NC, lst(L_NAT + a // 16, (e - a) // 16), "L_NAT", "n" + ps)
        dma("y", T.oc[:, 4 * a:4 * e], T.q3n[:, a:e].bitcast(dt.uint8), "out", ["n" + ps], [])
        mm(ps, "qv", 0, "q3n", a, e, ["qv", "n" + ps, "n" + ps + "s"])
    act(T.oeb[:], T.plc[:].indirect(T.lk[:, 0:10]), AF.Copy, ["plc", "lk"], ["oeb"])
    for a, e, ps in runs:
        cp(T.yb[:, a:e], T[ps][:, 0:e - a], [ps], ["y" + ps])
        dma("y", T.y[:, a:e], T.yb[:, a:e], "out", ["y" + ps], [])
    dma("s", T.oe[:], T.oeb[0:128:16, :], "out", ["oeb"], [])
    for k in range(4):
        dma("s", T.osc[4 * k:4 * k + 4, :], T.q3ns[32 * k:32 * k + 4, :], "out", ["npas", "npes"], [])
    for s in SEMAPHORES:
        if total.get(s):
            wait("g", (s, total[s]))
